import numpy as np
import ml_dtypes


def mxq(x, axis, fmt="e4m3"):
    dtype, down = {"e4m3": (ml_dtypes.float8_e4m3fn, 7), "e5m2": (ml_dtypes.float8_e5m2, 14)}[fmt]
    v = np.moveaxis(np.asarray(x, np.float32).astype(ml_dtypes.bfloat16).astype(np.float64), axis, -1)
    blocks = v.reshape(v.shape[:-1] + (-1, 32))
    amax = np.abs(blocks).max(-1, keepdims=True)
    byte = np.maximum(np.where(amax > 0, np.frexp(amax)[1] - 1 + 127, 0) - down, 1)
    scale = np.exp2(byte - 127.0)
    codes = (blocks / scale).astype(np.float32).astype(dtype).astype(np.float64)
    return np.moveaxis((codes * scale).reshape(v.shape), -1, axis)


WIDE = False


def mx_kscale(k):
    if not WIDE:
        return np.ones(k)
    levels = np.array([10, -10, 5, -5, 0])
    if k % 512:
        return np.exp2(np.random.permutation(np.resize(levels, k // 32))).repeat(32)
    a = np.empty((k // 512, 16))
    for p in range(k // 512):
        a[p, :8] = np.random.permutation(np.resize(levels, 8))
        for g in range(8):
            far = levels[np.abs(levels - a[p, g]) >= 10]
            a[p, g + 8] = far[np.random.randint(len(far))]
    return np.exp2(a.ravel()).repeat(32)


def f64(x):
    return np.asarray(x).astype(np.float64)


def striped(idx):
    return np.tile(idx.reshape(-1, 16).T, (8, 1)).astype(np.uint16)


def unstriped(offs):
    return offs[:16].T.reshape(-1).astype(np.int64)


E2M1 = np.array([0.0, 0.5, 1.0, 1.5, 2.0, 3.0, 4.0, 6.0, -0.0, -0.5, -1.0, -1.5, -2.0, -3.0, -4.0, -6.0])


def pack_weight(w, fmt):
    k, n = w.shape
    w = f64(np.asarray(w, np.float32).astype(ml_dtypes.bfloat16)).reshape(k // 32, 32, n)
    amax = np.abs(w).max(1)
    if fmt == "e4m3":
        byte = np.frexp(amax)[1] - 1 + 127 - 7
    else:
        mant, ex = np.frexp(amax / 6.0)
        byte = np.where(mant > 0.5, ex, ex - 1) + 127
    byte = np.clip(np.where(amax > 0, byte, 1), 1, 254)
    scaled = (w * np.exp2(127.0 - byte)[:, None, :]).reshape(k, n).astype(np.float32)
    by_word = np.ascontiguousarray(scaled.reshape(k // 512, 128, 4, n).transpose(0, 1, 3, 2))
    if fmt == "e4m3":
        words = by_word.astype(ml_dtypes.float8_e4m3fn).view(np.uint8)
    else:
        c = by_word.astype(ml_dtypes.float4_e2m1fn).view(np.uint8) & 0xF
        words = (c[..., 0::2] | (c[..., 1::2] << 4)).reshape(k // 512, 128, 2 * n)
    return np.ascontiguousarray(words), np.ascontiguousarray(byte.astype(np.uint8).reshape(k // 512, 16, n))


def unpack_weight(words, scales, fmt):
    g, _, n = scales.shape
    words = np.ascontiguousarray(words).reshape(g, 128, n, -1)
    if fmt == "e4m3":
        vals = words.view(ml_dtypes.float8_e4m3fn).astype(np.float64)
    else:
        nib = np.empty((g, 128, n, 4), np.uint8)
        nib[..., 0::2] = words & 0xF
        nib[..., 1::2] = words >> 4
        vals = E2M1[nib]
    vals = vals * np.repeat(np.exp2(scales.astype(np.float64) - 127.0), 8, axis=1)[..., None]
    return vals.transpose(0, 1, 3, 2).reshape(g * 512, n)


def gelu(v):
    return 0.5 * v * (1.0 + np.tanh(np.sqrt(2.0 / np.pi) * (v + 0.044715 * v**3)))


K, H, T, S, T2, S2 = 1536, 512, 2048, 1024, 1024, 512

def setup_inputs():
    n = np.random.standard_normal
    s = mx_kscale(K)[:, None]
    u = mx_kscale(H)[:, None]
    tab_words, tab_scales = pack_weight(n((K, T)) * s, "e4m3")
    tab2_words, tab2_scales = pack_weight(n((H, T2)) / np.sqrt(H) / u, "e4m3")
    wa = n((K, H)) / np.sqrt(K) / s * u.T
    wb_words, wb_scales = pack_weight(n((K, H)) / np.sqrt(K) / s, "e2m1")
    return {
        "tab_words": tab_words, "tab_scales": tab_scales,
        "offs": striped(np.random.permutation(T)[:S]),
        "tab2_words": tab2_words, "tab2_scales": tab2_scales,
        "offs2": striped(np.random.permutation(T2)[:S2]),
        "wa": wa.astype(np.float32),
        "wb_words": wb_words, "wb_scales": wb_scales,
        "c": (0.5 * n(S2)).astype(np.float32),
    }

def reference(tab_words, tab_scales, offs, tab2_words, tab2_scales, offs2, wa, wb_words, wb_scales, c):
    v = unpack_weight(tab_words, tab_scales, "e4m3")[:, unstriped(offs)]
    v2 = unpack_weight(tab2_words, tab2_scales, "e4m3")[:, unstriped(offs2)]
    wb = unpack_weight(wb_words, wb_scales, "e2m1")
    a = mxq(f64(wa), 0, "e4m3").T @ v
    b = wb.T @ v
    h = a / (1.0 + np.abs(b))
    y = v2.T @ mxq(h, 0, "e4m3")
    return np.tanh(y + f64(c)[:, None])

@@ -1,0 +1,200 @@
+from contextlib import ExitStack
+
+import concourse.mybir as mybir
+from concourse.masks import make_identity
+
+K, H, T, S, T2, S2 = 1536, 512, 2048, 1024, 1024, 512
+FLOPS = 2 * K * H * S * 2 + 2 * H * S2 * S
+
+F32 = mybir.dt.float32
+BF16 = mybir.dt.bfloat16
+I32 = mybir.dt.int32
+U32 = mybir.dt.uint32
+U16 = mybir.dt.uint16
+U8 = mybir.dt.uint8
+FP8X4 = mybir.dt.float8_e4m3fn_x4
+FP4X4 = mybir.dt.float4_e2m1fn_x4
+ACT = mybir.ActivationFunctionType
+ALU = mybir.AluOpType
+
+P = 128
+PASSES = K // 512
+VIEW_TILES = S // P
+CHUNK = 256
+SQUARE_ON = ["s","s","s","s","v","v","v","v"]
+
+
+def tile_list_grasp_view_value_kernel(tc, tab_words, tab_scales, offs, tab2_words, tab2_scales, offs2,
+                                               wa, wb_words, wb_scales, c, out):
+    nc = tc.nc
+    with ExitStack() as ctx:
+        keep = ctx.enter_context(tc.tile_pool(name="keep", bufs=1))
+        psum = ctx.enter_context(tc.psum_pool(name="psum", bufs=1))
+
+        def sb(name, shape, dtype, tag=None):
+            return keep.tile(shape, dtype, name=name, tag=tag or name, align_bytes=64)
+
+        def bank(index, name):
+            return psum.tile([P, 512], F32, name=name, tag="bank%d" % index)
+
+        offs_sb = keep.tile([P, S // 16], U16, name="offs_sb")
+        offs2_sb = keep.tile([P, S2 // 16], U16, name="offs2_sb")
+        tab_s = sb("tab_s", [P, T], U8, "stage0")
+        tab_w = [sb("tab_w%d" % a, [P, T], I32, "stage%d" % (a + 1)) for a in range(PASSES)]
+        tab2_s = sb("tab2_s", [P, T2], U8)
+        wb_w = sb("wb_w", [P, PASSES, 2 * H], U8)
+        wb_s = sb("wb_s", [P, PASSES, H], U8)
+        wa_bf = [sb("wa_bf%d" % a, [P, H, 4], BF16) for a in range(PASSES)]
+        wa_w = [sb("wa_w%d" % a, [P, H], U32) for a in range(PASSES)]
+        wa_s = [sb("wa_s%d" % a, [P, H], U8) for a in range(PASSES)]
+        v_w = [sb("v_w%d" % a, [P, S], U32) for a in range(PASSES)]
+        v_s = [sb("v_s%d" % a, [P, S], U8) for a in range(PASSES)]
+        v2_w = sb("v2_w", [P, S2], U32)
+        v2_s = sb("v2_s", [P, S2], U8)
+        bias = sb("bias", [P, S2 // P], F32)
+        ident = sb("ident", [P, P], F32)
+        warm = sb("warm", [P, 8], F32)
+        warm_out = sb("warm_out", [P, 8], F32)
+
+        nc.gpsimd.memset(tab_s[:].bitcast(I32), 0)
+        for q, queue in enumerate((nc.gpsimd, nc.scalar, nc.gpsimd, nc.scalar)):
+            queue.dma_start(tab_s[32 * q : 32 * q + 4 * PASSES, :].bitcast(I32),
+                            tab_scales[:, 4 * q : 4 * q + 4, :].bitcast(I32))
+        for a in (1, 2):
+            nc.gpsimd.memset(v_s[a][:].bitcast(I32), 0)
+        nc.vector.memset(wb_s[:].rearrange("p a n -> p (a n)").bitcast(I32), 0)
+        nc.vector.memset(warm[:], 1.0)
+        nc.scalar.activation(warm_out[:], warm[:], ACT.Abs_reciprocal_sqrt)
+        for q in range(4):
+            nc.gpsimd.dma_start(wb_s[32 * q : 32 * q + 4, :, :].bitcast(I32),
+                                wb_scales[:, 4 * q : 4 * q + 4, :].rearrange("a r n -> r a n").bitcast(I32))
+        make_identity(nc, ident[:])
+        with nc.allow_non_contiguous_dma(reason="one bias value a partition"):
+            nc.gpsimd.dma_start(bias[:], c.rearrange("(g p) -> p g", p=P))
+        nc.gpsimd.memset(tab2_s[:].bitcast(I32), 0)
+
+        def load_table(a):
+            nc.sync.dma_start(tab_w[a][:], tab_words[a].rearrange("p n t -> p (n t)").bitcast(I32))
+
+        nc.sync.dma_start(offs_sb[:], offs)
+        load_table(0)
+        nc.sync.dma_start(wb_w[:].bitcast(I32), wb_words.rearrange("a p n -> p a n").bitcast(I32))
+        load_table(1)
+        load_table(2)
+        nc.sync.dma_start(offs2_sb[:], offs2)
+
+        nc.vector.tensor_copy(v_s[0][:], tab_s[:].indirect(offs_sb[:]))
+        for a in (1, 2):
+            nc.scalar.dma_start(v_s[a][0:112, :].bitcast(I32), v_s[0][4 * a : 4 * a + 112, :].bitcast(I32))
+
+        wa_raw = []
+
+        def load_wa(a):
+            raw = sb("wa_raw%d" % a, [P, 4, H], F32, "stage%d" % a)
+            nc.sync.dma_start(raw[:], wa[512 * a : 512 * (a + 1), :].rearrange("(p t) r -> p t r", t=4))
+            wa_raw.append(raw)
+
+        def gather_words(a, j0, j1):
+            nc.vector.tensor_copy(v_w[a][:, j0:j1], tab_w[a][:].bitcast(U32).indirect(offs_sb[:, j0 // 16 : j1 // 16]))
+
+        load_wa(0)
+        for a in range(2):
+            for j0 in range(0, S, S // 2):
+                gather_words(a, j0, j0 + S // 2)
+            load_wa(a + 1)
+        for q in range(4):
+            nc.sync.dma_start(tab2_s[32 * q : 32 * q + 4, :].bitcast(I32),
+                              tab2_scales[0, 4 * q : 4 * q + 4, :].bitcast(I32))
+
+        def permuted(ap):
+            return ap.rearrange("j (p u e) -> j u p e", u=2, e=2)
+
+        def plain(ap):
+            return ap.rearrange("j (u p e) -> j u p e", u=2, e=2)
+
+        mag = [sb("mag%d" % g, [P, H], F32) for g in range(VIEW_TILES)]
+        root = [sb("root%d" % g, [P, H], F32) for g in range(VIEW_TILES)]
+        damp = [sb("damp%d" % g, [P, H], F32) for g in range(VIEW_TILES)]
+        for g in range(VIEW_TILES):
+            if g % 2 == 0:
+                gather_words(2, P * g, P * (g + 2))
+            cols = slice(P * g, P * (g + 1))
+            b_ps = bank(g, "b_ps%d" % g)
+            for a in range(PASSES):
+                nc.tensor.matmul_mx(out=b_ps[:], lhsT=v_w[a][:, cols].bitcast(FP8X4), lhsT_scale=v_s[a][:, cols],
+                                    rhs=wb_w[:, a, :].bitcast(FP4X4), rhs_scale=wb_s[:, a, :],
+                                    start=(a == 0), stop=(a == PASSES - 1))
+            nc.scalar.activation(plain(mag[g][:]), permuted(b_ps[:]), ACT.Abs)
+
+        tab2_w = sb("tab2_w", [P, T2], I32, "stage3")
+        nc.sync.dma_start(tab2_w[:], tab2_words[0].rearrange("p n t -> p (n t)").bitcast(I32))
+
+        def quantise_wa(a):
+            nc.vector.tensor_copy(wa_bf[a][:].rearrange("p (n i) t -> p n t i", i=4),
+                                  wa_raw[a][:].rearrange("p t (n i) -> p n t i", i=4))
+            nc.vector.quantize_mx(out=wa_w[a][:].bitcast(FP8X4), scales=wa_s[a][:],
+                                  in_=wa_bf[a][:].rearrange("p n t -> p (n t)"))
+
+        a_ps = [bank(g, "a_ps%d" % g) for g in range(VIEW_TILES)]
+
+        def project_a(a, g):
+            cols = slice(P * g, P * (g + 1))
+            nc.tensor.matmul_mx(out=a_ps[g][:], lhsT=v_w[a][:, cols].bitcast(FP8X4), lhsT_scale=v_s[a][:, cols],
+                                rhs=wa_w[a][:].bitcast(FP8X4), rhs_scale=wa_s[a][:],
+                                start=(a == 0), stop=(a == PASSES - 1))
+
+        def square(g):
+            if SQUARE_ON[g] == "s":
+                nc.scalar.activation(damp[g][:], root[g][:], ACT.Square)
+            elif SQUARE_ON[g] == "v":
+                nc.vector.tensor_tensor(damp[g][:], root[g][:], root[g][:], ALU.mult)
+            else:
+                nc.gpsimd.tensor_tensor(damp[g][:], root[g][:], root[g][:], ALU.mult)
+
+        quantise_wa(0)
+        quantise_wa(1)
+        quantise_wa(2)
+        nc.vector.tensor_copy(v2_s[:], tab2_s[:].indirect(offs2_sb[:]))
+        nc.vector.tensor_copy(v2_w[:], tab2_w[:].bitcast(U32).indirect(offs2_sb[:]))
+        for a in range(PASSES):
+            for g in range(VIEW_TILES):
+                project_a(a, g)
+        for g in range(VIEW_TILES):
+            nc.scalar.activation(root[g][:], mag[g][:], ACT.Abs_reciprocal_sqrt, bias=1.0)
+            if SQUARE_ON[g] != "v":
+                square(g)
+        warm_tanh = sb("warm_tanh", [P, 8], F32)
+        nc.scalar.activation(warm_tanh[:], root[VIEW_TILES - 1][:, 0:8], ACT.Tanh)
+
+        for ch in range(S // CHUNK):
+            h_bf = sb("h_bf%d" % ch, [P, 2, H], BF16)
+            for half in range(2):
+                g = 2 * ch + half
+                if SQUARE_ON[g] == "v":
+                    square(g)
+                nc.vector.tensor_tensor(plain(h_bf[:, half, :]), permuted(a_ps[g][:]), plain(damp[g][:]), ALU.mult)
+            h_words = h_bf[:].rearrange("j g r -> j (g r)").bitcast(F32)
+            ht_ps = bank(2 * ch, "ht_ps%d" % ch)
+            for n in range(4):
+                nc.tensor.transpose(ht_ps[:, P * n : P * (n + 1)], h_words[:, P * n : P * (n + 1)], ident[:])
+            ht_bf = sb("ht_bf%d" % ch, [P, 4 * CHUNK], BF16)
+            nc.scalar.copy(ht_bf[:].bitcast(F32).rearrange("p (g j u) -> p g j u", g=2, u=2),
+                           ht_ps[:].rearrange("p (g u j) -> p g j u", g=2, u=2))
+            h_w = sb("h_w%d" % ch, [P, CHUNK], U32)
+            h_s = sb("h_s%d" % ch, [P, CHUNK], U8)
+            nc.vector.quantize_mx(out=h_w[:].bitcast(FP8X4), scales=h_s[:], in_=ht_bf[:])
+            for pair in range(2):
+                y_ps = bank(2 * ch + 1 - pair, "y_ps%d_%d" % (ch, pair))
+                res = sb("res%d_%d" % (ch, pair), [P, 2, CHUNK], F32)
+                for n in range(2):
+                    rows = slice(P * (2 * pair + n), P * (2 * pair + n + 1))
+                    nc.tensor.matmul_mx(out=y_ps[:, CHUNK * n : CHUNK * (n + 1)], lhsT=v2_w[:, rows].bitcast(FP8X4),
+                                        lhsT_scale=v2_s[:, rows], rhs=h_w[:].bitcast(FP8X4), rhs_scale=h_s[:],
+                                        start=True, stop=True)
+                for n in range(2):
+                    i = 2 * pair + n
+                    nc.scalar.activation(res[:, n, :], y_ps[:, CHUNK * n : CHUNK * (n + 1)], ACT.Tanh,
+                                         bias=bias[:, i : i + 1])
+                nc.sync.dma_start(
+                    out[2 * P * pair : 2 * P * (pair + 1), CHUNK * ch : CHUNK * (ch + 1)].rearrange("(n p) j -> p n j", p=P),
+                    res[:])

@@ -21,7 +21,9 @@ P = 128
 PASSES = K // 512
 VIEW_TILES = S // P
 CHUNK = 256
-SQUARE_ON = ["s","s","s","s","v","v","v","v"]
+SLOT = 4 * T
+ROW0 = 20
+SQUARE_ON = ["g","g","g","g","g","g","g","g"]
 
 
 def tile_list_grasp_view_value_kernel(tc, tab_words, tab_scales, offs, tab2_words, tab2_scales, offs2,
@@ -29,82 +31,95 @@ def tile_list_grasp_view_value_kernel(tc, tab_words, tab_scales, offs, tab2_word
     nc = tc.nc
     with ExitStack() as ctx:
         keep = ctx.enter_context(tc.tile_pool(name="keep", bufs=1))
+        stage = ctx.enter_context(tc.tile_pool(name="stage", bufs=1))
         psum = ctx.enter_context(tc.psum_pool(name="psum", bufs=1))
 
-        def sb(name, shape, dtype, tag=None):
-            return keep.tile(shape, dtype, name=name, tag=tag or name, align_bytes=64)
+        def sb(name, shape, dtype, offset=None):
+            if offset is None:
+                return keep.tile(shape, dtype, name=name, align_bytes=64)
+            return stage.tile(shape, dtype, name=name, align_bytes=64, offset=offset)
 
         def bank(index, name):
             return psum.tile([P, 512], F32, name=name, tag="bank%d" % index)
 
         offs_sb = keep.tile([P, S // 16], U16, name="offs_sb")
         offs2_sb = keep.tile([P, S2 // 16], U16, name="offs2_sb")
-        tab_s = sb("tab_s", [P, T], U8, "stage0")
-        tab_w = [sb("tab_w%d" % a, [P, T], I32, "stage%d" % (a + 1)) for a in range(PASSES)]
+        tab_s = sb("tab_s", [P, T], U8, 2 * SLOT)
+        tab2_w = sb("tab2_w", [P, T2], I32)
+        tab_w = [sb("tab_w%d" % a, [P, T], I32, a * SLOT) for a in range(2)]
         tab2_s = sb("tab2_s", [P, T2], U8)
         wb_w = sb("wb_w", [P, PASSES, 2 * H], U8)
         wb_s = sb("wb_s", [P, PASSES, H], U8)
-        wa_bf = [sb("wa_bf%d" % a, [P, H, 4], BF16) for a in range(PASSES)]
         wa_w = [sb("wa_w%d" % a, [P, H], U32) for a in range(PASSES)]
         wa_s = [sb("wa_s%d" % a, [P, H], U8) for a in range(PASSES)]
         v_w = [sb("v_w%d" % a, [P, S], U32) for a in range(PASSES)]
-        v_s = [sb("v_s%d" % a, [P, S], U8) for a in range(PASSES)]
+        v_s = sb("v_s", [P, PASSES, S], U8)
+        v_s_packed = sb("v_s_packed", [P, S], U8, 3 * SLOT)
         v2_w = sb("v2_w", [P, S2], U32)
-        v2_s = sb("v2_s", [P, S2], U8)
         bias = sb("bias", [P, S2 // P], F32)
         ident = sb("ident", [P, P], F32)
         warm = sb("warm", [P, 8], F32)
         warm_out = sb("warm_out", [P, 8], F32)
 
-        nc.gpsimd.memset(tab_s[:].bitcast(I32), 0)
-        for q, queue in enumerate((nc.gpsimd, nc.scalar, nc.gpsimd, nc.scalar)):
-            queue.dma_start(tab_s[32 * q : 32 * q + 4 * PASSES, :].bitcast(I32),
-                            tab_scales[:, 4 * q : 4 * q + 4, :].bitcast(I32))
-        for a in (1, 2):
-            nc.gpsimd.memset(v_s[a][:].bitcast(I32), 0)
-        nc.vector.memset(wb_s[:].rearrange("p a n -> p (a n)").bitcast(I32), 0)
-        nc.vector.memset(warm[:], 1.0)
-        nc.scalar.activation(warm_out[:], warm[:], ACT.Abs_reciprocal_sqrt)
-        for q in range(4):
-            nc.gpsimd.dma_start(wb_s[32 * q : 32 * q + 4, :, :].bitcast(I32),
-                                wb_scales[:, 4 * q : 4 * q + 4, :].rearrange("a r n -> r a n").bitcast(I32))
-        make_identity(nc, ident[:])
-        with nc.allow_non_contiguous_dma(reason="one bias value a partition"):
-            nc.gpsimd.dma_start(bias[:], c.rearrange("(g p) -> p g", p=P))
-        nc.gpsimd.memset(tab2_s[:].bitcast(I32), 0)
-
         def load_table(a):
             nc.sync.dma_start(tab_w[a][:], tab_words[a].rearrange("p n t -> p (n t)").bitcast(I32))
 
+        def load_table_scales(q, queue):
+            queue.dma_start(tab_s[32 * q + ROW0 : 32 * q + 32, :].bitcast(I32),
+                            tab_scales[:, 4 * q : 4 * q + 4, :].bitcast(I32))
+
         nc.sync.dma_start(offs_sb[:], offs)
+        for q in range(4):
+            load_table_scales(q, nc.sync if q % 2 else nc.scalar)
+            nc.vector.memset(tab_s[32 * q : 32 * q + ROW0, :].bitcast(I32), 0)
         load_table(0)
         nc.sync.dma_start(wb_w[:].bitcast(I32), wb_words.rearrange("a p n -> p a n").bitcast(I32))
         load_table(1)
-        load_table(2)
         nc.sync.dma_start(offs2_sb[:], offs2)
+        nc.sync.dma_start(tab2_w[:], tab2_words[0].rearrange("p n t -> p (n t)").bitcast(I32))
 
-        nc.vector.tensor_copy(v_s[0][:], tab_s[:].indirect(offs_sb[:]))
-        for a in (1, 2):
-            nc.scalar.dma_start(v_s[a][0:112, :].bitcast(I32), v_s[0][4 * a : 4 * a + 112, :].bitcast(I32))
+        nc.vector.memset(warm[:], 1.0)
+        nc.scalar.activation(warm_out[:], warm[:], ACT.Abs_reciprocal_sqrt)
+        nc.gpsimd.memset(wb_s[:].rearrange("p a n -> p (a n)").bitcast(I32), 0)
+        for q in range(4):
+            nc.scalar.dma_start(wb_s[32 * q : 32 * q + 4, :, :].bitcast(I32),
+                                wb_scales[:, 4 * q : 4 * q + 4, :].rearrange("a r n -> r a n").bitcast(I32))
+        nc.vector.memset(v_s[96:128, :, :].rearrange("p a n -> p (a n)").bitcast(I32), 0)
+        nc.vector.memset(tab2_s[:].bitcast(I32), 0)
+        for q in range(4):
+            nc.gpsimd.dma_start(tab2_s[32 * q : 32 * q + 4, :].bitcast(I32),
+                                tab2_scales[0, 4 * q : 4 * q + 4, :].bitcast(I32))
+        with nc.allow_non_contiguous_dma(reason="one bias value a partition"):
+            nc.gpsimd.dma_start(bias[:], c.rearrange("(g p) -> p g", p=P))
+        make_identity(nc, ident[:])
+
+        nc.vector.tensor_copy(v_s_packed[:], tab_s[:].indirect(offs_sb[:]))
+
+        def shift_plane(a, queue):
+            row = ROW0 + 4 * a
+            queue.dma_start(v_s[0:100, a, :].bitcast(I32), v_s_packed[row : row + 100, :].bitcast(I32))
+
+        shift_plane(0, nc.sync)
+        shift_plane(1, nc.scalar)
+        tab_w.append(sb("tab_w2", [P, T], I32, 2 * SLOT))
+        load_table(2)
+        shift_plane(2, nc.sync)
 
         wa_raw = []
 
         def load_wa(a):
-            raw = sb("wa_raw%d" % a, [P, 4, H], F32, "stage%d" % a)
+            raw = sb("wa_raw%d" % a, [P, 4, H], F32, SLOT * (a if a < 2 else 3))
             nc.sync.dma_start(raw[:], wa[512 * a : 512 * (a + 1), :].rearrange("(p t) r -> p t r", t=4))
             wa_raw.append(raw)
 
         def gather_words(a, j0, j1):
             nc.vector.tensor_copy(v_w[a][:, j0:j1], tab_w[a][:].bitcast(U32).indirect(offs_sb[:, j0 // 16 : j1 // 16]))
 
-        load_wa(0)
         for a in range(2):
-            for j0 in range(0, S, S // 2):
-                gather_words(a, j0, j0 + S // 2)
-            load_wa(a + 1)
-        for q in range(4):
-            nc.sync.dma_start(tab2_s[32 * q : 32 * q + 4, :].bitcast(I32),
-                              tab2_scales[0, 4 * q : 4 * q + 4, :].bitcast(I32))
+            gather_words(a, 0, S)
+            load_wa(a)
+        load_wa(2)
+        nc.vector.tensor_copy(v2_w[:], tab2_w[:].bitcast(U32).indirect(offs2_sb[:]))
 
         def permuted(ap):
             return ap.rearrange("j (p u e) -> j u p e", u=2, e=2)
@@ -119,27 +134,26 @@ def tile_list_grasp_view_value_kernel(tc, tab_words, tab_scales, offs, tab2_word
             if g % 2 == 0:
                 gather_words(2, P * g, P * (g + 2))
             cols = slice(P * g, P * (g + 1))
-            b_ps = bank(g, "b_ps%d" % g)
+            b_ps = bank(g % 4, "b_ps%d" % g)
             for a in range(PASSES):
-                nc.tensor.matmul_mx(out=b_ps[:], lhsT=v_w[a][:, cols].bitcast(FP8X4), lhsT_scale=v_s[a][:, cols],
+                nc.tensor.matmul_mx(out=b_ps[:], lhsT=v_w[a][:, cols].bitcast(FP8X4), lhsT_scale=v_s[:, a, cols],
                                     rhs=wb_w[:, a, :].bitcast(FP4X4), rhs_scale=wb_s[:, a, :],
                                     start=(a == 0), stop=(a == PASSES - 1))
             nc.scalar.activation(plain(mag[g][:]), permuted(b_ps[:]), ACT.Abs)
 
-        tab2_w = sb("tab2_w", [P, T2], I32, "stage3")
-        nc.sync.dma_start(tab2_w[:], tab2_words[0].rearrange("p n t -> p (n t)").bitcast(I32))
 
         def quantise_wa(a):
-            nc.vector.tensor_copy(wa_bf[a][:].rearrange("p (n i) t -> p n t i", i=4),
+            wa_bf = sb("wa_bf%d" % a, [P, H, 4], BF16, 2 * SLOT)
+            nc.vector.tensor_copy(wa_bf[:].rearrange("p (n i) t -> p n t i", i=4),
                                   wa_raw[a][:].rearrange("p t (n i) -> p n t i", i=4))
             nc.vector.quantize_mx(out=wa_w[a][:].bitcast(FP8X4), scales=wa_s[a][:],
-                                  in_=wa_bf[a][:].rearrange("p n t -> p (n t)"))
+                                  in_=wa_bf[:].rearrange("p n t -> p (n t)"))
 
-        a_ps = [bank(g, "a_ps%d" % g) for g in range(VIEW_TILES)]
+        a_ps = [bank((g + 4) % 8, "a_ps%d" % g) for g in range(VIEW_TILES)]
 
         def project_a(a, g):
             cols = slice(P * g, P * (g + 1))
-            nc.tensor.matmul_mx(out=a_ps[g][:], lhsT=v_w[a][:, cols].bitcast(FP8X4), lhsT_scale=v_s[a][:, cols],
+            nc.tensor.matmul_mx(out=a_ps[g][:], lhsT=v_w[a][:, cols].bitcast(FP8X4), lhsT_scale=v_s[:, a, cols],
                                 rhs=wa_w[a][:].bitcast(FP8X4), rhs_scale=wa_s[a][:],
                                 start=(a == 0), stop=(a == PASSES - 1))
 
@@ -151,11 +165,11 @@ def tile_list_grasp_view_value_kernel(tc, tab_words, tab_scales, offs, tab2_word
             else:
                 nc.gpsimd.tensor_tensor(damp[g][:], root[g][:], root[g][:], ALU.mult)
 
+        v2_s = sb("v2_s", [P, S2], U8, 2 * SLOT + SLOT // 2)
+        nc.vector.tensor_copy(v2_s[:], tab2_s[:].indirect(offs2_sb[:]))
         quantise_wa(0)
         quantise_wa(1)
         quantise_wa(2)
-        nc.vector.tensor_copy(v2_s[:], tab2_s[:].indirect(offs2_sb[:]))
-        nc.vector.tensor_copy(v2_w[:], tab2_w[:].bitcast(U32).indirect(offs2_sb[:]))
         for a in range(PASSES):
             for g in range(VIEW_TILES):
                 project_a(a, g)
@@ -174,7 +188,7 @@ def tile_list_grasp_view_value_kernel(tc, tab_words, tab_scales, offs, tab2_word
                     square(g)
                 nc.vector.tensor_tensor(plain(h_bf[:, half, :]), permuted(a_ps[g][:]), plain(damp[g][:]), ALU.mult)
             h_words = h_bf[:].rearrange("j g r -> j (g r)").bitcast(F32)
-            ht_ps = bank(2 * ch, "ht_ps%d" % ch)
+            ht_ps = bank((2 * ch + 4) % 8, "ht_ps%d" % ch)
             for n in range(4):
                 nc.tensor.transpose(ht_ps[:, P * n : P * (n + 1)], h_words[:, P * n : P * (n + 1)], ident[:])
             ht_bf = sb("ht_bf%d" % ch, [P, 4 * CHUNK], BF16)
@@ -184,7 +198,7 @@ def tile_list_grasp_view_value_kernel(tc, tab_words, tab_scales, offs, tab2_word
             h_s = sb("h_s%d" % ch, [P, CHUNK], U8)
             nc.vector.quantize_mx(out=h_w[:].bitcast(FP8X4), scales=h_s[:], in_=ht_bf[:])
             for pair in range(2):
-                y_ps = bank(2 * ch + 1 - pair, "y_ps%d_%d" % (ch, pair))
+                y_ps = bank((2 * ch + 5 - pair) % 8, "y_ps%d_%d" % (ch, pair))
                 res = sb("res%d_%d" % (ch, pair), [P, 2, CHUNK], F32)
                 for n in range(2):
                     rows = slice(P * (2 * pair + n), P * (2 * pair + n + 1))

@@ -20,10 +20,10 @@ ALU = mybir.AluOpType
 P = 128
 PASSES = K // 512
 VIEW_TILES = S // P
-CHUNK = 256
+CHUNK_TILES = (2, 2, 2, 1, 1)
 SLOT = 4 * T
-ROW0 = 20
-SQUARE_ON = ["g","g","g","g","g","g","g","g"]
+LAST = 3 * SLOT + S2
+SQUARE_ON = ["s","s","s","s","s","s","v","v"]
 
 
 def tile_list_grasp_view_value_kernel(tc, tab_words, tab_scales, offs, tab2_words, tab2_scales, offs2,
@@ -44,17 +44,15 @@ def tile_list_grasp_view_value_kernel(tc, tab_words, tab_scales, offs, tab2_word
 
         offs_sb = keep.tile([P, S // 16], U16, name="offs_sb")
         offs2_sb = keep.tile([P, S2 // 16], U16, name="offs2_sb")
-        tab_s = sb("tab_s", [P, T], U8, 2 * SLOT)
-        tab2_w = sb("tab2_w", [P, T2], I32)
-        tab_w = [sb("tab_w%d" % a, [P, T], I32, a * SLOT) for a in range(2)]
+        tab_s = sb("tab_s", [P, T], U8, LAST + SLOT // 8)
+        tab_w = [sb("tab_w%d" % a, [P, T], I32, a * SLOT) for a in range(PASSES)]
         tab2_s = sb("tab2_s", [P, T2], U8)
         wb_w = sb("wb_w", [P, PASSES, 2 * H], U8)
         wb_s = sb("wb_s", [P, PASSES, H], U8)
         wa_w = [sb("wa_w%d" % a, [P, H], U32) for a in range(PASSES)]
         wa_s = [sb("wa_s%d" % a, [P, H], U8) for a in range(PASSES)]
-        v_w = [sb("v_w%d" % a, [P, S], U32) for a in range(PASSES)]
-        v_s = sb("v_s", [P, PASSES, S], U8)
-        v_s_packed = sb("v_s_packed", [P, S], U8, 3 * SLOT)
+        v_s_shifted = sb("v_s_shifted", [P, PASSES - 1, S], U8)
+        v_s_packed = sb("v_s_packed", [P, S], U8)
         v2_w = sb("v2_w", [P, S2], U32)
         bias = sb("bias", [P, S2 // P], F32)
         ident = sb("ident", [P, P], F32)
@@ -65,61 +63,63 @@ def tile_list_grasp_view_value_kernel(tc, tab_words, tab_scales, offs, tab2_word
             nc.sync.dma_start(tab_w[a][:], tab_words[a].rearrange("p n t -> p (n t)").bitcast(I32))
 
         def load_table_scales(q, queue):
-            queue.dma_start(tab_s[32 * q + ROW0 : 32 * q + 32, :].bitcast(I32),
+            queue.dma_start(tab_s[32 * q : 32 * q + 4 * PASSES, :].bitcast(I32),
                             tab_scales[:, 4 * q : 4 * q + 4, :].bitcast(I32))
 
+        nc.gpsimd.memset(tab_s[:].bitcast(I32), 0)
+        nc.gpsimd.memset(wb_s[:].rearrange("p a n -> p (a n)").bitcast(I32), 0)
+        nc.vector.memset(warm[:], 1.0)
+        nc.vector.memset(v_s_shifted[96:128, :, :].rearrange("p a n -> p (a n)").bitcast(I32), 0)
+        nc.vector.memset(tab2_s[:].bitcast(I32), 0)
+
         nc.sync.dma_start(offs_sb[:], offs)
+        load_table(0)
         for q in range(4):
             load_table_scales(q, nc.sync if q % 2 else nc.scalar)
-            nc.vector.memset(tab_s[32 * q : 32 * q + ROW0, :].bitcast(I32), 0)
-        load_table(0)
-        nc.sync.dma_start(wb_w[:].bitcast(I32), wb_words.rearrange("a p n -> p a n").bitcast(I32))
-        load_table(1)
-        nc.sync.dma_start(offs2_sb[:], offs2)
-        nc.sync.dma_start(tab2_w[:], tab2_words[0].rearrange("p n t -> p (n t)").bitcast(I32))
-
-        nc.vector.memset(warm[:], 1.0)
         nc.scalar.activation(warm_out[:], warm[:], ACT.Abs_reciprocal_sqrt)
-        nc.gpsimd.memset(wb_s[:].rearrange("p a n -> p (a n)").bitcast(I32), 0)
+        load_table(1)
+        nc.sync.dma_start(wb_w[:].bitcast(I32), wb_words.rearrange("a p n -> p a n").bitcast(I32))
         for q in range(4):
-            nc.scalar.dma_start(wb_s[32 * q : 32 * q + 4, :, :].bitcast(I32),
-                                wb_scales[:, 4 * q : 4 * q + 4, :].rearrange("a r n -> r a n").bitcast(I32))
-        nc.vector.memset(v_s[96:128, :, :].rearrange("p a n -> p (a n)").bitcast(I32), 0)
-        nc.vector.memset(tab2_s[:].bitcast(I32), 0)
+            nc.sync.dma_start(wb_s[32 * q : 32 * q + 4, :, :].bitcast(I32),
+                              wb_scales[:, 4 * q : 4 * q + 4, :].rearrange("a r n -> r a n").bitcast(I32))
+        load_table(2)
+        make_identity(nc, ident[:])
         for q in range(4):
             nc.gpsimd.dma_start(tab2_s[32 * q : 32 * q + 4, :].bitcast(I32),
                                 tab2_scales[0, 4 * q : 4 * q + 4, :].bitcast(I32))
         with nc.allow_non_contiguous_dma(reason="one bias value a partition"):
             nc.gpsimd.dma_start(bias[:], c.rearrange("(g p) -> p g", p=P))
-        make_identity(nc, ident[:])
 
+        v_w = {}
+
+        def gather_words(a, j0, j1, offset=None):
+            words = sb("v_w%d_%d" % (a, j0), [P, j1 - j0], U32, offset)
+            nc.vector.tensor_copy(words[:], tab_w[a][:].bitcast(U32).indirect(offs_sb[:, j0 // 16 : j1 // 16]))
+            for g in range(j0 // P, j1 // P):
+                v_w[a, g] = words[:, P * g - j0 : P * (g + 1) - j0].bitcast(FP8X4)
+
+        gather_words(0, 0, S // 2)
         nc.vector.tensor_copy(v_s_packed[:], tab_s[:].indirect(offs_sb[:]))
-
-        def shift_plane(a, queue):
-            row = ROW0 + 4 * a
-            queue.dma_start(v_s[0:100, a, :].bitcast(I32), v_s_packed[row : row + 100, :].bitcast(I32))
-
-        shift_plane(0, nc.sync)
-        shift_plane(1, nc.scalar)
-        tab_w.append(sb("tab_w2", [P, T], I32, 2 * SLOT))
-        load_table(2)
-        shift_plane(2, nc.sync)
+        for a, queue in ((1, nc.sync), (2, nc.scalar)):
+            queue.dma_start(v_s_shifted[0:112, a - 1, :].bitcast(I32),
+                            v_s_packed[4 * a : 4 * a + 112, :].bitcast(I32))
+        v_s = [v_s_packed[:], v_s_shifted[:, 0, :], v_s_shifted[:, 1, :]]
+        gather_words(0, S // 2, S, LAST)
+        nc.sync.dma_start(offs2_sb[:], offs2)
+        tab2_w = sb("tab2_w", [P, T2], I32, LAST + SLOT // 4)
+        nc.sync.dma_start(tab2_w[:], tab2_words[0].rearrange("p n t -> p (n t)").bitcast(I32))
 
         wa_raw = []
 
-        def load_wa(a):
-            raw = sb("wa_raw%d" % a, [P, 4, H], F32, SLOT * (a if a < 2 else 3))
+        def load_wa(a, offset):
+            raw = sb("wa_raw%d" % a, [P, 4, H], F32, offset)
             nc.sync.dma_start(raw[:], wa[512 * a : 512 * (a + 1), :].rearrange("(p t) r -> p t r", t=4))
             wa_raw.append(raw)
 
-        def gather_words(a, j0, j1):
-            nc.vector.tensor_copy(v_w[a][:, j0:j1], tab_w[a][:].bitcast(U32).indirect(offs_sb[:, j0 // 16 : j1 // 16]))
-
-        for a in range(2):
-            gather_words(a, 0, S)
-            load_wa(a)
-        load_wa(2)
-        nc.vector.tensor_copy(v2_w[:], tab2_w[:].bitcast(U32).indirect(offs2_sb[:]))
+        load_wa(0, 0)
+        gather_words(1, 0, S // 2)
+        gather_words(1, S // 2, S)
+        load_wa(1, SLOT)
 
         def permuted(ap):
             return ap.rearrange("j (p u e) -> j u p e", u=2, e=2)
@@ -136,14 +136,14 @@ def tile_list_grasp_view_value_kernel(tc, tab_words, tab_scales, offs, tab2_word
             cols = slice(P * g, P * (g + 1))
             b_ps = bank(g % 4, "b_ps%d" % g)
             for a in range(PASSES):
-                nc.tensor.matmul_mx(out=b_ps[:], lhsT=v_w[a][:, cols].bitcast(FP8X4), lhsT_scale=v_s[:, a, cols],
+                nc.tensor.matmul_mx(out=b_ps[:], lhsT=v_w[a, g], lhsT_scale=v_s[a][:, cols],
                                     rhs=wb_w[:, a, :].bitcast(FP4X4), rhs_scale=wb_s[:, a, :],
                                     start=(a == 0), stop=(a == PASSES - 1))
             nc.scalar.activation(plain(mag[g][:]), permuted(b_ps[:]), ACT.Abs)
 
 
         def quantise_wa(a):
-            wa_bf = sb("wa_bf%d" % a, [P, H, 4], BF16, 2 * SLOT)
+            wa_bf = sb("wa_bf%d" % a, [P, H, 4], BF16)
             nc.vector.tensor_copy(wa_bf[:].rearrange("p (n i) t -> p n t i", i=4),
                                   wa_raw[a][:].rearrange("p t (n i) -> p n t i", i=4))
             nc.vector.quantize_mx(out=wa_w[a][:].bitcast(FP8X4), scales=wa_s[a][:],
@@ -153,7 +153,7 @@ def tile_list_grasp_view_value_kernel(tc, tab_words, tab_scales, offs, tab2_word
 
         def project_a(a, g):
             cols = slice(P * g, P * (g + 1))
-            nc.tensor.matmul_mx(out=a_ps[g][:], lhsT=v_w[a][:, cols].bitcast(FP8X4), lhsT_scale=v_s[:, a, cols],
+            nc.tensor.matmul_mx(out=a_ps[g][:], lhsT=v_w[a, g], lhsT_scale=v_s[a][:, cols],
                                 rhs=wa_w[a][:].bitcast(FP8X4), rhs_scale=wa_s[a][:],
                                 start=(a == 0), stop=(a == PASSES - 1))
 
@@ -165,14 +165,13 @@ def tile_list_grasp_view_value_kernel(tc, tab_words, tab_scales, offs, tab2_word
             else:
                 nc.gpsimd.tensor_tensor(damp[g][:], root[g][:], root[g][:], ALU.mult)
 
-        v2_s = sb("v2_s", [P, S2], U8, 2 * SLOT + SLOT // 2)
+        load_wa(2, 2 * SLOT + S2)
+        nc.vector.tensor_copy(v2_w[:], tab2_w[:].bitcast(U32).indirect(offs2_sb[:]))
+        v2_s = sb("v2_s", [P, S2], U8, 2 * SLOT)
         nc.vector.tensor_copy(v2_s[:], tab2_s[:].indirect(offs2_sb[:]))
         quantise_wa(0)
         quantise_wa(1)
         quantise_wa(2)
-        for a in range(PASSES):
-            for g in range(VIEW_TILES):
-                project_a(a, g)
         for g in range(VIEW_TILES):
             nc.scalar.activation(root[g][:], mag[g][:], ACT.Abs_reciprocal_sqrt, bias=1.0)
             if SQUARE_ON[g] != "v":
@@ -180,35 +179,45 @@ def tile_list_grasp_view_value_kernel(tc, tab_words, tab_scales, offs, tab2_word
         warm_tanh = sb("warm_tanh", [P, 8], F32)
         nc.scalar.activation(warm_tanh[:], root[VIEW_TILES - 1][:, 0:8], ACT.Tanh)
 
-        for ch in range(S // CHUNK):
-            h_bf = sb("h_bf%d" % ch, [P, 2, H], BF16)
-            for half in range(2):
-                g = 2 * ch + half
+        first = 0
+        projected = 0
+        for tiles in CHUNK_TILES:
+            width = P * tiles
+            while projected < min(first + tiles + 2, VIEW_TILES):
+                for a in range(PASSES):
+                    project_a(a, projected)
+                projected += 1
+            h_bf = sb("h_bf%d" % first, [P, tiles, H], BF16)
+            for n in range(tiles):
+                g = first + n
                 if SQUARE_ON[g] == "v":
                     square(g)
-                nc.vector.tensor_tensor(plain(h_bf[:, half, :]), permuted(a_ps[g][:]), plain(damp[g][:]), ALU.mult)
+                nc.vector.tensor_tensor(plain(h_bf[:, n, :]), permuted(a_ps[g][:]), plain(damp[g][:]), ALU.mult)
             h_words = h_bf[:].rearrange("j g r -> j (g r)").bitcast(F32)
-            ht_ps = bank((2 * ch + 4) % 8, "ht_ps%d" % ch)
-            for n in range(4):
+            ht_ps = bank((first + 4) % 8, "ht_ps%d" % first)
+            for n in range(2 * tiles):
                 nc.tensor.transpose(ht_ps[:, P * n : P * (n + 1)], h_words[:, P * n : P * (n + 1)], ident[:])
-            ht_bf = sb("ht_bf%d" % ch, [P, 4 * CHUNK], BF16)
-            nc.scalar.copy(ht_bf[:].bitcast(F32).rearrange("p (g j u) -> p g j u", g=2, u=2),
-                           ht_ps[:].rearrange("p (g u j) -> p g j u", g=2, u=2))
-            h_w = sb("h_w%d" % ch, [P, CHUNK], U32)
-            h_s = sb("h_s%d" % ch, [P, CHUNK], U8)
+            ht_bf = sb("ht_bf%d" % first, [P, 4 * width], BF16)
+            nc.vector.tensor_copy(ht_bf[:].bitcast(F32).rearrange("p (g j u) -> p g j u", g=tiles, u=2),
+                                  ht_ps[:, 0 : 2 * width].rearrange("p (g u j) -> p g j u", g=tiles, u=2))
+            h_w = sb("h_w%d" % first, [P, width], U32)
+            h_s = sb("h_s%d" % first, [P, width], U8)
             nc.vector.quantize_mx(out=h_w[:].bitcast(FP8X4), scales=h_s[:], in_=ht_bf[:])
+            y_ps = [bank((first + 3 + tiles - n) % 8, "y_ps%d_%d" % (first, n)) for n in range(tiles)]
+            for i in range(S2 // P):
+                rows = slice(P * i, P * (i + 1))
+                place = (i * width) % 512
+                nc.tensor.matmul_mx(out=y_ps[i * width // 512][:, place : place + width],
+                                    lhsT=v2_w[:, rows].bitcast(FP8X4), lhsT_scale=v2_s[:, rows],
+                                    rhs=h_w[:].bitcast(FP8X4), rhs_scale=h_s[:], start=True, stop=True)
             for pair in range(2):
-                y_ps = bank((2 * ch + 5 - pair) % 8, "y_ps%d_%d" % (ch, pair))
-                res = sb("res%d_%d" % (ch, pair), [P, 2, CHUNK], F32)
-                for n in range(2):
-                    rows = slice(P * (2 * pair + n), P * (2 * pair + n + 1))
-                    nc.tensor.matmul_mx(out=y_ps[:, CHUNK * n : CHUNK * (n + 1)], lhsT=v2_w[:, rows].bitcast(FP8X4),
-                                        lhsT_scale=v2_s[:, rows], rhs=h_w[:].bitcast(FP8X4), rhs_scale=h_s[:],
-                                        start=True, stop=True)
+                res = sb("res%d_%d" % (first, pair), [P, 2, width], F32)
                 for n in range(2):
                     i = 2 * pair + n
-                    nc.scalar.activation(res[:, n, :], y_ps[:, CHUNK * n : CHUNK * (n + 1)], ACT.Tanh,
+                    place = (i * width) % 512
+                    nc.scalar.activation(res[:, n, :], y_ps[i * width // 512][:, place : place + width], ACT.Tanh,
                                          bias=bias[:, i : i + 1])
                 nc.sync.dma_start(
-                    out[2 * P * pair : 2 * P * (pair + 1), CHUNK * ch : CHUNK * (ch + 1)].rearrange("(n p) j -> p n j", p=P),
+                    out[2 * P * pair : 2 * P * (pair + 1), P * first : P * first + width].rearrange("(n p) j -> p n j", p=P),
                     res[:])
+            first += tiles

@@ -23,7 +23,7 @@ VIEW_TILES = S // P
 CHUNK_TILES = (2, 2, 2, 1, 1)
 SLOT = 4 * T
 LAST = 3 * SLOT + S2
-SQUARE_ON = ["s","s","s","s","s","s","v","v"]
+SQUARE_ON = ["s","s","s","s","s","s","s","s"]
 
 
 def tile_list_grasp_view_value_kernel(tc, tab_words, tab_scales, offs, tab2_words, tab2_scales, offs2,
@@ -78,17 +78,19 @@ def tile_list_grasp_view_value_kernel(tc, tab_words, tab_scales, offs, tab2_word
             load_table_scales(q, nc.sync if q % 2 else nc.scalar)
         nc.scalar.activation(warm_out[:], warm[:], ACT.Abs_reciprocal_sqrt)
         load_table(1)
+        nc.sync.dma_start(offs2_sb[:], offs2)
         nc.sync.dma_start(wb_w[:].bitcast(I32), wb_words.rearrange("a p n -> p a n").bitcast(I32))
         for q in range(4):
             nc.sync.dma_start(wb_s[32 * q : 32 * q + 4, :, :].bitcast(I32),
                               wb_scales[:, 4 * q : 4 * q + 4, :].rearrange("a r n -> r a n").bitcast(I32))
         load_table(2)
         make_identity(nc, ident[:])
-        for q in range(4):
-            nc.gpsimd.dma_start(tab2_s[32 * q : 32 * q + 4, :].bitcast(I32),
-                                tab2_scales[0, 4 * q : 4 * q + 4, :].bitcast(I32))
-        with nc.allow_non_contiguous_dma(reason="one bias value a partition"):
-            nc.gpsimd.dma_start(bias[:], c.rearrange("(g p) -> p g", p=P))
+        c_rows = sb("c_rows", [P, P], F32)
+        nc.gpsimd.memset(c_rows[:], 0.0)
+        nc.scalar.dma_start(c_rows[0 : S2 // P, :], c.rearrange("(g p) -> g p", p=P))
+        c_ps = bank(7, "c_ps")
+        nc.tensor.transpose(c_ps[:, 0:P], c_rows[:], ident[:])
+        nc.scalar.copy(bias[:], c_ps[:, 0 : S2 // P])
 
         v_w = {}
 
@@ -100,12 +102,11 @@ def tile_list_grasp_view_value_kernel(tc, tab_words, tab_scales, offs, tab2_word
 
         gather_words(0, 0, S // 2)
         nc.vector.tensor_copy(v_s_packed[:], tab_s[:].indirect(offs_sb[:]))
-        for a, queue in ((1, nc.sync), (2, nc.scalar)):
+        for a, queue in ((1, nc.sync), (2, nc.sync)):
             queue.dma_start(v_s_shifted[0:112, a - 1, :].bitcast(I32),
                             v_s_packed[4 * a : 4 * a + 112, :].bitcast(I32))
         v_s = [v_s_packed[:], v_s_shifted[:, 0, :], v_s_shifted[:, 1, :]]
         gather_words(0, S // 2, S, LAST)
-        nc.sync.dma_start(offs2_sb[:], offs2)
         tab2_w = sb("tab2_w", [P, T2], I32, LAST + SLOT // 4)
         nc.sync.dma_start(tab2_w[:], tab2_words[0].rearrange("p n t -> p (n t)").bitcast(I32))
 
@@ -117,6 +118,9 @@ def tile_list_grasp_view_value_kernel(tc, tab_words, tab_scales, offs, tab2_word
             wa_raw.append(raw)
 
         load_wa(0, 0)
+        for q in range(4):
+            nc.sync.dma_start(tab2_s[32 * q : 32 * q + 4, :].bitcast(I32),
+                              tab2_scales[0, 4 * q : 4 * q + 4, :].bitcast(I32))
         gather_words(1, 0, S // 2)
         gather_words(1, S // 2, S)
         load_wa(1, SLOT)
@@ -144,8 +148,8 @@ def tile_list_grasp_view_value_kernel(tc, tab_words, tab_scales, offs, tab2_word
 
         def quantise_wa(a):
             wa_bf = sb("wa_bf%d" % a, [P, H, 4], BF16)
-            nc.vector.tensor_copy(wa_bf[:].rearrange("p (n i) t -> p n t i", i=4),
-                                  wa_raw[a][:].rearrange("p t (n i) -> p n t i", i=4))
+            nc.vector.tensor_copy(wa_bf[:],
+                                  wa_raw[a][:].rearrange("p t n -> p n t"))
             nc.vector.quantize_mx(out=wa_w[a][:].bitcast(FP8X4), scales=wa_s[a][:],
                                   in_=wa_bf[:].rearrange("p n t -> p (n t)"))
 

@@ -20,14 +20,17 @@ ALU = mybir.AluOpType
 P = 128
 PASSES = K // 512
 VIEW_TILES = S // P
-CHUNK_TILES = (2, 2, 2, 1, 1)
-SLOT = 4 * T
-LAST = 3 * SLOT + S2
-SQUARE_ON = ["s","s","s","s","s","s","s","s"]
+HALF = S // 2
+CHUNK_TILES = (4, 2, 2)
+B_BANKS = 4
+A_BANKS = 8 - B_BANKS
+PAIRS = VIEW_TILES // 2
+TILES_SQUARED_ON_SCALAR = 7
+KIB = 1024
 
 
 def tile_list_grasp_view_value_kernel(tc, tab_words, tab_scales, offs, tab2_words, tab2_scales, offs2,
-                                               wa, wb_words, wb_scales, c, out):
+                                                  wa, wb_words, wb_scales, c, out):
     nc = tc.nc
     with ExitStack() as ctx:
         keep = ctx.enter_context(tc.tile_pool(name="keep", bufs=1))
@@ -44,53 +47,43 @@ def tile_list_grasp_view_value_kernel(tc, tab_words, tab_scales, offs, tab2_word
 
         offs_sb = keep.tile([P, S // 16], U16, name="offs_sb")
         offs2_sb = keep.tile([P, S2 // 16], U16, name="offs2_sb")
-        tab_s = sb("tab_s", [P, T], U8, LAST + SLOT // 8)
-        tab_w = [sb("tab_w%d" % a, [P, T], I32, a * SLOT) for a in range(PASSES)]
-        tab2_s = sb("tab2_s", [P, T2], U8)
+        tab_s = sb("tab_s", [P, T], U8, 7 * KIB)
+        tab_w = [sb("tab_w%d" % a, [P, T], I32, (None, 20 * KIB, 28 * KIB)[a]) for a in range(PASSES)]
         wb_w = sb("wb_w", [P, PASSES, 2 * H], U8)
         wb_s = sb("wb_s", [P, PASSES, H], U8)
         wa_w = [sb("wa_w%d" % a, [P, H], U32) for a in range(PASSES)]
         wa_s = [sb("wa_s%d" % a, [P, H], U8) for a in range(PASSES)]
-        v_s_shifted = sb("v_s_shifted", [P, PASSES - 1, S], U8)
         v_s_packed = sb("v_s_packed", [P, S], U8)
+        v_s_shifted = sb("v_s_shifted", [P, PASSES - 1, S], U8)
         v2_w = sb("v2_w", [P, S2], U32)
-        bias = sb("bias", [P, S2 // P], F32)
+        v2_s = sb("v2_s", [P, S2], U8)
         ident = sb("ident", [P, P], F32)
         warm = sb("warm", [P, 8], F32)
         warm_out = sb("warm_out", [P, 8], F32)
-
-        def load_table(a):
-            nc.sync.dma_start(tab_w[a][:], tab_words[a].rearrange("p n t -> p (n t)").bitcast(I32))
-
-        def load_table_scales(q, queue):
-            queue.dma_start(tab_s[32 * q : 32 * q + 4 * PASSES, :].bitcast(I32),
-                            tab_scales[:, 4 * q : 4 * q + 4, :].bitcast(I32))
 
         nc.gpsimd.memset(tab_s[:].bitcast(I32), 0)
         nc.gpsimd.memset(wb_s[:].rearrange("p a n -> p (a n)").bitcast(I32), 0)
         nc.vector.memset(warm[:], 1.0)
         nc.vector.memset(v_s_shifted[96:128, :, :].rearrange("p a n -> p (a n)").bitcast(I32), 0)
-        nc.vector.memset(tab2_s[:].bitcast(I32), 0)
+        make_identity(nc, ident[:])
+
+        def load_table(a):
+            nc.sync.dma_start(tab_w[a][:], tab_words[a].rearrange("p n t -> p (n t)").bitcast(I32))
 
         nc.sync.dma_start(offs_sb[:], offs)
         load_table(0)
-        for q in range(4):
-            load_table_scales(q, nc.sync if q % 2 else nc.scalar)
-        nc.scalar.activation(warm_out[:], warm[:], ACT.Abs_reciprocal_sqrt)
-        load_table(1)
         nc.sync.dma_start(offs2_sb[:], offs2)
+        for q in range(4):
+            queue = nc.sync if q < 2 else nc.scalar
+            queue.dma_start(tab_s[32 * q : 32 * q + 4 * PASSES, :].bitcast(I32),
+                            tab_scales[:, 4 * q : 4 * q + 4, :].bitcast(I32))
+        nc.scalar.activation(warm_out[:], warm[:], ACT.Abs_reciprocal_sqrt)
         nc.sync.dma_start(wb_w[:].bitcast(I32), wb_words.rearrange("a p n -> p a n").bitcast(I32))
+        load_table(1)
         for q in range(4):
             nc.sync.dma_start(wb_s[32 * q : 32 * q + 4, :, :].bitcast(I32),
                               wb_scales[:, 4 * q : 4 * q + 4, :].rearrange("a r n -> r a n").bitcast(I32))
         load_table(2)
-        make_identity(nc, ident[:])
-        c_rows = sb("c_rows", [P, P], F32)
-        nc.gpsimd.memset(c_rows[:], 0.0)
-        nc.scalar.dma_start(c_rows[0 : S2 // P, :], c.rearrange("(g p) -> g p", p=P))
-        c_ps = bank(7, "c_ps")
-        nc.tensor.transpose(c_ps[:, 0:P], c_rows[:], ident[:])
-        nc.scalar.copy(bias[:], c_ps[:, 0 : S2 // P])
 
         v_w = {}
 
@@ -100,128 +93,149 @@ def tile_list_grasp_view_value_kernel(tc, tab_words, tab_scales, offs, tab2_word
             for g in range(j0 // P, j1 // P):
                 v_w[a, g] = words[:, P * g - j0 : P * (g + 1) - j0].bitcast(FP8X4)
 
-        gather_words(0, 0, S // 2)
-        nc.vector.tensor_copy(v_s_packed[:], tab_s[:].indirect(offs_sb[:]))
-        for a, queue in ((1, nc.sync), (2, nc.sync)):
-            queue.dma_start(v_s_shifted[0:112, a - 1, :].bitcast(I32),
-                            v_s_packed[4 * a : 4 * a + 112, :].bitcast(I32))
-        v_s = [v_s_packed[:], v_s_shifted[:, 0, :], v_s_shifted[:, 1, :]]
-        gather_words(0, S // 2, S, LAST)
-        tab2_w = sb("tab2_w", [P, T2], I32, LAST + SLOT // 4)
-        nc.sync.dma_start(tab2_w[:], tab2_words[0].rearrange("p n t -> p (n t)").bitcast(I32))
+        def v_s(a, g):
+            plane = v_s_packed[:] if a == 0 else v_s_shifted[:, a - 1, :]
+            return plane[:, P * g : P * (g + 1)]
 
-        wa_raw = []
+        wa_raw = {}
 
         def load_wa(a, offset):
-            raw = sb("wa_raw%d" % a, [P, 4, H], F32, offset)
-            nc.sync.dma_start(raw[:], wa[512 * a : 512 * (a + 1), :].rearrange("(p t) r -> p t r", t=4))
-            wa_raw.append(raw)
+            wa_raw[a] = sb("wa_raw%d" % a, [P, 4, H], F32, offset)
+            nc.sync.dma_start(wa_raw[a][:], wa[512 * a : 512 * (a + 1), :].rearrange("(p j) r -> p j r", j=4))
 
-        load_wa(0, 0)
-        for q in range(4):
-            nc.sync.dma_start(tab2_s[32 * q : 32 * q + 4, :].bitcast(I32),
-                              tab2_scales[0, 4 * q : 4 * q + 4, :].bitcast(I32))
-        gather_words(1, 0, S // 2)
-        gather_words(1, S // 2, S)
-        load_wa(1, SLOT)
+        b_ps = {}
 
-        def permuted(ap):
-            return ap.rearrange("j (p u e) -> j u p e", u=2, e=2)
-
-        def plain(ap):
-            return ap.rearrange("j (u p e) -> j u p e", u=2, e=2)
-
-        mag = [sb("mag%d" % g, [P, H], F32) for g in range(VIEW_TILES)]
-        root = [sb("root%d" % g, [P, H], F32) for g in range(VIEW_TILES)]
-        damp = [sb("damp%d" % g, [P, H], F32) for g in range(VIEW_TILES)]
-        for g in range(VIEW_TILES):
-            if g % 2 == 0:
-                gather_words(2, P * g, P * (g + 2))
-            cols = slice(P * g, P * (g + 1))
-            b_ps = bank(g % 4, "b_ps%d" % g)
-            for a in range(PASSES):
-                nc.tensor.matmul_mx(out=b_ps[:], lhsT=v_w[a, g], lhsT_scale=v_s[a][:, cols],
-                                    rhs=wb_w[:, a, :].bitcast(FP4X4), rhs_scale=wb_s[:, a, :],
-                                    start=(a == 0), stop=(a == PASSES - 1))
-            nc.scalar.activation(plain(mag[g][:]), permuted(b_ps[:]), ACT.Abs)
-
-
-        def quantise_wa(a):
-            wa_bf = sb("wa_bf%d" % a, [P, H, 4], BF16)
-            nc.vector.tensor_copy(wa_bf[:],
-                                  wa_raw[a][:].rearrange("p t n -> p n t"))
-            nc.vector.quantize_mx(out=wa_w[a][:].bitcast(FP8X4), scales=wa_s[a][:],
-                                  in_=wa_bf[:].rearrange("p n t -> p (n t)"))
-
-        a_ps = [bank((g + 4) % 8, "a_ps%d" % g) for g in range(VIEW_TILES)]
-
-        def project_a(a, g):
-            cols = slice(P * g, P * (g + 1))
-            nc.tensor.matmul_mx(out=a_ps[g][:], lhsT=v_w[a, g], lhsT_scale=v_s[a][:, cols],
-                                rhs=wa_w[a][:].bitcast(FP8X4), rhs_scale=wa_s[a][:],
+        def project_b(a, g):
+            if a == 0:
+                b_ps[g] = bank(g % B_BANKS, "b_ps%d" % g)
+            nc.tensor.matmul_mx(out=b_ps[g][:], lhsT=v_w[a, g], lhsT_scale=v_s(a, g),
+                                rhs=wb_w[:, a, :].bitcast(FP4X4), rhs_scale=wb_s[:, a, :],
                                 start=(a == 0), stop=(a == PASSES - 1))
 
-        def square(g):
-            if SQUARE_ON[g] == "s":
-                nc.scalar.activation(damp[g][:], root[g][:], ACT.Square)
-            elif SQUARE_ON[g] == "v":
-                nc.vector.tensor_tensor(damp[g][:], root[g][:], root[g][:], ALU.mult)
-            else:
-                nc.gpsimd.tensor_tensor(damp[g][:], root[g][:], root[g][:], ALU.mult)
+        gather_words(0, 0, HALF)
+        for j0 in (0, HALF):
+            cols = slice(j0, j0 + HALF)
+            nc.vector.tensor_copy(v_s_packed[:, cols], tab_s[:].indirect(offs_sb[:, j0 // 16 : (j0 + HALF) // 16]))
+            for a, queue in ((1, nc.scalar), (2, nc.sync)):
+                queue.dma_start(v_s_shifted[0:112, a - 1, cols].bitcast(I32),
+                                v_s_packed[4 * a : 4 * a + 112, cols].bitcast(I32))
+        load_wa(0, 0)
+        load_wa(1, 8 * KIB)
+        gather_words(1, 0, HALF)
+        for a in range(2):
+            for g in range(B_BANKS):
+                project_b(a, g)
+        gather_words(2, 0, 2 * P)
+        gather_words(2, 2 * P, HALF)
+        gather_words(2, HALF, S)
+        gather_words(1, HALF, S, 28 * KIB)
+        gather_words(0, HALF, S, 30 * KIB)
+        load_wa(2, 16 * KIB)
 
-        load_wa(2, 2 * SLOT + S2)
+        def woven(ap):
+            return ap.rearrange("p (t j) -> p j t", t=4)
+
+        def plain(ap):
+            return ap.rearrange("p (j t) -> p j t", t=4)
+
+        mag = [sb("mag%d" % g, [P, H], F32) for g in range(VIEW_TILES)]
+        root = [sb("root%d" % n, [P, 2, H], F32) for n in range(PAIRS)]
+        damp = [sb("damp%d" % n, [P, 2, H], F32) for n in range(PAIRS)]
+        for step in range(VIEW_TILES + 2):
+            if step < VIEW_TILES:
+                if step >= B_BANKS:
+                    project_b(0, step)
+                    project_b(1, step)
+                project_b(2, step)
+                nc.scalar.activation(mag[step][:].rearrange("j (t m) -> j t m", t=4),
+                                     b_ps[step][:].rearrange("j (m t) -> j t m", t=4), ACT.Abs)
+            g = step - 2
+            if g >= 0:
+                turned = bank(g % B_BANKS, "turned%d" % g)
+                for t in range(4):
+                    cols = slice(P * t, P * (t + 1))
+                    nc.tensor.transpose(turned[:, cols], mag[g][:, cols], ident[:])
+                nc.scalar.activation(plain(root[g // 2][:, g % 2, :]), woven(turned[:]),
+                                     ACT.Abs_reciprocal_sqrt, bias=1.0)
+                if g % 2 == 1 and g < TILES_SQUARED_ON_SCALAR:
+                    nc.scalar.activation(damp[g // 2][:], root[g // 2][:], ACT.Square)
+                elif g == TILES_SQUARED_ON_SCALAR - 1:
+                    nc.scalar.activation(damp[g // 2][:, 0, :], root[g // 2][:, 0, :], ACT.Square)
+
+        a_ps = {}
+
+        def a_bank(g):
+            return B_BANKS + g % A_BANKS
+
+        def project_a(a, g):
+            if a == 0:
+                a_ps[g] = bank(a_bank(g), "a_ps%d" % g)
+            for t in range(4):
+                cols = slice(P * t, P * (t + 1))
+                nc.tensor.matmul_mx(out=a_ps[g][:, cols], lhsT=wa_w[a][:, cols].bitcast(FP8X4),
+                                    lhsT_scale=wa_s[a][:, cols], rhs=v_w[a, g], rhs_scale=v_s(a, g),
+                                    start=(a == 0 and t == 0), stop=(a == PASSES - 1 and t == 3))
+
+        for a in range(PASSES):
+            wa_bf = sb("wa_bf%d" % a, [P, 4 * H], BF16)
+            dealt = wa_bf[:].rearrange("p (u v m j) -> p u m j v", u=2, v=2, j=4)
+            rows = wa_raw[a][:].rearrange("p j (m u v) -> p u m j v", u=2, v=2)
+            for u in range(2):
+                nc.vector.tensor_copy(dealt[:, u], rows[:, u])
+            for u in range(2):
+                cols = slice(2 * P * u, 2 * P * (u + 1))
+                nc.vector.quantize_mx(out=wa_w[a][:, cols].bitcast(FP8X4), scales=wa_s[a][:, cols],
+                                      in_=wa_bf[:, 8 * P * u : 8 * P * (u + 1)])
+            if a == 0:
+                tab2_w = sb("tab2_w", [P, T2], I32, 0)
+                nc.sync.dma_start(tab2_w[:], tab2_words[0].rearrange("p n t -> p (n t)").bitcast(I32))
+                tab2_s = sb("tab2_s", [P, T2], U8, 5 * KIB)
+                nc.gpsimd.memset(tab2_s[:].bitcast(I32), 0)
+                for q in range(4):
+                    nc.sync.dma_start(tab2_s[32 * q : 32 * q + 4, :].bitcast(I32),
+                                      tab2_scales[0, 4 * q : 4 * q + 4, :].bitcast(I32))
+                bias = sb("bias", [P, S2 // P], F32, 4 * KIB)
+                with nc.allow_non_contiguous_dma(reason="one bias value a partition"):
+                    nc.sync.dma_start(bias[:], c.rearrange("(n p) -> p n", p=P))
+            for g in range(A_BANKS):
+                project_a(a, g)
         nc.vector.tensor_copy(v2_w[:], tab2_w[:].bitcast(U32).indirect(offs2_sb[:]))
-        v2_s = sb("v2_s", [P, S2], U8, 2 * SLOT)
         nc.vector.tensor_copy(v2_s[:], tab2_s[:].indirect(offs2_sb[:]))
-        quantise_wa(0)
-        quantise_wa(1)
-        quantise_wa(2)
-        for g in range(VIEW_TILES):
-            nc.scalar.activation(root[g][:], mag[g][:], ACT.Abs_reciprocal_sqrt, bias=1.0)
-            if SQUARE_ON[g] != "v":
-                square(g)
-        warm_tanh = sb("warm_tanh", [P, 8], F32)
-        nc.scalar.activation(warm_tanh[:], root[VIEW_TILES - 1][:, 0:8], ACT.Tanh)
 
         first = 0
-        projected = 0
         for tiles in CHUNK_TILES:
             width = P * tiles
-            while projected < min(first + tiles + 2, VIEW_TILES):
-                for a in range(PASSES):
-                    project_a(a, projected)
-                projected += 1
             h_bf = sb("h_bf%d" % first, [P, tiles, H], BF16)
             for n in range(tiles):
                 g = first + n
-                if SQUARE_ON[g] == "v":
-                    square(g)
-                nc.vector.tensor_tensor(plain(h_bf[:, n, :]), permuted(a_ps[g][:]), plain(damp[g][:]), ALU.mult)
-            h_words = h_bf[:].rearrange("j g r -> j (g r)").bitcast(F32)
-            ht_ps = bank((first + 4) % 8, "ht_ps%d" % first)
-            for n in range(2 * tiles):
-                nc.tensor.transpose(ht_ps[:, P * n : P * (n + 1)], h_words[:, P * n : P * (n + 1)], ident[:])
-            ht_bf = sb("ht_bf%d" % first, [P, 4 * width], BF16)
-            nc.vector.tensor_copy(ht_bf[:].bitcast(F32).rearrange("p (g j u) -> p g j u", g=tiles, u=2),
-                                  ht_ps[:, 0 : 2 * width].rearrange("p (g u j) -> p g j u", g=tiles, u=2))
+                if g >= TILES_SQUARED_ON_SCALAR:
+                    one = root[g // 2][:, g % 2, :]
+                    nc.vector.tensor_tensor(damp[g // 2][:, g % 2, :], one, one, ALU.mult)
+                nc.vector.tensor_tensor(plain(h_bf[:, n, :]), woven(a_ps[g][:]), plain(damp[g // 2][:, g % 2, :]),
+                                        ALU.mult)
+                if g + A_BANKS < VIEW_TILES:
+                    for a in range(PASSES):
+                        project_a(a, g + A_BANKS)
             h_w = sb("h_w%d" % first, [P, width], U32)
             h_s = sb("h_s%d" % first, [P, width], U8)
-            nc.vector.quantize_mx(out=h_w[:].bitcast(FP8X4), scales=h_s[:], in_=ht_bf[:])
-            y_ps = [bank((first + 3 + tiles - n) % 8, "y_ps%d_%d" % (first, n)) for n in range(tiles)]
+            nc.vector.quantize_mx(out=h_w[:].bitcast(FP8X4), scales=h_s[:],
+                                  in_=h_bf[:].rearrange("p g r -> p (g r)"))
+            y_ps = [bank(g if g < B_BANKS else a_bank(g), "y_ps%d" % g) for g in range(first, first + tiles)]
             for i in range(S2 // P):
                 rows = slice(P * i, P * (i + 1))
                 place = (i * width) % 512
                 nc.tensor.matmul_mx(out=y_ps[i * width // 512][:, place : place + width],
                                     lhsT=v2_w[:, rows].bitcast(FP8X4), lhsT_scale=v2_s[:, rows],
                                     rhs=h_w[:].bitcast(FP8X4), rhs_scale=h_s[:], start=True, stop=True)
-            for pair in range(2):
-                res = sb("res%d_%d" % (first, pair), [P, 2, width], F32)
-                for n in range(2):
-                    i = 2 * pair + n
+            rows_a_store = min(2, 4 // tiles)
+            for i0 in range(0, S2 // P, rows_a_store):
+                res = sb("res%d_%d" % (first, i0), [P, rows_a_store, width], F32)
+                for n in range(rows_a_store):
+                    i = i0 + n
                     place = (i * width) % 512
                     nc.scalar.activation(res[:, n, :], y_ps[i * width // 512][:, place : place + width], ACT.Tanh,
                                          bias=bias[:, i : i + 1])
                 nc.sync.dma_start(
-                    out[2 * P * pair : 2 * P * (pair + 1), P * first : P * first + width].rearrange("(n p) j -> p n j", p=P),
+                    out[P * i0 : P * (i0 + rows_a_store), P * first : P * first + width].rearrange("(n p) j -> p n j", p=P),
                     res[:])
             first += tiles

@@ -21,11 +21,11 @@ P = 128
 PASSES = K // 512
 VIEW_TILES = S // P
 HALF = S // 2
-CHUNK_TILES = (4, 2, 2)
+CHUNK_TILES = (2, 4, 1, 1)
 B_BANKS = 4
 A_BANKS = 8 - B_BANKS
 PAIRS = VIEW_TILES // 2
-TILES_SQUARED_ON_SCALAR = 7
+TILES_SQUARED_ON_VECTOR = 3
 KIB = 1024
 
 
@@ -113,24 +113,29 @@ def tile_list_grasp_view_value_kernel(tc, tab_words, tab_scales, offs, tab2_word
                                 start=(a == 0), stop=(a == PASSES - 1))
 
         gather_words(0, 0, HALF)
-        for j0 in (0, HALF):
+        def shift_scales(j0):
             cols = slice(j0, j0 + HALF)
-            nc.vector.tensor_copy(v_s_packed[:, cols], tab_s[:].indirect(offs_sb[:, j0 // 16 : (j0 + HALF) // 16]))
-            for a, queue in ((1, nc.scalar), (2, nc.sync)):
-                queue.dma_start(v_s_shifted[0:112, a - 1, cols].bitcast(I32),
-                                v_s_packed[4 * a : 4 * a + 112, cols].bitcast(I32))
+            for a in range(1, PASSES):
+                nc.sync.dma_start(v_s_shifted[0:112, a - 1, cols].bitcast(I32),
+                                  v_s_packed[4 * a : 4 * a + 112, cols].bitcast(I32))
+
+        for j0 in (0, HALF):
+            nc.vector.tensor_copy(v_s_packed[:, j0 : j0 + HALF],
+                                  tab_s[:].indirect(offs_sb[:, j0 // 16 : (j0 + HALF) // 16]))
+        shift_scales(0)
         load_wa(0, 0)
+        shift_scales(HALF)
         load_wa(1, 8 * KIB)
         gather_words(1, 0, HALF)
+        gather_words(1, HALF, S)
+        load_wa(2, 16 * KIB)
         for a in range(2):
             for g in range(B_BANKS):
                 project_b(a, g)
         gather_words(2, 0, 2 * P)
         gather_words(2, 2 * P, HALF)
         gather_words(2, HALF, S)
-        gather_words(1, HALF, S, 28 * KIB)
         gather_words(0, HALF, S, 30 * KIB)
-        load_wa(2, 16 * KIB)
 
         def woven(ap):
             return ap.rearrange("p (t j) -> p j t", t=4)
@@ -141,6 +146,18 @@ def tile_list_grasp_view_value_kernel(tc, tab_words, tab_scales, offs, tab2_word
         mag = [sb("mag%d" % g, [P, H], F32) for g in range(VIEW_TILES)]
         root = [sb("root%d" % n, [P, 2, H], F32) for n in range(PAIRS)]
         damp = [sb("damp%d" % n, [P, 2, H], F32) for n in range(PAIRS)]
+
+        def square(last):
+            on_vector = last < TILES_SQUARED_ON_VECTOR
+            begin = last if last == TILES_SQUARED_ON_VECTOR else last - last % 2
+            part = slice(begin % 2, last % 2 + 1)
+            src = root[last // 2][:, part, :].rearrange("p n r -> p (n r)")
+            dst = damp[last // 2][:, part, :].rearrange("p n r -> p (n r)")
+            if on_vector:
+                nc.vector.tensor_tensor(dst, src, src, ALU.mult)
+            else:
+                nc.scalar.activation(dst, src, ACT.Square)
+
         for step in range(VIEW_TILES + 2):
             if step < VIEW_TILES:
                 if step >= B_BANKS:
@@ -157,10 +174,8 @@ def tile_list_grasp_view_value_kernel(tc, tab_words, tab_scales, offs, tab2_word
                     nc.tensor.transpose(turned[:, cols], mag[g][:, cols], ident[:])
                 nc.scalar.activation(plain(root[g // 2][:, g % 2, :]), woven(turned[:]),
                                      ACT.Abs_reciprocal_sqrt, bias=1.0)
-                if g % 2 == 1 and g < TILES_SQUARED_ON_SCALAR:
-                    nc.scalar.activation(damp[g // 2][:], root[g // 2][:], ACT.Square)
-                elif g == TILES_SQUARED_ON_SCALAR - 1:
-                    nc.scalar.activation(damp[g // 2][:, 0, :], root[g // 2][:, 0, :], ACT.Square)
+                if g % 2 == 1 or g + 1 == TILES_SQUARED_ON_VECTOR:
+                    square(g)
 
         a_ps = {}
 
@@ -208,9 +223,6 @@ def tile_list_grasp_view_value_kernel(tc, tab_words, tab_scales, offs, tab2_word
             h_bf = sb("h_bf%d" % first, [P, tiles, H], BF16)
             for n in range(tiles):
                 g = first + n
-                if g >= TILES_SQUARED_ON_SCALAR:
-                    one = root[g // 2][:, g % 2, :]
-                    nc.vector.tensor_tensor(damp[g // 2][:, g % 2, :], one, one, ALU.mult)
                 nc.vector.tensor_tensor(plain(h_bf[:, n, :]), woven(a_ps[g][:]), plain(damp[g // 2][:, g % 2, :]),
                                         ALU.mult)
                 if g + A_BANKS < VIEW_TILES:

@@ -21,9 +21,7 @@ P = 128
 PASSES = K // 512
 VIEW_TILES = S // P
 HALF = S // 2
-CHUNK_TILES = (2, 4, 1, 1)
-B_BANKS = 4
-A_BANKS = 8 - B_BANKS
+CHUNK_TILES = (2, 4, 2)
 PAIRS = VIEW_TILES // 2
 TILES_SQUARED_ON_VECTOR = 3
 KIB = 1024
@@ -106,11 +104,12 @@ def tile_list_grasp_view_value_kernel(tc, tab_words, tab_scales, offs, tab2_word
         b_ps = {}
 
         def project_b(a, g):
-            if a == 0:
-                b_ps[g] = bank(g % B_BANKS, "b_ps%d" % g)
+            order = (0, 1, 2) if g < VIEW_TILES // 2 else (2, 1, 0)
+            if a == order[0]:
+                b_ps[g] = bank(g, "b_ps%d" % g)
             nc.tensor.matmul_mx(out=b_ps[g][:], lhsT=v_w[a, g], lhsT_scale=v_s(a, g),
                                 rhs=wb_w[:, a, :].bitcast(FP4X4), rhs_scale=wb_s[:, a, :],
-                                start=(a == 0), stop=(a == PASSES - 1))
+                                start=(a == order[0]), stop=(a == order[-1]))
 
         gather_words(0, 0, HALF)
         def shift_scales(j0):
@@ -129,8 +128,13 @@ def tile_list_grasp_view_value_kernel(tc, tab_words, tab_scales, offs, tab2_word
         gather_words(1, 0, HALF)
         gather_words(1, HALF, S)
         load_wa(2, 16 * KIB)
+        tab2_s = sb("tab2_s", [P, T2], U8, 24 * KIB)
+        nc.gpsimd.memset(tab2_s[:].bitcast(I32), 0)
+        for q in range(4):
+            nc.sync.dma_start(tab2_s[32 * q : 32 * q + 4, :].bitcast(I32),
+                              tab2_scales[0, 4 * q : 4 * q + 4, :].bitcast(I32))
         for a in range(2):
-            for g in range(B_BANKS):
+            for g in range(VIEW_TILES // 2):
                 project_b(a, g)
         gather_words(2, 0, 2 * P)
         gather_words(2, 2 * P, HALF)
@@ -160,15 +164,15 @@ def tile_list_grasp_view_value_kernel(tc, tab_words, tab_scales, offs, tab2_word
 
         for step in range(VIEW_TILES + 2):
             if step < VIEW_TILES:
-                if step >= B_BANKS:
-                    project_b(0, step)
-                    project_b(1, step)
                 project_b(2, step)
+                if step >= VIEW_TILES // 2:
+                    project_b(1, step)
+                    project_b(0, step)
                 nc.scalar.activation(mag[step][:].rearrange("j (t m) -> j t m", t=4),
                                      b_ps[step][:].rearrange("j (m t) -> j t m", t=4), ACT.Abs)
             g = step - 2
             if g >= 0:
-                turned = bank(g % B_BANKS, "turned%d" % g)
+                turned = bank(g + 1 - 2 * (g % 2), "turned%d" % g)
                 for t in range(4):
                     cols = slice(P * t, P * (t + 1))
                     nc.tensor.transpose(turned[:, cols], mag[g][:, cols], ident[:])
@@ -179,12 +183,9 @@ def tile_list_grasp_view_value_kernel(tc, tab_words, tab_scales, offs, tab2_word
 
         a_ps = {}
 
-        def a_bank(g):
-            return B_BANKS + g % A_BANKS
-
         def project_a(a, g):
             if a == 0:
-                a_ps[g] = bank(a_bank(g), "a_ps%d" % g)
+                a_ps[g] = bank(g + 1 - 2 * (g % 2), "a_ps%d" % g)
             for t in range(4):
                 cols = slice(P * t, P * (t + 1))
                 nc.tensor.matmul_mx(out=a_ps[g][:, cols], lhsT=wa_w[a][:, cols].bitcast(FP8X4),
@@ -204,18 +205,20 @@ def tile_list_grasp_view_value_kernel(tc, tab_words, tab_scales, offs, tab2_word
             if a == 0:
                 tab2_w = sb("tab2_w", [P, T2], I32, 0)
                 nc.sync.dma_start(tab2_w[:], tab2_words[0].rearrange("p n t -> p (n t)").bitcast(I32))
-                tab2_s = sb("tab2_s", [P, T2], U8, 5 * KIB)
-                nc.gpsimd.memset(tab2_s[:].bitcast(I32), 0)
-                for q in range(4):
-                    nc.sync.dma_start(tab2_s[32 * q : 32 * q + 4, :].bitcast(I32),
-                                      tab2_scales[0, 4 * q : 4 * q + 4, :].bitcast(I32))
                 bias = sb("bias", [P, S2 // P], F32, 4 * KIB)
                 with nc.allow_non_contiguous_dma(reason="one bias value a partition"):
                     nc.sync.dma_start(bias[:], c.rearrange("(n p) -> p n", p=P))
-            for g in range(A_BANKS):
+            for g in range(VIEW_TILES // 2):
                 project_a(a, g)
         nc.vector.tensor_copy(v2_w[:], tab2_w[:].bitcast(U32).indirect(offs2_sb[:]))
         nc.vector.tensor_copy(v2_s[:], tab2_s[:].indirect(offs2_sb[:]))
+
+        def project_a_whole(tiles):
+            for g in tiles:
+                for a in range(PASSES):
+                    project_a(a, g)
+
+        project_a_whole(range(VIEW_TILES // 2, VIEW_TILES - 2))
 
         first = 0
         for tiles in CHUNK_TILES:
@@ -225,20 +228,19 @@ def tile_list_grasp_view_value_kernel(tc, tab_words, tab_scales, offs, tab2_word
                 g = first + n
                 nc.vector.tensor_tensor(plain(h_bf[:, n, :]), woven(a_ps[g][:]), plain(damp[g // 2][:, g % 2, :]),
                                         ALU.mult)
-                if g + A_BANKS < VIEW_TILES:
-                    for a in range(PASSES):
-                        project_a(a, g + A_BANKS)
             h_w = sb("h_w%d" % first, [P, width], U32)
             h_s = sb("h_s%d" % first, [P, width], U8)
             nc.vector.quantize_mx(out=h_w[:].bitcast(FP8X4), scales=h_s[:],
                                   in_=h_bf[:].rearrange("p g r -> p (g r)"))
-            y_ps = [bank(g if g < B_BANKS else a_bank(g), "y_ps%d" % g) for g in range(first, first + tiles)]
+            y_ps = [bank(g + 1 - 2 * (g % 2), "y_ps%d" % g) for g in range(first, first + tiles)]
             for i in range(S2 // P):
                 rows = slice(P * i, P * (i + 1))
                 place = (i * width) % 512
                 nc.tensor.matmul_mx(out=y_ps[i * width // 512][:, place : place + width],
                                     lhsT=v2_w[:, rows].bitcast(FP8X4), lhsT_scale=v2_s[:, rows],
                                     rhs=h_w[:].bitcast(FP8X4), rhs_scale=h_s[:], start=True, stop=True)
+            if first == 0:
+                project_a_whole(range(VIEW_TILES - 2, VIEW_TILES))
             rows_a_store = min(2, 4 // tiles)
             for i0 in range(0, S2 // P, rows_a_store):
                 res = sb("res%d_%d" % (first, i0), [P, rows_a_store, width], F32)

@@ -56,12 +56,9 @@ def tile_list_grasp_view_value_kernel(tc, tab_words, tab_scales, offs, tab2_word
         v2_w = sb("v2_w", [P, S2], U32)
         v2_s = sb("v2_s", [P, S2], U8)
         ident = sb("ident", [P, P], F32)
-        warm = sb("warm", [P, 8], F32)
-        warm_out = sb("warm_out", [P, 8], F32)
 
         nc.gpsimd.memset(tab_s[:].bitcast(I32), 0)
         nc.gpsimd.memset(wb_s[:].rearrange("p a n -> p (a n)").bitcast(I32), 0)
-        nc.vector.memset(warm[:], 1.0)
         nc.vector.memset(v_s_shifted[96:128, :, :].rearrange("p a n -> p (a n)").bitcast(I32), 0)
         make_identity(nc, ident[:])
 
@@ -75,7 +72,6 @@ def tile_list_grasp_view_value_kernel(tc, tab_words, tab_scales, offs, tab2_word
             queue = nc.sync if q < 2 else nc.scalar
             queue.dma_start(tab_s[32 * q : 32 * q + 4 * PASSES, :].bitcast(I32),
                             tab_scales[:, 4 * q : 4 * q + 4, :].bitcast(I32))
-        nc.scalar.activation(warm_out[:], warm[:], ACT.Abs_reciprocal_sqrt)
         nc.sync.dma_start(wb_w[:].bitcast(I32), wb_words.rearrange("a p n -> p a n").bitcast(I32))
         load_table(1)
         for q in range(4):

@@ -23,7 +23,7 @@ VIEW_TILES = S // P
 HALF = S // 2
 CHUNK_TILES = (2, 4, 2)
 PAIRS = VIEW_TILES // 2
-TILES_SQUARED_ON_VECTOR = 3
+TILES_SQUARED_ON_VECTOR = 2
 KIB = 1024
 
 
@@ -43,41 +43,55 @@ def tile_list_grasp_view_value_kernel(tc, tab_words, tab_scales, offs, tab2_word
         def bank(index, name):
             return psum.tile([P, 512], F32, name=name, tag="bank%d" % index)
 
+        def partner(g):
+            return g + 1 - 2 * (g % 2)
+
         offs_sb = keep.tile([P, S // 16], U16, name="offs_sb")
         offs2_sb = keep.tile([P, S2 // 16], U16, name="offs2_sb")
-        tab_s = sb("tab_s", [P, T], U8, 7 * KIB)
-        tab_w = [sb("tab_w%d" % a, [P, T], I32, (None, 20 * KIB, 28 * KIB)[a]) for a in range(PASSES)]
+        tab_s = sb("tab_s", [P, T], U8, 8 * KIB)
+        tab_w = [sb("tab_w%d" % a, [P, T], I32, (None, None, 0)[a]) for a in range(PASSES)]
+        tab2_w = sb("tab2_w", [P, T2], I32)
+        tab2_s = sb("tab2_s", [P, T2], U8)
         wb_w = sb("wb_w", [P, PASSES, 2 * H], U8)
         wb_s = sb("wb_s", [P, PASSES, H], U8)
+        wa_raw = [sb("wa_raw%d" % a, [P, 4, H], F32) for a in range(PASSES)]
         wa_w = [sb("wa_w%d" % a, [P, H], U32) for a in range(PASSES)]
         wa_s = [sb("wa_s%d" % a, [P, H], U8) for a in range(PASSES)]
         v_s_packed = sb("v_s_packed", [P, S], U8)
-        v_s_shifted = sb("v_s_shifted", [P, PASSES - 1, S], U8)
+        v_s_shifted = [sb("v_s_shifted%d" % a, [P, S], U8) for a in range(1, PASSES)]
         v2_w = sb("v2_w", [P, S2], U32)
         v2_s = sb("v2_s", [P, S2], U8)
+        bias = sb("bias", [P, S2 // P], F32)
         ident = sb("ident", [P, P], F32)
 
         nc.gpsimd.memset(tab_s[:].bitcast(I32), 0)
         nc.gpsimd.memset(wb_s[:].rearrange("p a n -> p (a n)").bitcast(I32), 0)
-        nc.vector.memset(v_s_shifted[96:128, :, :].rearrange("p a n -> p (a n)").bitcast(I32), 0)
+        for plane in v_s_shifted:
+            nc.vector.memset(plane[96:128, :].bitcast(I32), 0)
         make_identity(nc, ident[:])
+        nc.gpsimd.memset(tab2_s[:].bitcast(I32), 0)
 
         def load_table(a):
             nc.sync.dma_start(tab_w[a][:], tab_words[a].rearrange("p n t -> p (n t)").bitcast(I32))
 
+        def load_wa(a):
+            nc.sync.dma_start(wa_raw[a][:], wa[512 * a : 512 * (a + 1), :].rearrange("(p j) r -> p j r", j=4))
+
         nc.sync.dma_start(offs_sb[:], offs)
         load_table(0)
-        nc.sync.dma_start(offs2_sb[:], offs2)
         for q in range(4):
-            queue = nc.sync if q < 2 else nc.scalar
+            queue = nc.scalar if q < 2 else nc.sync
             queue.dma_start(tab_s[32 * q : 32 * q + 4 * PASSES, :].bitcast(I32),
-                            tab_scales[:, 4 * q : 4 * q + 4, :].bitcast(I32))
+                                tab_scales[:, 4 * q : 4 * q + 4, :].bitcast(I32))
         nc.sync.dma_start(wb_w[:].bitcast(I32), wb_words.rearrange("a p n -> p a n").bitcast(I32))
         load_table(1)
         for q in range(4):
             nc.sync.dma_start(wb_s[32 * q : 32 * q + 4, :, :].bitcast(I32),
                               wb_scales[:, 4 * q : 4 * q + 4, :].rearrange("a r n -> r a n").bitcast(I32))
         load_table(2)
+
+        warm = sb("warm", [P, 1], F32)
+        nc.scalar.activation(warm[:], ident[:, 0:1], ACT.Abs_reciprocal_sqrt, bias=1.0)
 
         v_w = {}
 
@@ -88,54 +102,42 @@ def tile_list_grasp_view_value_kernel(tc, tab_words, tab_scales, offs, tab2_word
                 v_w[a, g] = words[:, P * g - j0 : P * (g + 1) - j0].bitcast(FP8X4)
 
         def v_s(a, g):
-            plane = v_s_packed[:] if a == 0 else v_s_shifted[:, a - 1, :]
+            plane = v_s_packed if a == 0 else v_s_shifted[a - 1]
             return plane[:, P * g : P * (g + 1)]
 
-        wa_raw = {}
+        gather_words(0, 0, HALF)
+        nc.vector.tensor_copy(v_s_packed[:], tab_s[:].indirect(offs_sb[:]))
+        for a in range(1, PASSES):
+            queue = nc.sync if a == 1 else nc.scalar
+            queue.dma_start(v_s_shifted[a - 1][0:112, :].bitcast(I32),
+                              v_s_packed[4 * a : 4 * a + 112, :].bitcast(I32))
+        load_wa(0)
+        load_wa(1)
+        for q in range(4):
+            nc.sync.dma_start(tab2_s[32 * q : 32 * q + 4, :].bitcast(I32),
+                              tab2_scales[0, 4 * q : 4 * q + 4, :].bitcast(I32))
+        load_wa(2)
+        nc.sync.dma_start(offs2_sb[:], offs2)
+        nc.sync.dma_start(tab2_w[:], tab2_words[0].rearrange("p n t -> p (n t)").bitcast(I32))
+        with nc.allow_non_contiguous_dma(reason="one bias value a partition"):
+            nc.sync.dma_start(bias[:], c.rearrange("(n p) -> p n", p=P))
 
-        def load_wa(a, offset):
-            wa_raw[a] = sb("wa_raw%d" % a, [P, 4, H], F32, offset)
-            nc.sync.dma_start(wa_raw[a][:], wa[512 * a : 512 * (a + 1), :].rearrange("(p j) r -> p j r", j=4))
+        gather_words(0, HALF, S, 8 * KIB)
+        gather_words(1, 0, HALF)
+        gather_words(2, 0, 2 * P)
+        gather_words(2, 2 * P, HALF)
+        gather_words(2, HALF, S)
+        gather_words(1, HALF, S, 0)
 
         b_ps = {}
 
         def project_b(a, g):
-            order = (0, 1, 2) if g < VIEW_TILES // 2 else (2, 1, 0)
+            order = (0, 1, 2) if g < VIEW_TILES // 2 else (0, 2, 1)
             if a == order[0]:
                 b_ps[g] = bank(g, "b_ps%d" % g)
             nc.tensor.matmul_mx(out=b_ps[g][:], lhsT=v_w[a, g], lhsT_scale=v_s(a, g),
                                 rhs=wb_w[:, a, :].bitcast(FP4X4), rhs_scale=wb_s[:, a, :],
                                 start=(a == order[0]), stop=(a == order[-1]))
-
-        gather_words(0, 0, HALF)
-        def shift_scales(j0):
-            cols = slice(j0, j0 + HALF)
-            for a in range(1, PASSES):
-                nc.sync.dma_start(v_s_shifted[0:112, a - 1, cols].bitcast(I32),
-                                  v_s_packed[4 * a : 4 * a + 112, cols].bitcast(I32))
-
-        for j0 in (0, HALF):
-            nc.vector.tensor_copy(v_s_packed[:, j0 : j0 + HALF],
-                                  tab_s[:].indirect(offs_sb[:, j0 // 16 : (j0 + HALF) // 16]))
-        shift_scales(0)
-        load_wa(0, 0)
-        shift_scales(HALF)
-        load_wa(1, 8 * KIB)
-        gather_words(1, 0, HALF)
-        gather_words(1, HALF, S)
-        load_wa(2, 16 * KIB)
-        tab2_s = sb("tab2_s", [P, T2], U8, 24 * KIB)
-        nc.gpsimd.memset(tab2_s[:].bitcast(I32), 0)
-        for q in range(4):
-            nc.sync.dma_start(tab2_s[32 * q : 32 * q + 4, :].bitcast(I32),
-                              tab2_scales[0, 4 * q : 4 * q + 4, :].bitcast(I32))
-        for a in range(2):
-            for g in range(VIEW_TILES // 2):
-                project_b(a, g)
-        gather_words(2, 0, 2 * P)
-        gather_words(2, 2 * P, HALF)
-        gather_words(2, HALF, S)
-        gather_words(0, HALF, S, 30 * KIB)
 
         def woven(ap):
             return ap.rearrange("p (t j) -> p j t", t=4)
@@ -144,51 +146,58 @@ def tile_list_grasp_view_value_kernel(tc, tab_words, tab_scales, offs, tab2_word
             return ap.rearrange("p (j t) -> p j t", t=4)
 
         mag = [sb("mag%d" % g, [P, H], F32) for g in range(VIEW_TILES)]
-        root = [sb("root%d" % n, [P, 2, H], F32) for n in range(PAIRS)]
-        damp = [sb("damp%d" % n, [P, 2, H], F32) for n in range(PAIRS)]
+        root = [sb("root%d" % n, [P, 2 * H], F32) for n in range(PAIRS)]
+        damp = [sb("damp%d" % n, [P, 2 * H], F32) for n in range(PAIRS)]
 
-        def square(last):
-            on_vector = last < TILES_SQUARED_ON_VECTOR
-            begin = last if last == TILES_SQUARED_ON_VECTOR else last - last % 2
-            part = slice(begin % 2, last % 2 + 1)
-            src = root[last // 2][:, part, :].rearrange("p n r -> p (n r)")
-            dst = damp[last // 2][:, part, :].rearrange("p n r -> p (n r)")
-            if on_vector:
-                nc.vector.tensor_tensor(dst, src, src, ALU.mult)
-            else:
-                nc.scalar.activation(dst, src, ACT.Square)
+        def magnitude(g):
+            nc.scalar.activation(mag[g][:].rearrange("j (t m) -> j t m", t=4),
+                                 b_ps[g][:].rearrange("j (m t) -> j t m", t=4), ACT.Abs)
 
-        for step in range(VIEW_TILES + 2):
-            if step < VIEW_TILES:
-                project_b(2, step)
-                if step >= VIEW_TILES // 2:
-                    project_b(1, step)
-                    project_b(0, step)
-                nc.scalar.activation(mag[step][:].rearrange("j (t m) -> j t m", t=4),
-                                     b_ps[step][:].rearrange("j (m t) -> j t m", t=4), ACT.Abs)
-            g = step - 2
-            if g >= 0:
-                turned = bank(g + 1 - 2 * (g % 2), "turned%d" % g)
+        def of_tile(pair_tiles, g):
+            return pair_tiles[g // 2][:, H * (g % 2) : H * (g % 2 + 1)]
+
+        def inverse_roots(n):
+            turned = {}
+            for g in (2 * n, 2 * n + 1):
+                turned[g] = bank(partner(g), "turned%d" % g)
                 for t in range(4):
                     cols = slice(P * t, P * (t + 1))
-                    nc.tensor.transpose(turned[:, cols], mag[g][:, cols], ident[:])
-                nc.scalar.activation(plain(root[g // 2][:, g % 2, :]), woven(turned[:]),
+                    nc.tensor.transpose(turned[g][:, cols], mag[g][:, cols], ident[:])
+            for g in (2 * n, 2 * n + 1):
+                nc.scalar.activation(plain(of_tile(root, g)), woven(turned[g][:]),
                                      ACT.Abs_reciprocal_sqrt, bias=1.0)
-                if g % 2 == 1 or g + 1 == TILES_SQUARED_ON_VECTOR:
-                    square(g)
+
+        for g in range(VIEW_TILES):
+            project_b(0, g)
+        for g in range(VIEW_TILES // 2):
+            project_b(1, g)
+            project_b(2, g)
+            magnitude(g)
+        for n in range(PAIRS):
+            inverse_roots(n)
+            if n < PAIRS // 2:
+                for g in (VIEW_TILES // 2 + 2 * n, VIEW_TILES // 2 + 2 * n + 1):
+                    for a in (2, 1):
+                        project_b(a, g)
+                    magnitude(g)
+
+        for g in range(TILES_SQUARED_ON_VECTOR):
+            nc.vector.tensor_tensor(of_tile(damp, g), of_tile(root, g), of_tile(root, g), ALU.mult)
+        for g in range(TILES_SQUARED_ON_VECTOR, VIEW_TILES):
+            nc.scalar.activation(of_tile(damp, g), of_tile(root, g), ACT.Square)
 
         a_ps = {}
 
         def project_a(a, g):
             if a == 0:
-                a_ps[g] = bank(g + 1 - 2 * (g % 2), "a_ps%d" % g)
+                a_ps[g] = bank(partner(g), "a_ps%d" % g)
             for t in range(4):
                 cols = slice(P * t, P * (t + 1))
                 nc.tensor.matmul_mx(out=a_ps[g][:, cols], lhsT=wa_w[a][:, cols].bitcast(FP8X4),
                                     lhsT_scale=wa_s[a][:, cols], rhs=v_w[a, g], rhs_scale=v_s(a, g),
                                     start=(a == 0 and t == 0), stop=(a == PASSES - 1 and t == 3))
 
-        for a in range(PASSES):
+        def quantise_wa(a):
             wa_bf = sb("wa_bf%d" % a, [P, 4 * H], BF16)
             dealt = wa_bf[:].rearrange("p (u v m j) -> p u m j v", u=2, v=2, j=4)
             rows = wa_raw[a][:].rearrange("p j (m u v) -> p u m j v", u=2, v=2)
@@ -198,45 +207,37 @@ def tile_list_grasp_view_value_kernel(tc, tab_words, tab_scales, offs, tab2_word
                 cols = slice(2 * P * u, 2 * P * (u + 1))
                 nc.vector.quantize_mx(out=wa_w[a][:, cols].bitcast(FP8X4), scales=wa_s[a][:, cols],
                                       in_=wa_bf[:, 8 * P * u : 8 * P * (u + 1)])
-            if a == 0:
-                tab2_w = sb("tab2_w", [P, T2], I32, 0)
-                nc.sync.dma_start(tab2_w[:], tab2_words[0].rearrange("p n t -> p (n t)").bitcast(I32))
-                bias = sb("bias", [P, S2 // P], F32, 4 * KIB)
-                with nc.allow_non_contiguous_dma(reason="one bias value a partition"):
-                    nc.sync.dma_start(bias[:], c.rearrange("(n p) -> p n", p=P))
+
+        for a in range(PASSES):
+            quantise_wa(a)
             for g in range(VIEW_TILES // 2):
                 project_a(a, g)
-        nc.vector.tensor_copy(v2_w[:], tab2_w[:].bitcast(U32).indirect(offs2_sb[:]))
         nc.vector.tensor_copy(v2_s[:], tab2_s[:].indirect(offs2_sb[:]))
-
-        def project_a_whole(tiles):
-            for g in tiles:
-                for a in range(PASSES):
-                    project_a(a, g)
-
-        project_a_whole(range(VIEW_TILES // 2, VIEW_TILES - 2))
+        nc.vector.tensor_copy(v2_w[:], tab2_w[:].bitcast(U32).indirect(offs2_sb[:]))
 
         first = 0
+        ahead = VIEW_TILES // 2
         for tiles in CHUNK_TILES:
             width = P * tiles
+            while ahead < min(first + tiles + 4, VIEW_TILES):
+                for a in range(PASSES):
+                    project_a(a, ahead)
+                ahead += 1
             h_bf = sb("h_bf%d" % first, [P, tiles, H], BF16)
             for n in range(tiles):
                 g = first + n
-                nc.vector.tensor_tensor(plain(h_bf[:, n, :]), woven(a_ps[g][:]), plain(damp[g // 2][:, g % 2, :]),
-                                        ALU.mult)
+                nc.vector.tensor_tensor(plain(h_bf[:, n, :]), woven(a_ps[g][:]), plain(of_tile(damp, g)), ALU.mult)
             h_w = sb("h_w%d" % first, [P, width], U32)
             h_s = sb("h_s%d" % first, [P, width], U8)
             nc.vector.quantize_mx(out=h_w[:].bitcast(FP8X4), scales=h_s[:],
                                   in_=h_bf[:].rearrange("p g r -> p (g r)"))
-            y_ps = [bank(g + 1 - 2 * (g % 2), "y_ps%d" % g) for g in range(first, first + tiles)]
+            y_ps = [bank(partner(g), "y_ps%d" % g) for g in range(first, first + tiles)]
             for i in range(S2 // P):
                 rows = slice(P * i, P * (i + 1))
                 place = (i * width) % 512
                 nc.tensor.matmul_mx(out=y_ps[i * width // 512][:, place : place + width],
                                     lhsT=v2_w[:, rows].bitcast(FP8X4), lhsT_scale=v2_s[:, rows],
                                     rhs=h_w[:].bitcast(FP8X4), rhs_scale=h_s[:], start=True, stop=True)
-            if first == 0:
-                project_a_whole(range(VIEW_TILES - 2, VIEW_TILES))
             rows_a_store = min(2, 4 // tiles)
             for i0 in range(0, S2 // P, rows_a_store):
                 res = sb("res%d_%d" % (first, i0), [P, rows_a_store, width], F32)

@@ -23,7 +23,7 @@ VIEW_TILES = S // P
 HALF = S // 2
 CHUNK_TILES = (2, 4, 2)
 PAIRS = VIEW_TILES // 2
-TILES_SQUARED_ON_VECTOR = 2
+TILES_SQUARED_ON_GPSIMD = 3
 KIB = 1024
 
 
@@ -48,7 +48,7 @@ def tile_list_grasp_view_value_kernel(tc, tab_words, tab_scales, offs, tab2_word
 
         offs_sb = keep.tile([P, S // 16], U16, name="offs_sb")
         offs2_sb = keep.tile([P, S2 // 16], U16, name="offs2_sb")
-        tab_s = sb("tab_s", [P, T], U8, 8 * KIB)
+        tab_s = sb("tab_s", [P, T], U8)
         tab_w = [sb("tab_w%d" % a, [P, T], I32, (None, None, 0)[a]) for a in range(PASSES)]
         tab2_w = sb("tab2_w", [P, T2], I32)
         tab2_s = sb("tab2_s", [P, T2], U8)
@@ -64,7 +64,7 @@ def tile_list_grasp_view_value_kernel(tc, tab_words, tab_scales, offs, tab2_word
         bias = sb("bias", [P, S2 // P], F32)
         ident = sb("ident", [P, P], F32)
 
-        nc.gpsimd.memset(tab_s[:].bitcast(I32), 0)
+        nc.vector.memset(tab_s[:].bitcast(I32), 0)
         nc.gpsimd.memset(wb_s[:].rearrange("p a n -> p (a n)").bitcast(I32), 0)
         for plane in v_s_shifted:
             nc.vector.memset(plane[96:128, :].bitcast(I32), 0)
@@ -106,12 +106,20 @@ def tile_list_grasp_view_value_kernel(tc, tab_words, tab_scales, offs, tab2_word
             return plane[:, P * g : P * (g + 1)]
 
         gather_words(0, 0, HALF)
-        nc.vector.tensor_copy(v_s_packed[:], tab_s[:].indirect(offs_sb[:]))
-        for a in range(1, PASSES):
-            queue = nc.sync if a == 1 else nc.scalar
-            queue.dma_start(v_s_shifted[a - 1][0:112, :].bitcast(I32),
-                              v_s_packed[4 * a : 4 * a + 112, :].bitcast(I32))
+        gather_words(0, HALF, S)
+        for j0 in (0, HALF):
+            nc.vector.tensor_copy(v_s_packed[:, j0 : j0 + HALF],
+                                  tab_s[:].indirect(offs_sb[:, j0 // 16 : (j0 + HALF) // 16]))
+
+        def shift_scales(queue, a, j0):
+            queue.dma_start(v_s_shifted[a - 1][0:112, j0 : j0 + HALF].bitcast(I32),
+                            v_s_packed[4 * a : 4 * a + 112, j0 : j0 + HALF].bitcast(I32))
+
+        shift_scales(nc.sync, 1, 0)
+        shift_scales(nc.scalar, 2, 0)
         load_wa(0)
+        shift_scales(nc.sync, 2, HALF)
+        shift_scales(nc.sync, 1, HALF)
         load_wa(1)
         for q in range(4):
             nc.sync.dma_start(tab2_s[32 * q : 32 * q + 4, :].bitcast(I32),
@@ -122,7 +130,6 @@ def tile_list_grasp_view_value_kernel(tc, tab_words, tab_scales, offs, tab2_word
         with nc.allow_non_contiguous_dma(reason="one bias value a partition"):
             nc.sync.dma_start(bias[:], c.rearrange("(n p) -> p n", p=P))
 
-        gather_words(0, HALF, S, 8 * KIB)
         gather_words(1, 0, HALF)
         gather_words(2, 0, 2 * P)
         gather_words(2, 2 * P, HALF)
@@ -147,7 +154,7 @@ def tile_list_grasp_view_value_kernel(tc, tab_words, tab_scales, offs, tab2_word
 
         mag = [sb("mag%d" % g, [P, H], F32) for g in range(VIEW_TILES)]
         root = [sb("root%d" % n, [P, 2 * H], F32) for n in range(PAIRS)]
-        damp = [sb("damp%d" % n, [P, 2 * H], F32) for n in range(PAIRS)]
+        damp = [sb("damp%d" % n, [P, 2 * H], F32, (10 * KIB, 14 * KIB, None, None)[n]) for n in range(PAIRS)]
 
         def magnitude(g):
             nc.scalar.activation(mag[g][:].rearrange("j (t m) -> j t m", t=4),
@@ -181,24 +188,21 @@ def tile_list_grasp_view_value_kernel(tc, tab_words, tab_scales, offs, tab2_word
                         project_b(a, g)
                     magnitude(g)
 
-        for g in range(TILES_SQUARED_ON_VECTOR):
-            nc.vector.tensor_tensor(of_tile(damp, g), of_tile(root, g), of_tile(root, g), ALU.mult)
-        for g in range(TILES_SQUARED_ON_VECTOR, VIEW_TILES):
-            nc.scalar.activation(of_tile(damp, g), of_tile(root, g), ACT.Square)
 
         a_ps = {}
 
         def project_a(a, g):
-            if a == 0:
+            order = (0, 1, 2) if g < VIEW_TILES // 2 else (2, 0, 1)
+            if a == order[0]:
                 a_ps[g] = bank(partner(g), "a_ps%d" % g)
             for t in range(4):
                 cols = slice(P * t, P * (t + 1))
                 nc.tensor.matmul_mx(out=a_ps[g][:, cols], lhsT=wa_w[a][:, cols].bitcast(FP8X4),
                                     lhsT_scale=wa_s[a][:, cols], rhs=v_w[a, g], rhs_scale=v_s(a, g),
-                                    start=(a == 0 and t == 0), stop=(a == PASSES - 1 and t == 3))
+                                    start=(a == order[0] and t == 0), stop=(a == order[-1] and t == 3))
 
         def quantise_wa(a):
-            wa_bf = sb("wa_bf%d" % a, [P, 4 * H], BF16)
+            wa_bf = sb("wa_bf%d" % a, [P, 4 * H], BF16, 12 * KIB if a == PASSES - 1 else None)
             dealt = wa_bf[:].rearrange("p (u v m j) -> p u m j v", u=2, v=2, j=4)
             rows = wa_raw[a][:].rearrange("p j (m u v) -> p u m j v", u=2, v=2)
             for u in range(2):
@@ -212,6 +216,10 @@ def tile_list_grasp_view_value_kernel(tc, tab_words, tab_scales, offs, tab2_word
             quantise_wa(a)
             for g in range(VIEW_TILES // 2):
                 project_a(a, g)
+        for g in range(TILES_SQUARED_ON_GPSIMD):
+            nc.gpsimd.tensor_tensor(of_tile(damp, g), of_tile(root, g), of_tile(root, g), ALU.mult)
+        for g in range(TILES_SQUARED_ON_GPSIMD, VIEW_TILES):
+            nc.scalar.activation(of_tile(damp, g), of_tile(root, g), ACT.Square)
         nc.vector.tensor_copy(v2_s[:], tab2_s[:].indirect(offs2_sb[:]))
         nc.vector.tensor_copy(v2_w[:], tab2_w[:].bitcast(U32).indirect(offs2_sb[:]))
 
@@ -220,7 +228,7 @@ def tile_list_grasp_view_value_kernel(tc, tab_words, tab_scales, offs, tab2_word
         for tiles in CHUNK_TILES:
             width = P * tiles
             while ahead < min(first + tiles + 4, VIEW_TILES):
-                for a in range(PASSES):
+                for a in (2, 0, 1):
                     project_a(a, ahead)
                 ahead += 1
             h_bf = sb("h_bf%d" % first, [P, tiles, H], BF16)

@@ -1,7 +1,6 @@
 from contextlib import ExitStack
 
 import concourse.mybir as mybir
-from concourse.masks import make_identity
 
 K, H, T, S, T2, S2 = 1536, 512, 2048, 1024, 1024, 512
 FLOPS = 2 * K * H * S * 2 + 2 * H * S2 * S
@@ -22,8 +21,8 @@ PASSES = K // 512
 VIEW_TILES = S // P
 HALF = S // 2
 CHUNK_TILES = (2, 4, 2)
-PAIRS = VIEW_TILES // 2
-TILES_SQUARED_ON_GPSIMD = 3
+TILES_SQUARED_ON_GPSIMD = (0, 1, 2, 5, 7)
+TILES_SQUARED_ON_SCALAR = (3, 4, 6)
 KIB = 1024
 
 
@@ -43,16 +42,15 @@ def tile_list_grasp_view_value_kernel(tc, tab_words, tab_scales, offs, tab2_word
         def bank(index, name):
             return psum.tile([P, 512], F32, name=name, tag="bank%d" % index)
 
-        def partner(g):
-            return g + 1 - 2 * (g % 2)
-
         offs_sb = keep.tile([P, S // 16], U16, name="offs_sb")
         offs2_sb = keep.tile([P, S2 // 16], U16, name="offs2_sb")
-        tab_s = sb("tab_s", [P, T], U8)
+        tab_s = sb("tab_s", [P, T], U8, 8 * KIB)
         tab_w = [sb("tab_w%d" % a, [P, T], I32, (None, None, 0)[a]) for a in range(PASSES)]
         tab2_w = sb("tab2_w", [P, T2], I32)
         tab2_s = sb("tab2_s", [P, T2], U8)
-        wb_w = sb("wb_w", [P, PASSES, 2 * H], U8)
+        wb_w_first = sb("wb_w_first", [P, PASSES - 1, 2 * H], U8)
+        wb_w_last = sb("wb_w_last", [P, 2 * H], U8)
+        wb_w = [wb_w_first[:, 0, :], wb_w_first[:, 1, :], wb_w_last[:]]
         wb_s = sb("wb_s", [P, PASSES, H], U8)
         wa_raw = [sb("wa_raw%d" % a, [P, 4, H], F32) for a in range(PASSES)]
         wa_w = [sb("wa_w%d" % a, [P, H], U32) for a in range(PASSES)]
@@ -62,13 +60,15 @@ def tile_list_grasp_view_value_kernel(tc, tab_words, tab_scales, offs, tab2_word
         v2_w = sb("v2_w", [P, S2], U32)
         v2_s = sb("v2_s", [P, S2], U8)
         bias = sb("bias", [P, S2 // P], F32)
-        ident = sb("ident", [P, P], F32)
+        one = sb("one", [P, 1], F32)
+        wb_w_dealt = [sb("wb_w_dealt%d" % a, [P, 2 * H], U8) for a in range(PASSES)]
+        wb_s_dealt = [sb("wb_s_dealt%d" % a, [P, H], U8) for a in range(PASSES)]
 
         nc.vector.memset(tab_s[:].bitcast(I32), 0)
         nc.gpsimd.memset(wb_s[:].rearrange("p a n -> p (a n)").bitcast(I32), 0)
         for plane in v_s_shifted:
             nc.vector.memset(plane[96:128, :].bitcast(I32), 0)
-        make_identity(nc, ident[:])
+        nc.gpsimd.memset(one[:], 1.0)
         nc.gpsimd.memset(tab2_s[:].bitcast(I32), 0)
 
         def load_table(a):
@@ -83,30 +83,47 @@ def tile_list_grasp_view_value_kernel(tc, tab_words, tab_scales, offs, tab2_word
             queue = nc.scalar if q < 2 else nc.sync
             queue.dma_start(tab_s[32 * q : 32 * q + 4 * PASSES, :].bitcast(I32),
                                 tab_scales[:, 4 * q : 4 * q + 4, :].bitcast(I32))
-        nc.sync.dma_start(wb_w[:].bitcast(I32), wb_words.rearrange("a p n -> p a n").bitcast(I32))
+        nc.sync.dma_start(wb_w_first[:].bitcast(I32), wb_words[0:2].rearrange("a p n -> p a n").bitcast(I32))
         load_table(1)
         for q in range(4):
             nc.sync.dma_start(wb_s[32 * q : 32 * q + 4, :, :].bitcast(I32),
                               wb_scales[:, 4 * q : 4 * q + 4, :].rearrange("a r n -> r a n").bitcast(I32))
+        nc.sync.dma_start(wb_w_last[:].bitcast(I32), wb_words[2].bitcast(I32))
         load_table(2)
 
         warm = sb("warm", [P, 1], F32)
-        nc.scalar.activation(warm[:], ident[:, 0:1], ACT.Abs_reciprocal_sqrt, bias=1.0)
+        nc.scalar.activation(warm[:], one[:], ACT.Abs_reciprocal_sqrt, bias=1.0)
+
+        def deal_wb_words(a):
+            nc.gpsimd.tensor_copy(wb_w_dealt[a][:].rearrange("p (t m e) -> p t e m", t=4, e=2),
+                                  wb_w[a].rearrange("p (m t e) -> p t e m", t=4, e=2))
+
+        def deal_wb_scales(a):
+            nc.gpsimd.tensor_copy(wb_s_dealt[a][:].rearrange("p (t m) -> p t m", t=4),
+                                  wb_s[:, a, :].rearrange("p (m t) -> p t m", t=4))
+
+        deal_wb_words(0)
+        deal_wb_words(1)
+        deal_wb_scales(0)
+        deal_wb_scales(1)
+        deal_wb_words(2)
+        deal_wb_scales(2)
 
         v_w = {}
+        v_w_half = {}
 
         def gather_words(a, j0, j1, offset=None):
             words = sb("v_w%d_%d" % (a, j0), [P, j1 - j0], U32, offset)
             nc.vector.tensor_copy(words[:], tab_w[a][:].bitcast(U32).indirect(offs_sb[:, j0 // 16 : j1 // 16]))
+            v_w_half[a, j0 // HALF] = words[:].bitcast(FP8X4)
             for g in range(j0 // P, j1 // P):
                 v_w[a, g] = words[:, P * g - j0 : P * (g + 1) - j0].bitcast(FP8X4)
 
-        def v_s(a, g):
+        def v_s(a, j0, width):
             plane = v_s_packed if a == 0 else v_s_shifted[a - 1]
-            return plane[:, P * g : P * (g + 1)]
+            return plane[:, j0 : j0 + width]
 
         gather_words(0, 0, HALF)
-        gather_words(0, HALF, S)
         for j0 in (0, HALF):
             nc.vector.tensor_copy(v_s_packed[:, j0 : j0 + HALF],
                                   tab_s[:].indirect(offs_sb[:, j0 // 16 : (j0 + HALF) // 16]))
@@ -116,7 +133,7 @@ def tile_list_grasp_view_value_kernel(tc, tab_words, tab_scales, offs, tab2_word
                             v_s_packed[4 * a : 4 * a + 112, j0 : j0 + HALF].bitcast(I32))
 
         shift_scales(nc.sync, 1, 0)
-        shift_scales(nc.scalar, 2, 0)
+        shift_scales(nc.sync, 2, 0)
         load_wa(0)
         shift_scales(nc.sync, 2, HALF)
         shift_scales(nc.sync, 1, HALF)
@@ -131,74 +148,57 @@ def tile_list_grasp_view_value_kernel(tc, tab_words, tab_scales, offs, tab2_word
             nc.sync.dma_start(bias[:], c.rearrange("(n p) -> p n", p=P))
 
         gather_words(1, 0, HALF)
-        gather_words(2, 0, 2 * P)
-        gather_words(2, 2 * P, HALF)
+        gather_words(0, HALF, S, 8 * KIB)
+        gather_words(2, 0, HALF)
         gather_words(2, HALF, S)
         gather_words(1, HALF, S, 0)
 
         b_ps = {}
 
-        def project_b(a, g):
-            order = (0, 1, 2) if g < VIEW_TILES // 2 else (0, 2, 1)
+        def project_b(a, half, t):
+            order = (0, 1, 2) if half == 0 else (0, 2, 1)
             if a == order[0]:
-                b_ps[g] = bank(g, "b_ps%d" % g)
-            nc.tensor.matmul_mx(out=b_ps[g][:], lhsT=v_w[a, g], lhsT_scale=v_s(a, g),
-                                rhs=wb_w[:, a, :].bitcast(FP4X4), rhs_scale=wb_s[:, a, :],
+                b_ps[half, t] = bank(4 * half + t, "b_ps%d_%d" % (half, t))
+            nc.tensor.matmul_mx(out=b_ps[half, t][:],
+                                lhsT=wb_w_dealt[a][:, 2 * P * t : 2 * P * (t + 1)].bitcast(FP4X4),
+                                lhsT_scale=wb_s_dealt[a][:, P * t : P * (t + 1)],
+                                rhs=v_w_half[a, half], rhs_scale=v_s(a, HALF * half, HALF),
                                 start=(a == order[0]), stop=(a == order[-1]))
 
-        def woven(ap):
-            return ap.rearrange("p (t j) -> p j t", t=4)
+        root = [sb("root%d" % half, [P, 2, 2 * HALF], F32) for half in range(2)]
+        damp = {}
+        for name, tiles, offset in (("damp_g", TILES_SQUARED_ON_GPSIMD, 10 * KIB), ("damp_s", TILES_SQUARED_ON_SCALAR, None)):
+            squares = sb(name, [P, len(tiles) * H], F32, offset)
+            for n, g in enumerate(tiles):
+                damp[g] = squares[:, H * n : H * (n + 1)].rearrange("p (u x) -> p u x", u=2)
 
-        def plain(ap):
-            return ap.rearrange("p (j t) -> p j t", t=4)
+        def inverse_roots(half, u):
+            mag = sb("mag%d_%d" % (half, u), [P, 2, HALF], F32)
+            for v in range(2):
+                nc.scalar.activation(mag[:, v, :], b_ps[half, 2 * u + v][:], ACT.Abs)
+            nc.scalar.activation(root[half][:, u, :].rearrange("p (j v) -> p j v", v=2),
+                                 mag[:].rearrange("p v j -> p j v"), ACT.Abs_reciprocal_sqrt, bias=1.0)
 
-        mag = [sb("mag%d" % g, [P, H], F32) for g in range(VIEW_TILES)]
-        root = [sb("root%d" % n, [P, 2 * H], F32) for n in range(PAIRS)]
-        damp = [sb("damp%d" % n, [P, 2 * H], F32, (10 * KIB, 14 * KIB, None, None)[n]) for n in range(PAIRS)]
+        def roots_of_tile(g):
+            return root[g // 4][:, :, 2 * P * (g % 4) : 2 * P * (g % 4 + 1)]
 
-        def magnitude(g):
-            nc.scalar.activation(mag[g][:].rearrange("j (t m) -> j t m", t=4),
-                                 b_ps[g][:].rearrange("j (m t) -> j t m", t=4), ACT.Abs)
-
-        def of_tile(pair_tiles, g):
-            return pair_tiles[g // 2][:, H * (g % 2) : H * (g % 2 + 1)]
-
-        def inverse_roots(n):
-            turned = {}
-            for g in (2 * n, 2 * n + 1):
-                turned[g] = bank(partner(g), "turned%d" % g)
-                for t in range(4):
-                    cols = slice(P * t, P * (t + 1))
-                    nc.tensor.transpose(turned[g][:, cols], mag[g][:, cols], ident[:])
-            for g in (2 * n, 2 * n + 1):
-                nc.scalar.activation(plain(of_tile(root, g)), woven(turned[g][:]),
-                                     ACT.Abs_reciprocal_sqrt, bias=1.0)
-
-        for g in range(VIEW_TILES):
-            project_b(0, g)
-        for g in range(VIEW_TILES // 2):
-            project_b(1, g)
-            project_b(2, g)
-            magnitude(g)
-        for n in range(PAIRS):
-            inverse_roots(n)
-            if n < PAIRS // 2:
-                for g in (VIEW_TILES // 2 + 2 * n, VIEW_TILES // 2 + 2 * n + 1):
-                    for a in (2, 1):
-                        project_b(a, g)
-                    magnitude(g)
-
+        for half in range(2):
+            for u in range(2):
+                for a in ((0, 1, 2), (0, 2, 1))[half]:
+                    for v in range(2):
+                        project_b(a, half, 2 * u + v)
+                inverse_roots(half, u)
 
         a_ps = {}
 
         def project_a(a, g):
-            order = (0, 1, 2) if g < VIEW_TILES // 2 else (2, 0, 1)
+            order = ((0, 1, 2), (0, 1, 2), (1, 0, 2), (2, 0, 1))[g // 2]
             if a == order[0]:
-                a_ps[g] = bank(partner(g), "a_ps%d" % g)
+                a_ps[g] = bank(g, "a_ps%d" % g)
             for t in range(4):
                 cols = slice(P * t, P * (t + 1))
                 nc.tensor.matmul_mx(out=a_ps[g][:, cols], lhsT=wa_w[a][:, cols].bitcast(FP8X4),
-                                    lhsT_scale=wa_s[a][:, cols], rhs=v_w[a, g], rhs_scale=v_s(a, g),
+                                    lhsT_scale=wa_s[a][:, cols], rhs=v_w[a, g], rhs_scale=v_s(a, P * g, P),
                                     start=(a == order[0] and t == 0), stop=(a == order[-1] and t == 3))
 
         def quantise_wa(a):
@@ -214,32 +214,35 @@ def tile_list_grasp_view_value_kernel(tc, tab_words, tab_scales, offs, tab2_word
 
         for a in range(PASSES):
             quantise_wa(a)
-            for g in range(VIEW_TILES // 2):
+            for g in range(4):
                 project_a(a, g)
-        for g in range(TILES_SQUARED_ON_GPSIMD):
-            nc.gpsimd.tensor_tensor(of_tile(damp, g), of_tile(root, g), of_tile(root, g), ALU.mult)
-        for g in range(TILES_SQUARED_ON_GPSIMD, VIEW_TILES):
-            nc.scalar.activation(of_tile(damp, g), of_tile(root, g), ACT.Square)
+            for g in (4, 5):
+                for late in ((), (1, 0), (2,))[a]:
+                    project_a(late, g)
+        for g in (6, 7):
+            for a in (2, 0, 1):
+                project_a(a, g)
+        for g in TILES_SQUARED_ON_GPSIMD:
+            nc.gpsimd.tensor_tensor(damp[g], roots_of_tile(g), roots_of_tile(g), ALU.mult)
+        for g in TILES_SQUARED_ON_SCALAR:
+            nc.scalar.activation(damp[g], roots_of_tile(g), ACT.Square)
         nc.vector.tensor_copy(v2_s[:], tab2_s[:].indirect(offs2_sb[:]))
         nc.vector.tensor_copy(v2_w[:], tab2_w[:].bitcast(U32).indirect(offs2_sb[:]))
 
         first = 0
-        ahead = VIEW_TILES // 2
         for tiles in CHUNK_TILES:
             width = P * tiles
-            while ahead < min(first + tiles + 4, VIEW_TILES):
-                for a in (2, 0, 1):
-                    project_a(a, ahead)
-                ahead += 1
             h_bf = sb("h_bf%d" % first, [P, tiles, H], BF16)
             for n in range(tiles):
                 g = first + n
-                nc.vector.tensor_tensor(plain(h_bf[:, n, :]), woven(a_ps[g][:]), plain(of_tile(damp, g)), ALU.mult)
+                nc.vector.tensor_tensor(h_bf[:, n, :].rearrange("p (j u v) -> p j u v", u=2, v=2),
+                                        a_ps[g][:].rearrange("p (u v j) -> p j u v", u=2, v=2),
+                                        damp[g].rearrange("p u (j v) -> p j u v", v=2), ALU.mult)
             h_w = sb("h_w%d" % first, [P, width], U32)
             h_s = sb("h_s%d" % first, [P, width], U8)
             nc.vector.quantize_mx(out=h_w[:].bitcast(FP8X4), scales=h_s[:],
                                   in_=h_bf[:].rearrange("p g r -> p (g r)"))
-            y_ps = [bank(partner(g), "y_ps%d" % g) for g in range(first, first + tiles)]
+            y_ps = [bank(g, "y_ps%d" % g) for g in range(first, first + tiles)]
             for i in range(S2 // P):
                 rows = slice(P * i, P * (i + 1))
                 place = (i * width) % 512

@@ -20,9 +20,11 @@ P = 128
 PASSES = K // 512
 VIEW_TILES = S // P
 HALF = S // 2
-CHUNK_TILES = (2, 4, 2)
-TILES_SQUARED_ON_GPSIMD = (0, 1, 2, 5, 7)
-TILES_SQUARED_ON_SCALAR = (3, 4, 6)
+CHUNK_TILES = (4, 2, 2)
+TILES_SQUARED_ON_GPSIMD = (0, 1, 3)
+TILES_SQUARED_ON_SCALAR = (2, 4, 5, 6)
+LAST_TILE = VIEW_TILES - 1
+B_PASS_ORDER = (((0, 1, 2), (2, 0, 1)), ((0, 2, 1), (2, 0, 1)))
 KIB = 1024
 
 
@@ -49,8 +51,7 @@ def tile_list_grasp_view_value_kernel(tc, tab_words, tab_scales, offs, tab2_word
         tab2_w = sb("tab2_w", [P, T2], I32)
         tab2_s = sb("tab2_s", [P, T2], U8)
         wb_w_first = sb("wb_w_first", [P, PASSES - 1, 2 * H], U8)
-        wb_w_last = sb("wb_w_last", [P, 2 * H], U8)
-        wb_w = [wb_w_first[:, 0, :], wb_w_first[:, 1, :], wb_w_last[:]]
+        wb_w_last = sb("wb_w_last", [P, 2 * H], U8, 20 * KIB)
         wb_s = sb("wb_s", [P, PASSES, H], U8)
         wa_raw = [sb("wa_raw%d" % a, [P, 4, H], F32) for a in range(PASSES)]
         wa_w = [sb("wa_w%d" % a, [P, H], U32) for a in range(PASSES)]
@@ -61,8 +62,9 @@ def tile_list_grasp_view_value_kernel(tc, tab_words, tab_scales, offs, tab2_word
         v2_s = sb("v2_s", [P, S2], U8)
         bias = sb("bias", [P, S2 // P], F32)
         one = sb("one", [P, 1], F32)
-        wb_w_dealt = [sb("wb_w_dealt%d" % a, [P, 2 * H], U8) for a in range(PASSES)]
-        wb_s_dealt = [sb("wb_s_dealt%d" % a, [P, H], U8) for a in range(PASSES)]
+        wb_w_first_dealt = [sb("wb_w_first_dealt%d" % u, [P, PASSES - 1, H], U8, (None, 20 * KIB)[u]) for u in range(2)]
+        wb_w_last_dealt = sb("wb_w_last_dealt", [P, 2 * H], U8)
+        wb_s_dealt = [sb("wb_s_dealt%d" % u, [P, PASSES, 2 * P], U8) for u in range(2)]
 
         nc.vector.memset(tab_s[:].bitcast(I32), 0)
         nc.gpsimd.memset(wb_s[:].rearrange("p a n -> p (a n)").bitcast(I32), 0)
@@ -94,20 +96,25 @@ def tile_list_grasp_view_value_kernel(tc, tab_words, tab_scales, offs, tab2_word
         warm = sb("warm", [P, 1], F32)
         nc.scalar.activation(warm[:], one[:], ACT.Abs_reciprocal_sqrt, bias=1.0)
 
-        def deal_wb_words(a):
-            nc.gpsimd.tensor_copy(wb_w_dealt[a][:].rearrange("p (t m e) -> p t e m", t=4, e=2),
-                                  wb_w[a].rearrange("p (m t e) -> p t e m", t=4, e=2))
+        def deal_first_words(u):
+            nc.gpsimd.tensor_copy(wb_w_first_dealt[u][:].rearrange("p a (v m e) -> p a v e m", v=2, e=2),
+                                  wb_w_first[:].rearrange("p a (m u v e) -> p u a v e m", u=2, v=2, e=2)[:, u])
 
-        def deal_wb_scales(a):
-            nc.gpsimd.tensor_copy(wb_s_dealt[a][:].rearrange("p (t m) -> p t m", t=4),
-                                  wb_s[:, a, :].rearrange("p (m t) -> p t m", t=4))
+        def deal_scales(u):
+            nc.gpsimd.tensor_copy(wb_s_dealt[u][:].rearrange("p a (v m) -> p a v m", v=2),
+                                  wb_s[:].rearrange("p a (m u v) -> p u a v m", u=2, v=2)[:, u])
 
-        deal_wb_words(0)
-        deal_wb_words(1)
-        deal_wb_scales(0)
-        deal_wb_scales(1)
-        deal_wb_words(2)
-        deal_wb_scales(2)
+        deal_first_words(0)
+        deal_scales(0)
+        nc.gpsimd.tensor_copy(wb_w_last_dealt[:].rearrange("p (t m e) -> p t e m", t=4, e=2),
+                              wb_w_last[:].rearrange("p (m t e) -> p t e m", t=4, e=2))
+        deal_first_words(1)
+        deal_scales(1)
+
+        def wb_codes(a, t):
+            if a == PASSES - 1:
+                return wb_w_last_dealt[:, 2 * P * t : 2 * P * (t + 1)].bitcast(FP4X4)
+            return wb_w_first_dealt[t // 2][:, a, 2 * P * (t % 2) : 2 * P * (t % 2 + 1)].bitcast(FP4X4)
 
         v_w = {}
         v_w_half = {}
@@ -147,8 +154,8 @@ def tile_list_grasp_view_value_kernel(tc, tab_words, tab_scales, offs, tab2_word
         with nc.allow_non_contiguous_dma(reason="one bias value a partition"):
             nc.sync.dma_start(bias[:], c.rearrange("(n p) -> p n", p=P))
 
-        gather_words(1, 0, HALF)
         gather_words(0, HALF, S, 8 * KIB)
+        gather_words(1, 0, HALF)
         gather_words(2, 0, HALF)
         gather_words(2, HALF, S)
         gather_words(1, HALF, S, 0)
@@ -156,12 +163,12 @@ def tile_list_grasp_view_value_kernel(tc, tab_words, tab_scales, offs, tab2_word
         b_ps = {}
 
         def project_b(a, half, t):
-            order = (0, 1, 2) if half == 0 else (0, 2, 1)
+            order = B_PASS_ORDER[half][t // 2]
             if a == order[0]:
                 b_ps[half, t] = bank(4 * half + t, "b_ps%d_%d" % (half, t))
             nc.tensor.matmul_mx(out=b_ps[half, t][:],
-                                lhsT=wb_w_dealt[a][:, 2 * P * t : 2 * P * (t + 1)].bitcast(FP4X4),
-                                lhsT_scale=wb_s_dealt[a][:, P * t : P * (t + 1)],
+                                lhsT=wb_codes(a, t),
+                                lhsT_scale=wb_s_dealt[t // 2][:, a, P * (t % 2) : P * (t % 2 + 1)],
                                 rhs=v_w_half[a, half], rhs_scale=v_s(a, HALF * half, HALF),
                                 start=(a == order[0]), stop=(a == order[-1]))
 
@@ -184,7 +191,7 @@ def tile_list_grasp_view_value_kernel(tc, tab_words, tab_scales, offs, tab2_word
 
         for half in range(2):
             for u in range(2):
-                for a in ((0, 1, 2), (0, 2, 1))[half]:
+                for a in B_PASS_ORDER[half][u]:
                     for v in range(2):
                         project_b(a, half, 2 * u + v)
                 inverse_roots(half, u)
@@ -192,7 +199,7 @@ def tile_list_grasp_view_value_kernel(tc, tab_words, tab_scales, offs, tab2_word
         a_ps = {}
 
         def project_a(a, g):
-            order = ((0, 1, 2), (0, 1, 2), (1, 0, 2), (2, 0, 1))[g // 2]
+            order = (0, 1, 2) if g < VIEW_TILES // 2 else (2, 0, 1)
             if a == order[0]:
                 a_ps[g] = bank(g, "a_ps%d" % g)
             for t in range(4):
@@ -216,10 +223,7 @@ def tile_list_grasp_view_value_kernel(tc, tab_words, tab_scales, offs, tab2_word
             quantise_wa(a)
             for g in range(4):
                 project_a(a, g)
-            for g in (4, 5):
-                for late in ((), (1, 0), (2,))[a]:
-                    project_a(late, g)
-        for g in (6, 7):
+        for g in range(4, VIEW_TILES):
             for a in (2, 0, 1):
                 project_a(a, g)
         for g in TILES_SQUARED_ON_GPSIMD:
@@ -232,7 +236,7 @@ def tile_list_grasp_view_value_kernel(tc, tab_words, tab_scales, offs, tab2_word
         first = 0
         for tiles in CHUNK_TILES:
             width = P * tiles
-            h_bf = sb("h_bf%d" % first, [P, tiles, H], BF16)
+            h_bf = sb("h_bf%d" % first, [P, tiles, H], BF16, 22 * KIB if first == 0 else None)
             for n in range(tiles):
                 g = first + n
                 nc.vector.tensor_tensor(h_bf[:, n, :].rearrange("p (j u v) -> p j u v", u=2, v=2),
@@ -242,6 +246,10 @@ def tile_list_grasp_view_value_kernel(tc, tab_words, tab_scales, offs, tab2_word
             h_s = sb("h_s%d" % first, [P, width], U8)
             nc.vector.quantize_mx(out=h_w[:].bitcast(FP8X4), scales=h_s[:],
                                   in_=h_bf[:].rearrange("p g r -> p (g r)"))
+            if first == 0:
+                last_damp = sb("last_damp", [P, 2, 2 * P], F32, 22 * KIB)
+                damp[LAST_TILE] = last_damp[:]
+                nc.gpsimd.tensor_tensor(damp[LAST_TILE], roots_of_tile(LAST_TILE), roots_of_tile(LAST_TILE), ALU.mult)
             y_ps = [bank(g, "y_ps%d" % g) for g in range(first, first + tiles)]
             for i in range(S2 // P):
                 rows = slice(P * i, P * (i + 1))

@@ -20,12 +20,14 @@ P = 128
 PASSES = K // 512
 VIEW_TILES = S // P
 HALF = S // 2
-CHUNK_TILES = (4, 2, 2)
-TILES_SQUARED_ON_GPSIMD = (0, 1, 3)
-TILES_SQUARED_ON_SCALAR = (2, 4, 5, 6)
-LAST_TILE = VIEW_TILES - 1
-B_PASS_ORDER = (((0, 1, 2), (2, 0, 1)), ((0, 2, 1), (2, 0, 1)))
+CHUNK_TILES = (2, 2, 2, 1, 1)
+PARKED_ROWS = (8, 16, 72, 80)
+QUARTER = S // 4
+B_PASS_ORDER = ((0, 1, 2), (0, 1, 2), (0, 2, 1), (2, 0, 1))
+A_PASS_ORDER = ((0, 1, 2), (0, 1, 2), (0, 1, 2), (2, 0, 1))
 KIB = 1024
+GPSIMD_SQUARES = {0: 4 * KIB, 1: 8 * KIB, 4: 10 * KIB, 6: 12 * KIB, 7: 14 * KIB}
+SQUARED_BEHIND_CHUNK = {0: 6, 2: 7}
 
 
 def tile_list_grasp_view_value_kernel(tc, tab_words, tab_scales, offs, tab2_words, tab2_scales, offs2,
@@ -46,32 +48,30 @@ def tile_list_grasp_view_value_kernel(tc, tab_words, tab_scales, offs, tab2_word
 
         offs_sb = keep.tile([P, S // 16], U16, name="offs_sb")
         offs2_sb = keep.tile([P, S2 // 16], U16, name="offs2_sb")
-        tab_s = sb("tab_s", [P, T], U8, 8 * KIB)
-        tab_w = [sb("tab_w%d" % a, [P, T], I32, (None, None, 0)[a]) for a in range(PASSES)]
+        tab_s = sb("tab_s", [P, T], U8)
+        tab_w = [sb("tab_w%d" % a, [P, T], I32) for a in range(PASSES)]
         tab2_w = sb("tab2_w", [P, T2], I32)
         tab2_s = sb("tab2_s", [P, T2], U8)
-        wb_w_first = sb("wb_w_first", [P, PASSES - 1, 2 * H], U8)
-        wb_w_last = sb("wb_w_last", [P, 2 * H], U8, 20 * KIB)
+        wb_w = sb("wb_w", [P, PASSES, 2 * H], U8)
         wb_s = sb("wb_s", [P, PASSES, H], U8)
-        wa_raw = [sb("wa_raw%d" % a, [P, 4, H], F32) for a in range(PASSES)]
+        wa_raw = [sb("wa_raw%d" % a, [P, 4, H], F32, (None, None, 16 * KIB)[a]) for a in range(PASSES)]
         wa_w = [sb("wa_w%d" % a, [P, H], U32) for a in range(PASSES)]
         wa_s = [sb("wa_s%d" % a, [P, H], U8) for a in range(PASSES)]
-        v_s_packed = sb("v_s_packed", [P, S], U8)
-        v_s_shifted = [sb("v_s_shifted%d" % a, [P, S], U8) for a in range(1, PASSES)]
+        v_s_gathered = sb("v_s_gathered", [P, S], U8)
+        v_s_moved = sb("v_s_moved", [P, PASSES - 1, S], U8)
         v2_w = sb("v2_w", [P, S2], U32)
-        v2_s = sb("v2_s", [P, S2], U8)
+        v2_s = sb("v2_s", [P, S2], U8, 16 * KIB)
         bias = sb("bias", [P, S2 // P], F32)
         one = sb("one", [P, 1], F32)
-        wb_w_first_dealt = [sb("wb_w_first_dealt%d" % u, [P, PASSES - 1, H], U8, (None, 20 * KIB)[u]) for u in range(2)]
-        wb_w_last_dealt = sb("wb_w_last_dealt", [P, 2 * H], U8)
-        wb_s_dealt = [sb("wb_s_dealt%d" % u, [P, PASSES, 2 * P], U8) for u in range(2)]
+        wb_w_dealt = [sb("wb_w_dealt%d" % a, [P, H], U16) for a in range(PASSES)]
+        wb_s_dealt = [sb("wb_s_dealt%d" % a, [P, H], U8) for a in range(PASSES)]
 
-        nc.vector.memset(tab_s[:].bitcast(I32), 0)
+        nc.vector.memset(tab_s[:, : T // 2].bitcast(I32), 0)
+        nc.gpsimd.memset(tab_s[:, T // 2 :].bitcast(I32), 0)
         nc.gpsimd.memset(wb_s[:].rearrange("p a n -> p (a n)").bitcast(I32), 0)
-        for plane in v_s_shifted:
-            nc.vector.memset(plane[96:128, :].bitcast(I32), 0)
-        nc.gpsimd.memset(one[:], 1.0)
+        nc.gpsimd.memset(v_s_moved[:].rearrange("p a n -> p (a n)").bitcast(I32), 0)
         nc.gpsimd.memset(tab2_s[:].bitcast(I32), 0)
+        nc.gpsimd.memset(one[:], 1.0)
 
         def load_table(a):
             nc.sync.dma_start(tab_w[a][:], tab_words[a].rearrange("p n t -> p (n t)").bitcast(I32))
@@ -80,136 +80,110 @@ def tile_list_grasp_view_value_kernel(tc, tab_words, tab_scales, offs, tab2_word
             nc.sync.dma_start(wa_raw[a][:], wa[512 * a : 512 * (a + 1), :].rearrange("(p j) r -> p j r", j=4))
 
         nc.sync.dma_start(offs_sb[:], offs)
-        load_table(0)
         for q in range(4):
-            queue = nc.scalar if q < 2 else nc.sync
-            queue.dma_start(tab_s[32 * q : 32 * q + 4 * PASSES, :].bitcast(I32),
-                                tab_scales[:, 4 * q : 4 * q + 4, :].bitcast(I32))
-        nc.sync.dma_start(wb_w_first[:].bitcast(I32), wb_words[0:2].rearrange("a p n -> p a n").bitcast(I32))
-        load_table(1)
+            queue = nc.scalar if q < 3 else nc.sync
+            queue.dma_start(tab_s[32 * q : 32 * q + 4, :].bitcast(I32),
+                            tab_scales[0, 4 * q : 4 * q + 4, :].bitcast(I32))
+        for pair in range(2):
+            first_row = PARKED_ROWS[2 * pair]
+            nc.sync.dma_start(tab_s[first_row : first_row + 16, :].bitcast(I32),
+                              tab_scales[1:PASSES, 8 * pair : 8 * pair + 8, :].rearrange("a n t -> n a t").bitcast(I32))
+        load_table(0)
         for q in range(4):
             nc.sync.dma_start(wb_s[32 * q : 32 * q + 4, :, :].bitcast(I32),
                               wb_scales[:, 4 * q : 4 * q + 4, :].rearrange("a r n -> r a n").bitcast(I32))
-        nc.sync.dma_start(wb_w_last[:].bitcast(I32), wb_words[2].bitcast(I32))
+        nc.sync.dma_start(wb_w[:].bitcast(I32), wb_words.rearrange("a p n -> p a n").bitcast(I32))
+        load_table(1)
+
+        nc.vector.tensor_copy(v_s_gathered[:], tab_s[:].indirect(offs_sb[:]))
+        for q in range(4):
+            nc.sync.dma_start(v_s_moved[32 * q : 32 * q + 4, :, :].bitcast(I32),
+                              v_s_gathered[PARKED_ROWS[q] : PARKED_ROWS[q] + 8, :].bitcast(I32))
         load_table(2)
-
-        warm = sb("warm", [P, 1], F32)
-        nc.scalar.activation(warm[:], one[:], ACT.Abs_reciprocal_sqrt, bias=1.0)
-
-        def deal_first_words(u):
-            nc.gpsimd.tensor_copy(wb_w_first_dealt[u][:].rearrange("p a (v m e) -> p a v e m", v=2, e=2),
-                                  wb_w_first[:].rearrange("p a (m u v e) -> p u a v e m", u=2, v=2, e=2)[:, u])
-
-        def deal_scales(u):
-            nc.gpsimd.tensor_copy(wb_s_dealt[u][:].rearrange("p a (v m) -> p a v m", v=2),
-                                  wb_s[:].rearrange("p a (m u v) -> p u a v m", u=2, v=2)[:, u])
-
-        deal_first_words(0)
-        deal_scales(0)
-        nc.gpsimd.tensor_copy(wb_w_last_dealt[:].rearrange("p (t m e) -> p t e m", t=4, e=2),
-                              wb_w_last[:].rearrange("p (m t e) -> p t e m", t=4, e=2))
-        deal_first_words(1)
-        deal_scales(1)
-
-        def wb_codes(a, t):
-            if a == PASSES - 1:
-                return wb_w_last_dealt[:, 2 * P * t : 2 * P * (t + 1)].bitcast(FP4X4)
-            return wb_w_first_dealt[t // 2][:, a, 2 * P * (t % 2) : 2 * P * (t % 2 + 1)].bitcast(FP4X4)
-
-        v_w = {}
-        v_w_half = {}
-
-        def gather_words(a, j0, j1, offset=None):
-            words = sb("v_w%d_%d" % (a, j0), [P, j1 - j0], U32, offset)
-            nc.vector.tensor_copy(words[:], tab_w[a][:].bitcast(U32).indirect(offs_sb[:, j0 // 16 : j1 // 16]))
-            v_w_half[a, j0 // HALF] = words[:].bitcast(FP8X4)
-            for g in range(j0 // P, j1 // P):
-                v_w[a, g] = words[:, P * g - j0 : P * (g + 1) - j0].bitcast(FP8X4)
-
-        def v_s(a, j0, width):
-            plane = v_s_packed if a == 0 else v_s_shifted[a - 1]
-            return plane[:, j0 : j0 + width]
-
-        gather_words(0, 0, HALF)
-        for j0 in (0, HALF):
-            nc.vector.tensor_copy(v_s_packed[:, j0 : j0 + HALF],
-                                  tab_s[:].indirect(offs_sb[:, j0 // 16 : (j0 + HALF) // 16]))
-
-        def shift_scales(queue, a, j0):
-            queue.dma_start(v_s_shifted[a - 1][0:112, j0 : j0 + HALF].bitcast(I32),
-                            v_s_packed[4 * a : 4 * a + 112, j0 : j0 + HALF].bitcast(I32))
-
-        shift_scales(nc.sync, 1, 0)
-        shift_scales(nc.sync, 2, 0)
         load_wa(0)
-        shift_scales(nc.sync, 2, HALF)
-        shift_scales(nc.sync, 1, HALF)
         load_wa(1)
+        nc.sync.dma_start(offs2_sb[:], offs2)
+        nc.sync.dma_start(tab2_w[:], tab2_words[0].rearrange("p n t -> p (n t)").bitcast(I32))
         for q in range(4):
             nc.sync.dma_start(tab2_s[32 * q : 32 * q + 4, :].bitcast(I32),
                               tab2_scales[0, 4 * q : 4 * q + 4, :].bitcast(I32))
         load_wa(2)
-        nc.sync.dma_start(offs2_sb[:], offs2)
-        nc.sync.dma_start(tab2_w[:], tab2_words[0].rearrange("p n t -> p (n t)").bitcast(I32))
         with nc.allow_non_contiguous_dma(reason="one bias value a partition"):
             nc.sync.dma_start(bias[:], c.rearrange("(n p) -> p n", p=P))
 
-        gather_words(0, HALF, S, 8 * KIB)
-        gather_words(1, 0, HALF)
-        gather_words(2, 0, HALF)
-        gather_words(2, HALF, S)
-        gather_words(1, HALF, S, 0)
+        warm = sb("warm", [P, 1], F32)
+        nc.scalar.activation(warm[:], one[:], ACT.Abs_reciprocal_sqrt, bias=1.0)
+
+        for a in range(PASSES):
+            nc.gpsimd.tensor_copy(wb_s_dealt[a][:].rearrange("p (t m) -> p t m", t=4),
+                                  wb_s[:, a, :].rearrange("p (m t) -> p t m", t=4))
+            nc.scalar.copy(wb_w_dealt[a][:].rearrange("p (t m) -> p t m", t=4),
+                           wb_w[:, a, :].bitcast(U16).rearrange("p (m t) -> p t m", t=4))
+
+        v_w = {}
+
+        def gather_words(a, j0, width):
+            words = sb("v_w%d_%d" % (a, j0), [P, width], U32)
+            nc.vector.tensor_copy(words[:], tab_w[a][:].bitcast(U32).indirect(offs_sb[:, j0 // 16 : (j0 + width) // 16]))
+            for k in range(j0 // QUARTER, (j0 + width) // QUARTER):
+                v_w[a, k] = words[:, QUARTER * k - j0 : QUARTER * (k + 1) - j0]
+
+        def v_s(a, j0, width):
+            if a == 0:
+                return v_s_gathered[:, j0 : j0 + width]
+            return v_s_moved[:, a - 1, j0 : j0 + width]
+
+        for a in range(PASSES - 1):
+            for j0 in (0, HALF):
+                gather_words(a, j0, HALF)
+        for j0 in range(0, S, QUARTER):
+            gather_words(PASSES - 1, j0, QUARTER)
 
         b_ps = {}
 
-        def project_b(a, half, t):
-            order = B_PASS_ORDER[half][t // 2]
+        def project_b(a, k, u):
+            order = B_PASS_ORDER[k]
             if a == order[0]:
-                b_ps[half, t] = bank(4 * half + t, "b_ps%d_%d" % (half, t))
-            nc.tensor.matmul_mx(out=b_ps[half, t][:],
-                                lhsT=wb_codes(a, t),
-                                lhsT_scale=wb_s_dealt[t // 2][:, a, P * (t % 2) : P * (t % 2 + 1)],
-                                rhs=v_w_half[a, half], rhs_scale=v_s(a, HALF * half, HALF),
-                                start=(a == order[0]), stop=(a == order[-1]))
-
-        root = [sb("root%d" % half, [P, 2, 2 * HALF], F32) for half in range(2)]
-        damp = {}
-        for name, tiles, offset in (("damp_g", TILES_SQUARED_ON_GPSIMD, 10 * KIB), ("damp_s", TILES_SQUARED_ON_SCALAR, None)):
-            squares = sb(name, [P, len(tiles) * H], F32, offset)
-            for n, g in enumerate(tiles):
-                damp[g] = squares[:, H * n : H * (n + 1)].rearrange("p (u x) -> p u x", u=2)
-
-        def inverse_roots(half, u):
-            mag = sb("mag%d_%d" % (half, u), [P, 2, HALF], F32)
+                b_ps[k, u] = bank(2 * k + u, "b_ps%d_%d" % (k, u))
             for v in range(2):
-                nc.scalar.activation(mag[:, v, :], b_ps[half, 2 * u + v][:], ACT.Abs)
-            nc.scalar.activation(root[half][:, u, :].rearrange("p (j v) -> p j v", v=2),
-                                 mag[:].rearrange("p v j -> p j v"), ACT.Abs_reciprocal_sqrt, bias=1.0)
+                cols = slice(P * (2 * u + v), P * (2 * u + v + 1))
+                nc.tensor.matmul_mx(out=b_ps[k, u][:, QUARTER * v : QUARTER * (v + 1)],
+                                    lhsT=wb_w_dealt[a][:, cols].bitcast(U8).bitcast(FP4X4),
+                                    lhsT_scale=wb_s_dealt[a][:, cols],
+                                    rhs=v_w[a, k].bitcast(FP8X4), rhs_scale=v_s(a, QUARTER * k, QUARTER),
+                                    start=(a == order[0] and v == 0), stop=(a == order[-1] and v == 1))
 
-        def roots_of_tile(g):
-            return root[g // 4][:, :, 2 * P * (g % 4) : 2 * P * (g % 4 + 1)]
+        root = [sb("root%d" % k, [P, 2, 2 * QUARTER], F32) for k in range(4)]
 
-        for half in range(2):
+        def inverse_roots(k):
+            mag = sb("mag%d" % k, [P, 2, 2 * QUARTER], F32)
             for u in range(2):
-                for a in B_PASS_ORDER[half][u]:
-                    for v in range(2):
-                        project_b(a, half, 2 * u + v)
-                inverse_roots(half, u)
+                nc.scalar.activation(mag[:, u, :].rearrange("p (j v) -> p j v", v=2),
+                                     b_ps[k, u][:].rearrange("p (v j) -> p j v", v=2), ACT.Abs)
+            nc.scalar.activation(root[k][:], mag[:], ACT.Abs_reciprocal_sqrt, bias=1.0)
+
+        for k in range(4):
+            for a in B_PASS_ORDER[k]:
+                for u in range(2):
+                    project_b(a, k, u)
+            inverse_roots(k)
 
         a_ps = {}
 
         def project_a(a, g):
-            order = (0, 1, 2) if g < VIEW_TILES // 2 else (2, 0, 1)
+            order = A_PASS_ORDER[g // 2]
             if a == order[0]:
                 a_ps[g] = bank(g, "a_ps%d" % g)
+            views = slice(P * (g % 2), P * (g % 2 + 1))
             for t in range(4):
                 cols = slice(P * t, P * (t + 1))
                 nc.tensor.matmul_mx(out=a_ps[g][:, cols], lhsT=wa_w[a][:, cols].bitcast(FP8X4),
-                                    lhsT_scale=wa_s[a][:, cols], rhs=v_w[a, g], rhs_scale=v_s(a, P * g, P),
+                                    lhsT_scale=wa_s[a][:, cols], rhs=v_w[a, g // 2][:, views].bitcast(FP8X4),
+                                    rhs_scale=v_s(a, P * g, P),
                                     start=(a == order[0] and t == 0), stop=(a == order[-1] and t == 3))
 
         def quantise_wa(a):
-            wa_bf = sb("wa_bf%d" % a, [P, 4 * H], BF16, 12 * KIB if a == PASSES - 1 else None)
+            wa_bf = sb("wa_bf%d" % a, [P, 4 * H], BF16, 4 * KIB * a)
             dealt = wa_bf[:].rearrange("p (u v m j) -> p u m j v", u=2, v=2, j=4)
             rows = wa_raw[a][:].rearrange("p j (m u v) -> p u m j v", u=2, v=2)
             for u in range(2):
@@ -219,24 +193,33 @@ def tile_list_grasp_view_value_kernel(tc, tab_words, tab_scales, offs, tab2_word
                 nc.vector.quantize_mx(out=wa_w[a][:, cols].bitcast(FP8X4), scales=wa_s[a][:, cols],
                                       in_=wa_bf[:, 8 * P * u : 8 * P * (u + 1)])
 
-        for a in range(PASSES):
-            quantise_wa(a)
-            for g in range(4):
-                project_a(a, g)
-        for g in range(4, VIEW_TILES):
-            for a in (2, 0, 1):
-                project_a(a, g)
-        for g in TILES_SQUARED_ON_GPSIMD:
-            nc.gpsimd.tensor_tensor(damp[g], roots_of_tile(g), roots_of_tile(g), ALU.mult)
-        for g in TILES_SQUARED_ON_SCALAR:
-            nc.scalar.activation(damp[g], roots_of_tile(g), ACT.Square)
-        nc.vector.tensor_copy(v2_s[:], tab2_s[:].indirect(offs2_sb[:]))
+        quantise_wa(0)
+        quantise_wa(1)
         nc.vector.tensor_copy(v2_w[:], tab2_w[:].bitcast(U32).indirect(offs2_sb[:]))
+        quantise_wa(2)
+        nc.vector.tensor_copy(v2_s[:], tab2_s[:].indirect(offs2_sb[:]))
+        for g in range(VIEW_TILES):
+            for a in A_PASS_ORDER[g // 2]:
+                project_a(a, g)
+
+        damp = {}
+
+        def square_roots(g):
+            damp_tile = sb("damp%d" % g, [P, 2, 2 * P], F32, GPSIMD_SQUARES.get(g))
+            damp[g] = damp_tile[:]
+            roots = root[g // 2][:, :, 2 * P * (g % 2) : 2 * P * (g % 2 + 1)]
+            if g in GPSIMD_SQUARES:
+                nc.gpsimd.tensor_tensor(damp[g], roots, roots, ALU.mult)
+            else:
+                nc.scalar.activation(damp[g], roots, ACT.Square)
+
+        for g in range(VIEW_TILES - len(SQUARED_BEHIND_CHUNK)):
+            square_roots(g)
 
         first = 0
         for tiles in CHUNK_TILES:
             width = P * tiles
-            h_bf = sb("h_bf%d" % first, [P, tiles, H], BF16, 22 * KIB if first == 0 else None)
+            h_bf = sb("h_bf%d" % first, [P, tiles, H], BF16, GPSIMD_SQUARES.get(SQUARED_BEHIND_CHUNK.get(first)))
             for n in range(tiles):
                 g = first + n
                 nc.vector.tensor_tensor(h_bf[:, n, :].rearrange("p (j u v) -> p j u v", u=2, v=2),
@@ -246,10 +229,8 @@ def tile_list_grasp_view_value_kernel(tc, tab_words, tab_scales, offs, tab2_word
             h_s = sb("h_s%d" % first, [P, width], U8)
             nc.vector.quantize_mx(out=h_w[:].bitcast(FP8X4), scales=h_s[:],
                                   in_=h_bf[:].rearrange("p g r -> p (g r)"))
-            if first == 0:
-                last_damp = sb("last_damp", [P, 2, 2 * P], F32, 22 * KIB)
-                damp[LAST_TILE] = last_damp[:]
-                nc.gpsimd.tensor_tensor(damp[LAST_TILE], roots_of_tile(LAST_TILE), roots_of_tile(LAST_TILE), ALU.mult)
+            if first in SQUARED_BEHIND_CHUNK:
+                square_roots(SQUARED_BEHIND_CHUNK[first])
             y_ps = [bank(g, "y_ps%d" % g) for g in range(first, first + tiles)]
             for i in range(S2 // P):
                 rows = slice(P * i, P * (i + 1))

@@ -21,7 +21,8 @@ PASSES = K // 512
 VIEW_TILES = S // P
 HALF = S // 2
 CHUNK_TILES = (2, 2, 2, 1, 1)
-PARKED_ROWS = (8, 16, 72, 80)
+PARKED_ROW = (None, 4, 5)
+GRASP_PLANE = 4
 QUARTER = S // 4
 B_PASS_ORDER = ((0, 1, 2), (0, 1, 2), (0, 2, 1), (2, 0, 1))
 A_PASS_ORDER = ((0, 1, 2), (0, 1, 2), (0, 1, 2), (2, 0, 1))
@@ -80,33 +81,35 @@ def tile_list_grasp_view_value_kernel(tc, tab_words, tab_scales, offs, tab2_word
             nc.sync.dma_start(wa_raw[a][:], wa[512 * a : 512 * (a + 1), :].rearrange("(p j) r -> p j r", j=4))
 
         nc.sync.dma_start(offs_sb[:], offs)
-        for q in range(4):
-            queue = nc.scalar if q < 3 else nc.sync
-            queue.dma_start(tab_s[32 * q : 32 * q + 4, :].bitcast(I32),
-                            tab_scales[0, 4 * q : 4 * q + 4, :].bitcast(I32))
-        for pair in range(2):
-            first_row = PARKED_ROWS[2 * pair]
-            nc.sync.dma_start(tab_s[first_row : first_row + 16, :].bitcast(I32),
-                              tab_scales[1:PASSES, 8 * pair : 8 * pair + 8, :].rearrange("a n t -> n a t").bitcast(I32))
+        for r in range(4):
+            queue = nc.scalar if r < 3 else nc.sync
+            queue.dma_start(tab_s[r:P:32, :].bitcast(I32), tab_scales[0, r:16:4, :].bitcast(I32))
+        for a in range(1, PASSES):
+            nc.sync.dma_start(tab_s[PARKED_ROW[a] : P : 8, :].bitcast(I32), tab_scales[a].bitcast(I32))
         load_table(0)
-        for q in range(4):
-            nc.sync.dma_start(wb_s[32 * q : 32 * q + 4, :, :].bitcast(I32),
-                              wb_scales[:, 4 * q : 4 * q + 4, :].rearrange("a r n -> r a n").bitcast(I32))
+        for r in range(4):
+            nc.sync.dma_start(wb_s[r:P:32, :, :].bitcast(I32),
+                              wb_scales[:, r:16:4, :].rearrange("a q n -> q a n").bitcast(I32))
         nc.sync.dma_start(wb_w[:].bitcast(I32), wb_words.rearrange("a p n -> p a n").bitcast(I32))
         load_table(1)
 
         nc.vector.tensor_copy(v_s_gathered[:], tab_s[:].indirect(offs_sb[:]))
-        for q in range(4):
-            nc.sync.dma_start(v_s_moved[32 * q : 32 * q + 4, :, :].bitcast(I32),
-                              v_s_gathered[PARKED_ROWS[q] : PARKED_ROWS[q] + 8, :].bitcast(I32))
+
+        def move_scale_rows(a):
+            for r in range(4):
+                nc.sync.dma_start(v_s_moved[r:P:32, a - 1, :].bitcast(I32),
+                                  v_s_gathered[PARKED_ROW[a] + 8 * r : P : 32, :].bitcast(I32))
+
+        move_scale_rows(1)
         load_table(2)
+        move_scale_rows(2)
         load_wa(0)
         load_wa(1)
         nc.sync.dma_start(offs2_sb[:], offs2)
         nc.sync.dma_start(tab2_w[:], tab2_words[0].rearrange("p n t -> p (n t)").bitcast(I32))
-        for q in range(4):
-            nc.sync.dma_start(tab2_s[32 * q : 32 * q + 4, :].bitcast(I32),
-                              tab2_scales[0, 4 * q : 4 * q + 4, :].bitcast(I32))
+        for r in range(4):
+            nc.sync.dma_start(tab2_s[GRASP_PLANE + r : P : 32, :].bitcast(I32),
+                              tab2_scales[0, r:16:4, :].bitcast(I32))
         load_wa(2)
         with nc.allow_non_contiguous_dma(reason="one bias value a partition"):
             nc.sync.dma_start(bias[:], c.rearrange("(n p) -> p n", p=P))
@@ -236,7 +239,7 @@ def tile_list_grasp_view_value_kernel(tc, tab_words, tab_scales, offs, tab2_word
                 rows = slice(P * i, P * (i + 1))
                 place = (i * width) % 512
                 nc.tensor.matmul_mx(out=y_ps[i * width // 512][:, place : place + width],
-                                    lhsT=v2_w[:, rows].bitcast(FP8X4), lhsT_scale=v2_s[:, rows],
+                                    lhsT=v2_w[:, rows].bitcast(FP8X4), lhsT_scale=v2_s[GRASP_PLANE:P, rows],
                                     rhs=h_w[:].bitcast(FP8X4), rhs_scale=h_s[:], start=True, stop=True)
             rows_a_store = min(2, 4 // tiles)
             for i0 in range(0, S2 // P, rows_a_store):

@@ -67,12 +67,11 @@ def tile_list_grasp_view_value_kernel(tc, tab_words, tab_scales, offs, tab2_word
         wb_w_dealt = [sb("wb_w_dealt%d" % a, [P, H], U16) for a in range(PASSES)]
         wb_s_dealt = [sb("wb_s_dealt%d" % a, [P, H], U8) for a in range(PASSES)]
 
-        nc.vector.memset(tab_s[:, : T // 2].bitcast(I32), 0)
-        nc.gpsimd.memset(tab_s[:, T // 2 :].bitcast(I32), 0)
-        nc.gpsimd.memset(wb_s[:].rearrange("p a n -> p (a n)").bitcast(I32), 0)
-        nc.gpsimd.memset(v_s_moved[:].rearrange("p a n -> p (a n)").bitcast(I32), 0)
-        nc.gpsimd.memset(tab2_s[:].bitcast(I32), 0)
-        nc.gpsimd.memset(one[:], 1.0)
+        nc.vector.memset(tab_s[:].bitcast(I32), 0)
+        nc.vector.memset(wb_s[:].rearrange("p a n -> p (a n)").bitcast(I32), 0)
+        nc.vector.memset(v_s_moved[:].rearrange("p a n -> p (a n)").bitcast(I32), 0)
+        nc.vector.memset(tab2_s[:].bitcast(I32), 0)
+        nc.vector.memset(one[:], 1.0)
 
         def load_table(a):
             nc.sync.dma_start(tab_w[a][:], tab_words[a].rearrange("p n t -> p (n t)").bitcast(I32))
@@ -81,6 +80,7 @@ def tile_list_grasp_view_value_kernel(tc, tab_words, tab_scales, offs, tab2_word
             nc.sync.dma_start(wa_raw[a][:], wa[512 * a : 512 * (a + 1), :].rearrange("(p j) r -> p j r", j=4))
 
         nc.sync.dma_start(offs_sb[:], offs)
+        nc.sync.dma_start(offs2_sb[:], offs2)
         for r in range(4):
             queue = nc.scalar if r < 3 else nc.sync
             queue.dma_start(tab_s[r:P:32, :].bitcast(I32), tab_scales[0, r:16:4, :].bitcast(I32))
@@ -105,7 +105,6 @@ def tile_list_grasp_view_value_kernel(tc, tab_words, tab_scales, offs, tab2_word
         move_scale_rows(2)
         load_wa(0)
         load_wa(1)
-        nc.sync.dma_start(offs2_sb[:], offs2)
         nc.sync.dma_start(tab2_w[:], tab2_words[0].rearrange("p n t -> p (n t)").bitcast(I32))
         for r in range(4):
             nc.sync.dma_start(tab2_s[GRASP_PLANE + r : P : 32, :].bitcast(I32),

@@ -21,10 +21,10 @@ PASSES = K // 512
 VIEW_TILES = S // P
 HALF = S // 2
 CHUNK_TILES = (2, 2, 2, 1, 1)
-PARKED_ROW = (None, 4, 5)
+PARKED_ROWS = (8, 16, 72, 80)
 GRASP_PLANE = 4
 QUARTER = S // 4
-B_PASS_ORDER = ((0, 1, 2), (0, 1, 2), (0, 2, 1), (2, 0, 1))
+B_PASS_ORDER = ((0, 1, 2), (0, 2, 1), (2, 0, 1), (2, 0, 1))
 A_PASS_ORDER = ((0, 1, 2), (0, 1, 2), (0, 1, 2), (2, 0, 1))
 KIB = 1024
 GPSIMD_SQUARES = {0: 4 * KIB, 1: 8 * KIB, 4: 10 * KIB, 6: 12 * KIB, 7: 14 * KIB}
@@ -80,31 +80,28 @@ def tile_list_grasp_view_value_kernel(tc, tab_words, tab_scales, offs, tab2_word
             nc.sync.dma_start(wa_raw[a][:], wa[512 * a : 512 * (a + 1), :].rearrange("(p j) r -> p j r", j=4))
 
         nc.sync.dma_start(offs_sb[:], offs)
-        nc.sync.dma_start(offs2_sb[:], offs2)
+        nc.sync.dma_start(wb_w[:].bitcast(I32), wb_words.rearrange("a p n -> p a n").bitcast(I32))
         for r in range(4):
             queue = nc.scalar if r < 3 else nc.sync
             queue.dma_start(tab_s[r:P:32, :].bitcast(I32), tab_scales[0, r:16:4, :].bitcast(I32))
-        for a in range(1, PASSES):
-            nc.sync.dma_start(tab_s[PARKED_ROW[a] : P : 8, :].bitcast(I32), tab_scales[a].bitcast(I32))
+        for pair in range(2):
+            first_row = PARKED_ROWS[2 * pair]
+            nc.sync.dma_start(tab_s[first_row : first_row + 16, :].bitcast(I32),
+                              tab_scales[1:PASSES, 8 * pair : 8 * pair + 8, :].rearrange("a n t -> n a t").bitcast(I32))
         load_table(0)
         for r in range(4):
             nc.sync.dma_start(wb_s[r:P:32, :, :].bitcast(I32),
                               wb_scales[:, r:16:4, :].rearrange("a q n -> q a n").bitcast(I32))
-        nc.sync.dma_start(wb_w[:].bitcast(I32), wb_words.rearrange("a p n -> p a n").bitcast(I32))
         load_table(1)
 
         nc.vector.tensor_copy(v_s_gathered[:], tab_s[:].indirect(offs_sb[:]))
-
-        def move_scale_rows(a):
-            for r in range(4):
-                nc.sync.dma_start(v_s_moved[r:P:32, a - 1, :].bitcast(I32),
-                                  v_s_gathered[PARKED_ROW[a] + 8 * r : P : 32, :].bitcast(I32))
-
-        move_scale_rows(1)
+        for q in (0, 2, 1, 3):
+            nc.sync.dma_start(v_s_moved[32 * q : 32 * q + 4, :, :].bitcast(I32),
+                              v_s_gathered[PARKED_ROWS[q] : PARKED_ROWS[q] + 8, :].bitcast(I32))
         load_table(2)
-        move_scale_rows(2)
         load_wa(0)
         load_wa(1)
+        nc.sync.dma_start(offs2_sb[:], offs2)
         nc.sync.dma_start(tab2_w[:], tab2_words[0].rearrange("p n t -> p (n t)").bitcast(I32))
         for r in range(4):
             nc.sync.dma_start(tab2_s[GRASP_PLANE + r : P : 32, :].bitcast(I32),
@@ -155,14 +152,15 @@ def tile_list_grasp_view_value_kernel(tc, tab_words, tab_scales, offs, tab2_word
                                     rhs=v_w[a, k].bitcast(FP8X4), rhs_scale=v_s(a, QUARTER * k, QUARTER),
                                     start=(a == order[0] and v == 0), stop=(a == order[-1] and v == 1))
 
-        root = [sb("root%d" % k, [P, 2, 2 * QUARTER], F32) for k in range(4)]
+        root = [sb("root%d" % k, [P, 4 * QUARTER], F32) for k in range(4)]
 
         def inverse_roots(k):
             mag = sb("mag%d" % k, [P, 2, 2 * QUARTER], F32)
             for u in range(2):
                 nc.scalar.activation(mag[:, u, :].rearrange("p (j v) -> p j v", v=2),
                                      b_ps[k, u][:].rearrange("p (v j) -> p j v", v=2), ACT.Abs)
-            nc.scalar.activation(root[k][:], mag[:], ACT.Abs_reciprocal_sqrt, bias=1.0)
+            nc.scalar.activation(root[k][:].rearrange("p (j u v) -> p j u v", u=2, v=2),
+                                 mag[:].rearrange("p u (j v) -> p j u v", v=2), ACT.Abs_reciprocal_sqrt, bias=1.0)
 
         for k in range(4):
             for a in B_PASS_ORDER[k]:
@@ -207,9 +205,9 @@ def tile_list_grasp_view_value_kernel(tc, tab_words, tab_scales, offs, tab2_word
         damp = {}
 
         def square_roots(g):
-            damp_tile = sb("damp%d" % g, [P, 2, 2 * P], F32, GPSIMD_SQUARES.get(g))
+            damp_tile = sb("damp%d" % g, [P, H], F32, GPSIMD_SQUARES.get(g))
             damp[g] = damp_tile[:]
-            roots = root[g // 2][:, :, 2 * P * (g % 2) : 2 * P * (g % 2 + 1)]
+            roots = root[g // 2][:, H * (g % 2) : H * (g % 2 + 1)]
             if g in GPSIMD_SQUARES:
                 nc.gpsimd.tensor_tensor(damp[g], roots, roots, ALU.mult)
             else:
@@ -224,9 +222,9 @@ def tile_list_grasp_view_value_kernel(tc, tab_words, tab_scales, offs, tab2_word
             h_bf = sb("h_bf%d" % first, [P, tiles, H], BF16, GPSIMD_SQUARES.get(SQUARED_BEHIND_CHUNK.get(first)))
             for n in range(tiles):
                 g = first + n
-                nc.vector.tensor_tensor(h_bf[:, n, :].rearrange("p (j u v) -> p j u v", u=2, v=2),
-                                        a_ps[g][:].rearrange("p (u v j) -> p j u v", u=2, v=2),
-                                        damp[g].rearrange("p u (j v) -> p j u v", v=2), ALU.mult)
+                nc.vector.tensor_tensor(h_bf[:, n, :].rearrange("p (j t) -> p j t", t=4),
+                                        a_ps[g][:].rearrange("p (t j) -> p j t", t=4),
+                                        damp[g].rearrange("p (j t) -> p j t", t=4), ALU.mult)
             h_w = sb("h_w%d" % first, [P, width], U32)
             h_s = sb("h_s%d" % first, [P, width], U8)
             nc.vector.quantize_mx(out=h_w[:].bitcast(FP8X4), scales=h_s[:],

@@ -20,14 +20,15 @@ P = 128
 PASSES = K // 512
 VIEW_TILES = S // P
 HALF = S // 2
-CHUNK_TILES = (2, 2, 2, 1, 1)
+Y_BANKS = ((0, 1), (2, 3), (4, 5), (0, 1))
+STORE_ROWS = ((1, 1, 2), (2, 2), (2, 2), (2, 1, 1))
 PARKED_ROWS = (8, 16, 72, 80)
 GRASP_PLANE = 4
 QUARTER = S // 4
-B_PASS_ORDER = ((0, 1, 2), (0, 2, 1), (2, 0, 1), (2, 0, 1))
+B_PASS_ORDER = ((0, 1, 2), (0, 1, 2), (0, 2, 1), (2, 0, 1))
 A_PASS_ORDER = ((0, 1, 2), (0, 1, 2), (0, 1, 2), (2, 0, 1))
 KIB = 1024
-GPSIMD_SQUARES = {0: 4 * KIB, 1: 8 * KIB, 4: 10 * KIB, 6: 12 * KIB, 7: 14 * KIB}
+GPSIMD_SQUARES = {0: 4 * KIB, 1: 13 * KIB // 2, 4: 10 * KIB, 6: 12 * KIB, 7: 14 * KIB}
 SQUARED_BEHIND_CHUNK = {0: 6, 2: 7}
 
 
@@ -55,13 +56,12 @@ def tile_list_grasp_view_value_kernel(tc, tab_words, tab_scales, offs, tab2_word
         tab2_s = sb("tab2_s", [P, T2], U8)
         wb_w = sb("wb_w", [P, PASSES, 2 * H], U8)
         wb_s = sb("wb_s", [P, PASSES, H], U8)
-        wa_raw = [sb("wa_raw%d" % a, [P, 4, H], F32, (None, None, 16 * KIB)[a]) for a in range(PASSES)]
+        wa_raw = [sb("wa_raw%d" % a, [P, 4, H], F32) for a in range(PASSES)]
         wa_w = [sb("wa_w%d" % a, [P, H], U32) for a in range(PASSES)]
         wa_s = [sb("wa_s%d" % a, [P, H], U8) for a in range(PASSES)]
         v_s_gathered = sb("v_s_gathered", [P, S], U8)
         v_s_moved = sb("v_s_moved", [P, PASSES - 1, S], U8)
         v2_w = sb("v2_w", [P, S2], U32)
-        v2_s = sb("v2_s", [P, S2], U8, 16 * KIB)
         bias = sb("bias", [P, S2 // P], F32)
         one = sb("one", [P, 1], F32)
         wb_w_dealt = [sb("wb_w_dealt%d" % a, [P, H], U16) for a in range(PASSES)]
@@ -82,8 +82,7 @@ def tile_list_grasp_view_value_kernel(tc, tab_words, tab_scales, offs, tab2_word
         nc.sync.dma_start(offs_sb[:], offs)
         nc.sync.dma_start(wb_w[:].bitcast(I32), wb_words.rearrange("a p n -> p a n").bitcast(I32))
         for r in range(4):
-            queue = nc.scalar if r < 3 else nc.sync
-            queue.dma_start(tab_s[r:P:32, :].bitcast(I32), tab_scales[0, r:16:4, :].bitcast(I32))
+            nc.sync.dma_start(tab_s[r:P:32, :].bitcast(I32), tab_scales[0, r:16:4, :].bitcast(I32))
         for pair in range(2):
             first_row = PARKED_ROWS[2 * pair]
             nc.sync.dma_start(tab_s[first_row : first_row + 16, :].bitcast(I32),
@@ -113,9 +112,15 @@ def tile_list_grasp_view_value_kernel(tc, tab_words, tab_scales, offs, tab2_word
         warm = sb("warm", [P, 1], F32)
         nc.scalar.activation(warm[:], one[:], ACT.Abs_reciprocal_sqrt, bias=1.0)
 
+        def deal_wb_scales(a, slots):
+            nc.gpsimd.tensor_copy(wb_s_dealt[a][:].rearrange("p (t m) -> p t m", t=4)[:, slots],
+                                  wb_s[:, a, :].rearrange("p (m t) -> p t m", t=4)[:, slots])
+
+        deal_wb_scales(0, slice(0, 2))
+        deal_wb_scales(0, slice(2, 4))
         for a in range(PASSES):
-            nc.gpsimd.tensor_copy(wb_s_dealt[a][:].rearrange("p (t m) -> p t m", t=4),
-                                  wb_s[:, a, :].rearrange("p (m t) -> p t m", t=4))
+            if a > 0:
+                deal_wb_scales(a, slice(0, 4))
             nc.scalar.copy(wb_w_dealt[a][:].rearrange("p (t m) -> p t m", t=4),
                            wb_w[:, a, :].bitcast(U16).rearrange("p (m t) -> p t m", t=4))
 
@@ -132,9 +137,11 @@ def tile_list_grasp_view_value_kernel(tc, tab_words, tab_scales, offs, tab2_word
                 return v_s_gathered[:, j0 : j0 + width]
             return v_s_moved[:, a - 1, j0 : j0 + width]
 
-        for a in range(PASSES - 1):
-            for j0 in (0, HALF):
-                gather_words(a, j0, HALF)
+        gather_words(0, 0, QUARTER)
+        gather_words(0, QUARTER, QUARTER)
+        gather_words(0, HALF, HALF)
+        for j0 in (0, HALF):
+            gather_words(1, j0, HALF)
         for j0 in range(0, S, QUARTER):
             gather_words(PASSES - 1, j0, QUARTER)
 
@@ -196,8 +203,15 @@ def tile_list_grasp_view_value_kernel(tc, tab_words, tab_scales, offs, tab2_word
         quantise_wa(0)
         quantise_wa(1)
         nc.vector.tensor_copy(v2_w[:], tab2_w[:].bitcast(U32).indirect(offs2_sb[:]))
+        v2_s = []
+
+        def gather_grasp_scales(half, offset):
+            v2_s.append(sb("v2_s%d" % half, [P, S2 // 2], U8, offset))
+            nc.vector.tensor_copy(v2_s[half][:], tab2_s[:].indirect(offs2_sb[:, 16 * half : 16 * (half + 1)]))
+
+        gather_grasp_scales(0, None)
         quantise_wa(2)
-        nc.vector.tensor_copy(v2_s[:], tab2_s[:].indirect(offs2_sb[:]))
+        gather_grasp_scales(1, 9 * KIB)
         for g in range(VIEW_TILES):
             for a in A_PASS_ORDER[g // 2]:
                 project_a(a, g)
@@ -216,8 +230,7 @@ def tile_list_grasp_view_value_kernel(tc, tab_words, tab_scales, offs, tab2_word
         for g in range(VIEW_TILES - len(SQUARED_BEHIND_CHUNK)):
             square_roots(g)
 
-        first = 0
-        for tiles in CHUNK_TILES:
+        def embed_and_score(first, tiles, y_ps, column):
             width = P * tiles
             h_bf = sb("h_bf%d" % first, [P, tiles, H], BF16, GPSIMD_SQUARES.get(SQUARED_BEHIND_CHUNK.get(first)))
             for n in range(tiles):
@@ -231,22 +244,30 @@ def tile_list_grasp_view_value_kernel(tc, tab_words, tab_scales, offs, tab2_word
                                   in_=h_bf[:].rearrange("p g r -> p (g r)"))
             if first in SQUARED_BEHIND_CHUNK:
                 square_roots(SQUARED_BEHIND_CHUNK[first])
-            y_ps = [bank(g, "y_ps%d" % g) for g in range(first, first + tiles)]
+            if not y_ps:
+                y_ps.extend(bank(g, "y_ps%d" % first + "_%d" % g) for g in Y_BANKS[first // 2])
             for i in range(S2 // P):
-                rows = slice(P * i, P * (i + 1))
-                place = (i * width) % 512
-                nc.tensor.matmul_mx(out=y_ps[i * width // 512][:, place : place + width],
-                                    lhsT=v2_w[:, rows].bitcast(FP8X4), lhsT_scale=v2_s[GRASP_PLANE:P, rows],
+                place = QUARTER * (i % 2) + column
+                nc.tensor.matmul_mx(out=y_ps[i // 2][:, place : place + width],
+                                    lhsT=v2_w[:, P * i : P * (i + 1)].bitcast(FP8X4),
+                                    lhsT_scale=v2_s[i // 2][GRASP_PLANE:P, P * (i % 2) : P * (i % 2 + 1)],
                                     rhs=h_w[:].bitcast(FP8X4), rhs_scale=h_s[:], start=True, stop=True)
-            rows_a_store = min(2, 4 // tiles)
-            for i0 in range(0, S2 // P, rows_a_store):
-                res = sb("res%d_%d" % (first, i0), [P, rows_a_store, width], F32)
-                for n in range(rows_a_store):
+
+        for k in range(4):
+            y_ps = []
+            if k < 3:
+                embed_and_score(2 * k, 2, y_ps, 0)
+            else:
+                embed_and_score(2 * k, 1, y_ps, 0)
+                embed_and_score(2 * k + 1, 1, y_ps, P)
+            i0 = 0
+            for rows in STORE_ROWS[k]:
+                res = sb("res%d_%d" % (k, i0), [P, rows, QUARTER], F32)
+                for n in range(rows):
                     i = i0 + n
-                    place = (i * width) % 512
-                    nc.scalar.activation(res[:, n, :], y_ps[i * width // 512][:, place : place + width], ACT.Tanh,
-                                         bias=bias[:, i : i + 1])
+                    nc.scalar.activation(res[:, n, :], y_ps[i // 2][:, QUARTER * (i % 2) : QUARTER * (i % 2 + 1)],
+                                         ACT.Tanh, bias=bias[:, i : i + 1])
                 nc.sync.dma_start(
-                    out[P * i0 : P * (i0 + rows_a_store), P * first : P * first + width].rearrange("(n p) j -> p n j", p=P),
+                    out[P * i0 : P * (i0 + rows), QUARTER * k : QUARTER * (k + 1)].rearrange("(n p) j -> p n j", p=P),
                     res[:])
-            first += tiles
+                i0 += rows

@@ -20,7 +20,8 @@ P = 128
 PASSES = K // 512
 VIEW_TILES = S // P
 HALF = S // 2
-Y_BANKS = ((0, 1), (2, 3), (4, 5), (0, 1))
+A_BANKS = (0, 1, 2, 3, 4, 5, 6, 3)
+Y_BANKS = ((0, 1), (2, 7), (4, 5), (0, 1))
 STORE_ROWS = ((1, 1, 2), (2, 2), (2, 2), (2, 1, 1))
 PARKED_ROWS = (8, 16, 72, 80)
 GRASP_PLANE = 4
@@ -178,9 +179,9 @@ def tile_list_grasp_view_value_kernel(tc, tab_words, tab_scales, offs, tab2_word
         a_ps = {}
 
         def project_a(a, g):
-            order = A_PASS_ORDER[g // 2]
+            order = A_PASS_ORDER[g // 2] if g < VIEW_TILES - 1 else (0, 1, 2)
             if a == order[0]:
-                a_ps[g] = bank(g, "a_ps%d" % g)
+                a_ps[g] = bank(A_BANKS[g], "a_ps%d" % g)
             views = slice(P * (g % 2), P * (g % 2 + 1))
             for t in range(4):
                 cols = slice(P * t, P * (t + 1))
@@ -212,7 +213,7 @@ def tile_list_grasp_view_value_kernel(tc, tab_words, tab_scales, offs, tab2_word
         gather_grasp_scales(0, None)
         quantise_wa(2)
         gather_grasp_scales(1, 9 * KIB)
-        for g in range(VIEW_TILES):
+        for g in range(VIEW_TILES - 1):
             for a in A_PASS_ORDER[g // 2]:
                 project_a(a, g)
 
@@ -238,6 +239,9 @@ def tile_list_grasp_view_value_kernel(tc, tab_words, tab_scales, offs, tab2_word
                 nc.vector.tensor_tensor(h_bf[:, n, :].rearrange("p (j t) -> p j t", t=4),
                                         a_ps[g][:].rearrange("p (t j) -> p j t", t=4),
                                         damp[g].rearrange("p (j t) -> p j t", t=4), ALU.mult)
+                if g == A_BANKS[VIEW_TILES - 1]:
+                    for a in range(PASSES):
+                        project_a(a, VIEW_TILES - 1)
             h_w = sb("h_w%d" % first, [P, width], U32)
             h_s = sb("h_s%d" % first, [P, width], U8)
             nc.vector.quantize_mx(out=h_w[:].bitcast(FP8X4), scales=h_s[:],

@@ -23,13 +23,13 @@ HALF = S // 2
 A_BANKS = (0, 1, 2, 3, 4, 5, 6, 3)
 Y_BANKS = ((0, 1), (2, 7), (4, 5), (0, 1))
 STORE_ROWS = ((1, 1, 2), (2, 2), (2, 2), (2, 1, 1))
-PARKED_ROWS = (8, 16, 72, 80)
+PARKED_ROW = (None, 4, 5)
 GRASP_PLANE = 4
 QUARTER = S // 4
 B_PASS_ORDER = ((0, 1, 2), (0, 1, 2), (0, 2, 1), (2, 0, 1))
 A_PASS_ORDER = ((0, 1, 2), (0, 1, 2), (0, 1, 2), (2, 0, 1))
 KIB = 1024
-GPSIMD_SQUARES = {0: 4 * KIB, 1: 13 * KIB // 2, 4: 10 * KIB, 6: 12 * KIB, 7: 14 * KIB}
+GPSIMD_SQUARES = {0: 6 * KIB, 1: 9 * KIB, 4: 11 * KIB, 6: 13 * KIB, 7: 15 * KIB}
 SQUARED_BEHIND_CHUNK = {0: 6, 2: 7}
 
 
@@ -84,10 +84,8 @@ def tile_list_grasp_view_value_kernel(tc, tab_words, tab_scales, offs, tab2_word
         nc.sync.dma_start(wb_w[:].bitcast(I32), wb_words.rearrange("a p n -> p a n").bitcast(I32))
         for r in range(4):
             nc.sync.dma_start(tab_s[r:P:32, :].bitcast(I32), tab_scales[0, r:16:4, :].bitcast(I32))
-        for pair in range(2):
-            first_row = PARKED_ROWS[2 * pair]
-            nc.sync.dma_start(tab_s[first_row : first_row + 16, :].bitcast(I32),
-                              tab_scales[1:PASSES, 8 * pair : 8 * pair + 8, :].rearrange("a n t -> n a t").bitcast(I32))
+        for a in range(1, PASSES):
+            nc.sync.dma_start(tab_s[PARKED_ROW[a] : P : 8, :].bitcast(I32), tab_scales[a].bitcast(I32))
         load_table(0)
         for r in range(4):
             nc.sync.dma_start(wb_s[r:P:32, :, :].bitcast(I32),
@@ -95,10 +93,15 @@ def tile_list_grasp_view_value_kernel(tc, tab_words, tab_scales, offs, tab2_word
         load_table(1)
 
         nc.vector.tensor_copy(v_s_gathered[:], tab_s[:].indirect(offs_sb[:]))
-        for q in (0, 2, 1, 3):
-            nc.sync.dma_start(v_s_moved[32 * q : 32 * q + 4, :, :].bitcast(I32),
-                              v_s_gathered[PARKED_ROWS[q] : PARKED_ROWS[q] + 8, :].bitcast(I32))
+
+        def move_scale_rows(a):
+            for r in range(4):
+                nc.sync.dma_start(v_s_moved[r:P:32, a - 1, :].bitcast(I32),
+                                  v_s_gathered[PARKED_ROW[a] + 8 * r : P : 32, :].bitcast(I32))
+
+        move_scale_rows(1)
         load_table(2)
+        move_scale_rows(2)
         load_wa(0)
         load_wa(1)
         nc.sync.dma_start(offs2_sb[:], offs2)
@@ -191,28 +194,21 @@ def tile_list_grasp_view_value_kernel(tc, tab_words, tab_scales, offs, tab2_word
                                     start=(a == order[0] and t == 0), stop=(a == order[-1] and t == 3))
 
         def quantise_wa(a):
-            wa_bf = sb("wa_bf%d" % a, [P, 4 * H], BF16, 4 * KIB * a)
-            dealt = wa_bf[:].rearrange("p (u v m j) -> p u m j v", u=2, v=2, j=4)
+            wa_bf = [sb("wa_bf%d_%d" % (a, u), [P, 2 * H], BF16, 2 * KIB * (2 * a + u)) for u in range(2)]
             rows = wa_raw[a][:].rearrange("p j (m u v) -> p u m j v", u=2, v=2)
             for u in range(2):
-                nc.vector.tensor_copy(dealt[:, u], rows[:, u])
+                nc.vector.tensor_copy(wa_bf[u][:].rearrange("p (v m j) -> p m j v", v=2, j=4), rows[:, u])
             for u in range(2):
                 cols = slice(2 * P * u, 2 * P * (u + 1))
                 nc.vector.quantize_mx(out=wa_w[a][:, cols].bitcast(FP8X4), scales=wa_s[a][:, cols],
-                                      in_=wa_bf[:, 8 * P * u : 8 * P * (u + 1)])
+                                      in_=wa_bf[u][:])
 
         quantise_wa(0)
         quantise_wa(1)
         nc.vector.tensor_copy(v2_w[:], tab2_w[:].bitcast(U32).indirect(offs2_sb[:]))
-        v2_s = []
-
-        def gather_grasp_scales(half, offset):
-            v2_s.append(sb("v2_s%d" % half, [P, S2 // 2], U8, offset))
-            nc.vector.tensor_copy(v2_s[half][:], tab2_s[:].indirect(offs2_sb[:, 16 * half : 16 * (half + 1)]))
-
-        gather_grasp_scales(0, None)
         quantise_wa(2)
-        gather_grasp_scales(1, 9 * KIB)
+        v2_s = sb("v2_s", [P, S2], U8, 8 * KIB)
+        nc.vector.tensor_copy(v2_s[:], tab2_s[:].indirect(offs2_sb[:]))
         for g in range(VIEW_TILES - 1):
             for a in A_PASS_ORDER[g // 2]:
                 project_a(a, g)
@@ -254,7 +250,7 @@ def tile_list_grasp_view_value_kernel(tc, tab_words, tab_scales, offs, tab2_word
                 place = QUARTER * (i % 2) + column
                 nc.tensor.matmul_mx(out=y_ps[i // 2][:, place : place + width],
                                     lhsT=v2_w[:, P * i : P * (i + 1)].bitcast(FP8X4),
-                                    lhsT_scale=v2_s[i // 2][GRASP_PLANE:P, P * (i % 2) : P * (i % 2 + 1)],
+                                    lhsT_scale=v2_s[GRASP_PLANE:P, P * i : P * (i + 1)],
                                     rhs=h_w[:].bitcast(FP8X4), rhs_scale=h_s[:], start=True, stop=True)
 
         for k in range(4):

@@ -29,8 +29,9 @@ QUARTER = S // 4
 B_PASS_ORDER = ((0, 1, 2), (0, 1, 2), (0, 2, 1), (2, 0, 1))
 A_PASS_ORDER = ((0, 1, 2), (0, 1, 2), (0, 1, 2), (2, 0, 1))
 KIB = 1024
-GPSIMD_SQUARES = {0: 6 * KIB, 1: 9 * KIB, 4: 11 * KIB, 6: 13 * KIB, 7: 15 * KIB}
-SQUARED_BEHIND_CHUNK = {0: 6, 2: 7}
+GPSIMD_SQUARES = (0, 1, 4, 6, 7)
+DAMP_OFFSET = {0: 4 * KIB, 1: 13 * KIB // 2, 2: 13 * KIB, 4: 11 * KIB, 6: 13 * KIB, 7: 11 * KIB}
+SQUARED_BEHIND_PRODUCT = {2: 6, 4: 7}
 
 
 def tile_list_grasp_view_value_kernel(tc, tab_words, tab_scales, offs, tab2_words, tab2_scales, offs2,
@@ -207,7 +208,7 @@ def tile_list_grasp_view_value_kernel(tc, tab_words, tab_scales, offs, tab2_word
         quantise_wa(1)
         nc.vector.tensor_copy(v2_w[:], tab2_w[:].bitcast(U32).indirect(offs2_sb[:]))
         quantise_wa(2)
-        v2_s = sb("v2_s", [P, S2], U8, 8 * KIB)
+        v2_s = sb("v2_s", [P, S2], U8, 9 * KIB)
         nc.vector.tensor_copy(v2_s[:], tab2_s[:].indirect(offs2_sb[:]))
         for g in range(VIEW_TILES - 1):
             for a in A_PASS_ORDER[g // 2]:
@@ -216,7 +217,7 @@ def tile_list_grasp_view_value_kernel(tc, tab_words, tab_scales, offs, tab2_word
         damp = {}
 
         def square_roots(g):
-            damp_tile = sb("damp%d" % g, [P, H], F32, GPSIMD_SQUARES.get(g))
+            damp_tile = sb("damp%d" % g, [P, H], F32, DAMP_OFFSET.get(g))
             damp[g] = damp_tile[:]
             roots = root[g // 2][:, H * (g % 2) : H * (g % 2 + 1)]
             if g in GPSIMD_SQUARES:
@@ -224,17 +225,19 @@ def tile_list_grasp_view_value_kernel(tc, tab_words, tab_scales, offs, tab2_word
             else:
                 nc.scalar.activation(damp[g], roots, ACT.Square)
 
-        for g in range(VIEW_TILES - len(SQUARED_BEHIND_CHUNK)):
+        for g in range(VIEW_TILES - len(SQUARED_BEHIND_PRODUCT)):
             square_roots(g)
 
         def embed_and_score(first, tiles, y_ps, column):
             width = P * tiles
-            h_bf = sb("h_bf%d" % first, [P, tiles, H], BF16, GPSIMD_SQUARES.get(SQUARED_BEHIND_CHUNK.get(first)))
+            h_bf = sb("h_bf%d" % first, [P, tiles, H], BF16)
             for n in range(tiles):
                 g = first + n
                 nc.vector.tensor_tensor(h_bf[:, n, :].rearrange("p (j t) -> p j t", t=4),
                                         a_ps[g][:].rearrange("p (t j) -> p j t", t=4),
                                         damp[g].rearrange("p (j t) -> p j t", t=4), ALU.mult)
+                if g in SQUARED_BEHIND_PRODUCT:
+                    square_roots(SQUARED_BEHIND_PRODUCT[g])
                 if g == A_BANKS[VIEW_TILES - 1]:
                     for a in range(PASSES):
                         project_a(a, VIEW_TILES - 1)
@@ -242,8 +245,6 @@ def tile_list_grasp_view_value_kernel(tc, tab_words, tab_scales, offs, tab2_word
             h_s = sb("h_s%d" % first, [P, width], U8)
             nc.vector.quantize_mx(out=h_w[:].bitcast(FP8X4), scales=h_s[:],
                                   in_=h_bf[:].rearrange("p g r -> p (g r)"))
-            if first in SQUARED_BEHIND_CHUNK:
-                square_roots(SQUARED_BEHIND_CHUNK[first])
             if not y_ps:
                 y_ps.extend(bank(g, "y_ps%d" % first + "_%d" % g) for g in Y_BANKS[first // 2])
             for i in range(S2 // P):

@@ -30,7 +30,8 @@ B_PASS_ORDER = ((0, 1, 2), (0, 1, 2), (0, 2, 1), (2, 0, 1))
 A_PASS_ORDER = ((0, 1, 2), (0, 1, 2), (0, 1, 2), (2, 0, 1))
 KIB = 1024
 GPSIMD_SQUARES = (0, 1, 4, 6, 7)
-DAMP_OFFSET = {0: 4 * KIB, 1: 13 * KIB // 2, 2: 13 * KIB, 4: 11 * KIB, 6: 13 * KIB, 7: 11 * KIB}
+SHARED_SQUARE = 2
+DAMP_OFFSET = {0: 3 * KIB, 1: 7 * KIB, 2: 5 * KIB, 4: 11 * KIB, 6: 5 * KIB, 7: 11 * KIB}
 SQUARED_BEHIND_PRODUCT = {2: 6, 4: 7}
 
 
@@ -207,9 +208,15 @@ def tile_list_grasp_view_value_kernel(tc, tab_words, tab_scales, offs, tab2_word
         quantise_wa(0)
         quantise_wa(1)
         nc.vector.tensor_copy(v2_w[:], tab2_w[:].bitcast(U32).indirect(offs2_sb[:]))
+        v2_s = []
+
+        def gather_grasp_scales(half, offset):
+            v2_s.append(sb("v2_s%d" % half, [P, S2 // 2], U8, offset))
+            nc.vector.tensor_copy(v2_s[half][:], tab2_s[:].indirect(offs2_sb[:, 16 * half : 16 * (half + 1)]))
+
+        gather_grasp_scales(0, None)
         quantise_wa(2)
-        v2_s = sb("v2_s", [P, S2], U8, 9 * KIB)
-        nc.vector.tensor_copy(v2_s[:], tab2_s[:].indirect(offs2_sb[:]))
+        gather_grasp_scales(1, 9 * KIB)
         for g in range(VIEW_TILES - 1):
             for a in A_PASS_ORDER[g // 2]:
                 project_a(a, g)
@@ -222,6 +229,9 @@ def tile_list_grasp_view_value_kernel(tc, tab_words, tab_scales, offs, tab2_word
             roots = root[g // 2][:, H * (g % 2) : H * (g % 2 + 1)]
             if g in GPSIMD_SQUARES:
                 nc.gpsimd.tensor_tensor(damp[g], roots, roots, ALU.mult)
+            elif g == SHARED_SQUARE:
+                nc.gpsimd.tensor_tensor(damp[g][:, : H // 2], roots[:, : H // 2], roots[:, : H // 2], ALU.mult)
+                nc.scalar.activation(damp[g][:, H // 2 :], roots[:, H // 2 :], ACT.Square)
             else:
                 nc.scalar.activation(damp[g], roots, ACT.Square)
 
@@ -251,7 +261,7 @@ def tile_list_grasp_view_value_kernel(tc, tab_words, tab_scales, offs, tab2_word
                 place = QUARTER * (i % 2) + column
                 nc.tensor.matmul_mx(out=y_ps[i // 2][:, place : place + width],
                                     lhsT=v2_w[:, P * i : P * (i + 1)].bitcast(FP8X4),
-                                    lhsT_scale=v2_s[GRASP_PLANE:P, P * i : P * (i + 1)],
+                                    lhsT_scale=v2_s[i // 2][GRASP_PLANE:P, P * (i % 2) : P * (i % 2 + 1)],
                                     rhs=h_w[:].bitcast(FP8X4), rhs_scale=h_s[:], start=True, stop=True)
 
         for k in range(4):

from contextlib import ExitStack

import concourse.mybir as mybir

K, H, T, S, T2, S2 = 1536, 512, 2048, 1024, 1024, 512
FLOPS = 2 * K * H * S * 2 + 2 * H * S2 * S

F32 = mybir.dt.float32
BF16 = mybir.dt.bfloat16
I32 = mybir.dt.int32
U32 = mybir.dt.uint32
U16 = mybir.dt.uint16
U8 = mybir.dt.uint8
FP8X4 = mybir.dt.float8_e4m3fn_x4
FP4X4 = mybir.dt.float4_e2m1fn_x4
ACT = mybir.ActivationFunctionType
ALU = mybir.AluOpType

P = 128
PASSES = K // 512
VIEW_TILES = S // P
HALF = S // 2
A_BANKS = (0, 1, 2, 3, 4, 5, 6, 3)
Y_BANKS = ((0, 1), (2, 7), (4, 5), (0, 1))
STORE_ROWS = ((1, 1, 2), (2, 2), (2, 2), (2, 1, 1))
PARKED_ROW = (None, 4, 5)
GRASP_PLANE = 4
QUARTER = S // 4
B_PASS_ORDER = ((0, 1, 2), (0, 1, 2), (0, 2, 1), (2, 0, 1))
A_PASS_ORDER = ((0, 1, 2), (0, 1, 2), (0, 1, 2), (2, 0, 1))
KIB = 1024
GPSIMD_SQUARES = (0, 1, 4, 6, 7)
SHARED_SQUARE = 2
DAMP_OFFSET = {0: 3 * KIB, 1: 7 * KIB, 2: 5 * KIB, 4: 11 * KIB, 6: 5 * KIB, 7: 11 * KIB}
SQUARED_BEHIND_PRODUCT = {2: 6, 4: 7}


def tile_list_grasp_view_value_kernel(tc, tab_words, tab_scales, offs, tab2_words, tab2_scales, offs2,
                                                  wa, wb_words, wb_scales, c, out):
    nc = tc.nc
    with ExitStack() as ctx:
        keep = ctx.enter_context(tc.tile_pool(name="keep", bufs=1))
        stage = ctx.enter_context(tc.tile_pool(name="stage", bufs=1))
        psum = ctx.enter_context(tc.psum_pool(name="psum", bufs=1))

        def sb(name, shape, dtype, offset=None):
            if offset is None:
                return keep.tile(shape, dtype, name=name, align_bytes=64)
            return stage.tile(shape, dtype, name=name, align_bytes=64, offset=offset)

        def bank(index, name):
            return psum.tile([P, 512], F32, name=name, tag="bank%d" % index)

        offs_sb = keep.tile([P, S // 16], U16, name="offs_sb")
        offs2_sb = keep.tile([P, S2 // 16], U16, name="offs2_sb")
        tab_s = sb("tab_s", [P, T], U8)
        tab_w = [sb("tab_w%d" % a, [P, T], I32) for a in range(PASSES)]
        tab2_w = sb("tab2_w", [P, T2], I32)
        tab2_s = sb("tab2_s", [P, T2], U8)
        wb_w = sb("wb_w", [P, PASSES, 2 * H], U8)
        wb_s = sb("wb_s", [P, PASSES, H], U8)
        wa_raw = [sb("wa_raw%d" % a, [P, 4, H], F32) for a in range(PASSES)]
        wa_w = [sb("wa_w%d" % a, [P, H], U32) for a in range(PASSES)]
        wa_s = [sb("wa_s%d" % a, [P, H], U8) for a in range(PASSES)]
        v_s_gathered = sb("v_s_gathered", [P, S], U8)
        v_s_moved = sb("v_s_moved", [P, PASSES - 1, S], U8)
        v2_w = sb("v2_w", [P, S2], U32)
        bias = sb("bias", [P, S2 // P], F32)
        one = sb("one", [P, 1], F32)
        wb_w_dealt = [sb("wb_w_dealt%d" % a, [P, H], U16) for a in range(PASSES)]
        wb_s_dealt = [sb("wb_s_dealt%d" % a, [P, H], U8) for a in range(PASSES)]

        nc.vector.memset(tab_s[:].bitcast(I32), 0)
        nc.vector.memset(wb_s[:].rearrange("p a n -> p (a n)").bitcast(I32), 0)
        nc.vector.memset(v_s_moved[:].rearrange("p a n -> p (a n)").bitcast(I32), 0)
        nc.vector.memset(tab2_s[:].bitcast(I32), 0)
        nc.vector.memset(one[:], 1.0)

        def load_table(a):
            nc.sync.dma_start(tab_w[a][:], tab_words[a].rearrange("p n t -> p (n t)").bitcast(I32))

        def load_wa(a):
            nc.sync.dma_start(wa_raw[a][:], wa[512 * a : 512 * (a + 1), :].rearrange("(p j) r -> p j r", j=4))

        nc.sync.dma_start(offs_sb[:], offs)
        nc.sync.dma_start(wb_w[:].bitcast(I32), wb_words.rearrange("a p n -> p a n").bitcast(I32))
        for r in range(4):
            nc.sync.dma_start(tab_s[r:P:32, :].bitcast(I32), tab_scales[0, r:16:4, :].bitcast(I32))
        for a in range(1, PASSES):
            nc.sync.dma_start(tab_s[PARKED_ROW[a] : P : 8, :].bitcast(I32), tab_scales[a].bitcast(I32))
        load_table(0)
        for r in range(4):
            nc.sync.dma_start(wb_s[r:P:32, :, :].bitcast(I32),
                              wb_scales[:, r:16:4, :].rearrange("a q n -> q a n").bitcast(I32))
        load_table(1)

        nc.vector.tensor_copy(v_s_gathered[:], tab_s[:].indirect(offs_sb[:]))

        def move_scale_rows(a):
            for r in range(4):
                nc.sync.dma_start(v_s_moved[r:P:32, a - 1, :].bitcast(I32),
                                  v_s_gathered[PARKED_ROW[a] + 8 * r : P : 32, :].bitcast(I32))

        move_scale_rows(1)
        load_table(2)
        move_scale_rows(2)
        load_wa(0)
        load_wa(1)
        nc.sync.dma_start(offs2_sb[:], offs2)
        nc.sync.dma_start(tab2_w[:], tab2_words[0].rearrange("p n t -> p (n t)").bitcast(I32))
        for r in range(4):
            nc.sync.dma_start(tab2_s[GRASP_PLANE + r : P : 32, :].bitcast(I32),
                              tab2_scales[0, r:16:4, :].bitcast(I32))
        load_wa(2)
        with nc.allow_non_contiguous_dma(reason="one bias value a partition"):
            nc.sync.dma_start(bias[:], c.rearrange("(n p) -> p n", p=P))

        warm = sb("warm", [P, 1], F32)
        nc.scalar.activation(warm[:], one[:], ACT.Abs_reciprocal_sqrt, bias=1.0)

        def deal_wb_scales(a, slots):
            nc.gpsimd.tensor_copy(wb_s_dealt[a][:].rearrange("p (t m) -> p t m", t=4)[:, slots],
                                  wb_s[:, a, :].rearrange("p (m t) -> p t m", t=4)[:, slots])

        deal_wb_scales(0, slice(0, 2))
        deal_wb_scales(0, slice(2, 4))
        for a in range(PASSES):
            if a > 0:
                deal_wb_scales(a, slice(0, 4))
            nc.scalar.copy(wb_w_dealt[a][:].rearrange("p (t m) -> p t m", t=4),
                           wb_w[:, a, :].bitcast(U16).rearrange("p (m t) -> p t m", t=4))

        v_w = {}

        def gather_words(a, j0, width):
            words = sb("v_w%d_%d" % (a, j0), [P, width], U32)
            nc.vector.tensor_copy(words[:], tab_w[a][:].bitcast(U32).indirect(offs_sb[:, j0 // 16 : (j0 + width) // 16]))
            for k in range(j0 // QUARTER, (j0 + width) // QUARTER):
                v_w[a, k] = words[:, QUARTER * k - j0 : QUARTER * (k + 1) - j0]

        def v_s(a, j0, width):
            if a == 0:
                return v_s_gathered[:, j0 : j0 + width]
            return v_s_moved[:, a - 1, j0 : j0 + width]

        gather_words(0, 0, QUARTER)
        gather_words(0, QUARTER, QUARTER)
        gather_words(0, HALF, HALF)
        for j0 in (0, HALF):
            gather_words(1, j0, HALF)
        for j0 in range(0, S, QUARTER):
            gather_words(PASSES - 1, j0, QUARTER)

        b_ps = {}

        def project_b(a, k, u):
            order = B_PASS_ORDER[k]
            if a == order[0]:
                b_ps[k, u] = bank(2 * k + u, "b_ps%d_%d" % (k, u))
            for v in range(2):
                cols = slice(P * (2 * u + v), P * (2 * u + v + 1))
                nc.tensor.matmul_mx(out=b_ps[k, u][:, QUARTER * v : QUARTER * (v + 1)],
                                    lhsT=wb_w_dealt[a][:, cols].bitcast(U8).bitcast(FP4X4),
                                    lhsT_scale=wb_s_dealt[a][:, cols],
                                    rhs=v_w[a, k].bitcast(FP8X4), rhs_scale=v_s(a, QUARTER * k, QUARTER),
                                    start=(a == order[0] and v == 0), stop=(a == order[-1] and v == 1))

        root = [sb("root%d" % k, [P, 4 * QUARTER], F32) for k in range(4)]

        def inverse_roots(k):
            mag = sb("mag%d" % k, [P, 2, 2 * QUARTER], F32)
            for u in range(2):
                nc.scalar.activation(mag[:, u, :].rearrange("p (j v) -> p j v", v=2),
                                     b_ps[k, u][:].rearrange("p (v j) -> p j v", v=2), ACT.Abs)
            nc.scalar.activation(root[k][:].rearrange("p (j u v) -> p j u v", u=2, v=2),
                                 mag[:].rearrange("p u (j v) -> p j u v", v=2), ACT.Abs_reciprocal_sqrt, bias=1.0)

        for k in range(4):
            for a in B_PASS_ORDER[k]:
                for u in range(2):
                    project_b(a, k, u)
            inverse_roots(k)

        a_ps = {}

        def project_a(a, g):
            order = A_PASS_ORDER[g // 2] if g < VIEW_TILES - 1 else (0, 1, 2)
            if a == order[0]:
                a_ps[g] = bank(A_BANKS[g], "a_ps%d" % g)
            views = slice(P * (g % 2), P * (g % 2 + 1))
            for t in range(4):
                cols = slice(P * t, P * (t + 1))
                nc.tensor.matmul_mx(out=a_ps[g][:, cols], lhsT=wa_w[a][:, cols].bitcast(FP8X4),
                                    lhsT_scale=wa_s[a][:, cols], rhs=v_w[a, g // 2][:, views].bitcast(FP8X4),
                                    rhs_scale=v_s(a, P * g, P),
                                    start=(a == order[0] and t == 0), stop=(a == order[-1] and t == 3))

        def quantise_wa(a):
            wa_bf = [sb("wa_bf%d_%d" % (a, u), [P, 2 * H], BF16, 2 * KIB * (2 * a + u)) for u in range(2)]
            rows = wa_raw[a][:].rearrange("p j (m u v) -> p u m j v", u=2, v=2)
            for u in range(2):
                nc.vector.tensor_copy(wa_bf[u][:].rearrange("p (v m j) -> p m j v", v=2, j=4), rows[:, u])
            for u in range(2):
                cols = slice(2 * P * u, 2 * P * (u + 1))
                nc.vector.quantize_mx(out=wa_w[a][:, cols].bitcast(FP8X4), scales=wa_s[a][:, cols],
                                      in_=wa_bf[u][:])

        quantise_wa(0)
        quantise_wa(1)
        nc.vector.tensor_copy(v2_w[:], tab2_w[:].bitcast(U32).indirect(offs2_sb[:]))
        v2_s = []

        def gather_grasp_scales(half, offset):
            v2_s.append(sb("v2_s%d" % half, [P, S2 // 2], U8, offset))
            nc.vector.tensor_copy(v2_s[half][:], tab2_s[:].indirect(offs2_sb[:, 16 * half : 16 * (half + 1)]))

        gather_grasp_scales(0, None)
        quantise_wa(2)
        gather_grasp_scales(1, 9 * KIB)
        for g in range(VIEW_TILES - 1):
            for a in A_PASS_ORDER[g // 2]:
                project_a(a, g)

        damp = {}

        def square_roots(g):
            damp_tile = sb("damp%d" % g, [P, H], F32, DAMP_OFFSET.get(g))
            damp[g] = damp_tile[:]
            roots = root[g // 2][:, H * (g % 2) : H * (g % 2 + 1)]
            if g in GPSIMD_SQUARES:
                nc.gpsimd.tensor_tensor(damp[g], roots, roots, ALU.mult)
            elif g == SHARED_SQUARE:
                nc.gpsimd.tensor_tensor(damp[g][:, : H // 2], roots[:, : H // 2], roots[:, : H // 2], ALU.mult)
                nc.scalar.activation(damp[g][:, H // 2 :], roots[:, H // 2 :], ACT.Square)
            else:
                nc.scalar.activation(damp[g], roots, ACT.Square)

        for g in range(VIEW_TILES - len(SQUARED_BEHIND_PRODUCT)):
            square_roots(g)

        def embed_and_score(first, tiles, y_ps, column):
            width = P * tiles
            h_bf = sb("h_bf%d" % first, [P, tiles, H], BF16)
            for n in range(tiles):
                g = first + n
                nc.vector.tensor_tensor(h_bf[:, n, :].rearrange("p (j t) -> p j t", t=4),
                                        a_ps[g][:].rearrange("p (t j) -> p j t", t=4),
                                        damp[g].rearrange("p (j t) -> p j t", t=4), ALU.mult)
                if g in SQUARED_BEHIND_PRODUCT:
                    square_roots(SQUARED_BEHIND_PRODUCT[g])
                if g == A_BANKS[VIEW_TILES - 1]:
                    for a in range(PASSES):
                        project_a(a, VIEW_TILES - 1)
            h_w = sb("h_w%d" % first, [P, width], U32)
            h_s = sb("h_s%d" % first, [P, width], U8)
            nc.vector.quantize_mx(out=h_w[:].bitcast(FP8X4), scales=h_s[:],
                                  in_=h_bf[:].rearrange("p g r -> p (g r)"))
            if not y_ps:
                y_ps.extend(bank(g, "y_ps%d" % first + "_%d" % g) for g in Y_BANKS[first // 2])
            for i in range(S2 // P):
                place = QUARTER * (i % 2) + column
                nc.tensor.matmul_mx(out=y_ps[i // 2][:, place : place + width],
                                    lhsT=v2_w[:, P * i : P * (i + 1)].bitcast(FP8X4),
                                    lhsT_scale=v2_s[i // 2][GRASP_PLANE:P, P * (i % 2) : P * (i % 2 + 1)],
                                    rhs=h_w[:].bitcast(FP8X4), rhs_scale=h_s[:], start=True, stop=True)

        for k in range(4):
            y_ps = []
            if k < 3:
                embed_and_score(2 * k, 2, y_ps, 0)
            else:
                embed_and_score(2 * k, 1, y_ps, 0)
                embed_and_score(2 * k + 1, 1, y_ps, P)
            i0 = 0
            for rows in STORE_ROWS[k]:
                res = sb("res%d_%d" % (k, i0), [P, rows, QUARTER], F32)
                for n in range(rows):
                    i = i0 + n
                    nc.scalar.activation(res[:, n, :], y_ps[i // 2][:, QUARTER * (i % 2) : QUARTER * (i % 2 + 1)],
                                         ACT.Tanh, bias=bias[:, i : i + 1])
                nc.sync.dma_start(
                    out[P * i0 : P * (i0 + rows), QUARTER * k : QUARTER * (k + 1)].rearrange("(n p) j -> p n j", p=P),
                    res[:])
                i0 += rows
